import numpy as np
import ml_dtypes


def mxq(x, axis, fmt="e4m3"):
    dtype, down = {"e4m3": (ml_dtypes.float8_e4m3fn, 7), "e5m2": (ml_dtypes.float8_e5m2, 14)}[fmt]
    v = np.moveaxis(np.asarray(x, np.float32).astype(ml_dtypes.bfloat16).astype(np.float64), axis, -1)
    blocks = v.reshape(v.shape[:-1] + (-1, 32))
    amax = np.abs(blocks).max(-1, keepdims=True)
    byte = np.maximum(np.where(amax > 0, np.frexp(amax)[1] - 1 + 127, 0) - down, 1)
    scale = np.exp2(byte - 127.0)
    codes = (blocks / scale).astype(np.float32).astype(dtype).astype(np.float64)
    return np.moveaxis((codes * scale).reshape(v.shape), -1, axis)


WIDE = False


def mx_kscale(k):
    if not WIDE:
        return np.ones(k)
    levels = np.array([18, -18])
    if k % 512:
        return np.exp2(np.random.permutation(np.resize(levels, k // 32))).repeat(32)
    a = np.empty((k // 512, 16))
    for p in range(k // 512):
        a[p, :8] = np.random.permutation(np.resize(levels, 8))
        for g in range(8):
            far = levels[np.abs(levels - a[p, g]) >= 10]
            a[p, g + 8] = far[np.random.randint(len(far))]
    return np.exp2(a.ravel()).repeat(32)


def f64(x):
    return np.asarray(x).astype(np.float64)


def striped(idx):
    return np.tile(np.asarray(idx).reshape(-1, 16).T, (8, 1)).astype(np.uint16)


def unstriped(offs):
    return offs[:16].T.reshape(-1).astype(np.int64)


B, N, T, D, R, K = 2, 512, 2048, 512, 512, 128


def setup_inputs():
    n = np.random.standard_normal
    idx = np.random.permutation(T)[:B * N]
    s = mx_kscale(D)[:, None]
    z = mx_kscale(R)[:, None]
    x = n((B, D, R))
    teach = np.exp(n((B, R, N)))
    teach = teach / teach.sum(-1, keepdims=True)
    return {
        "xT": (x * s).astype(np.float32),
        "wT": (n((D, T)) * (0.50 / np.sqrt(D)) / s).astype(np.float32),
        "y": teach.astype(np.float32),
        "wt": (np.random.uniform(0.5, 1.5, (B, R, 1)) * N / np.sqrt(R) * z).astype(np.float32),
        "xm": (x.transpose(0, 2, 1) / z / s[:, 0]).astype(np.float32),
        "pm": (n((D, K)) / np.sqrt(D) * s).astype(np.float32),
        "offs": striped(idx),
    }


def reference(xT, wT, y, wt, xm, pm, offs):
    idx = unstriped(offs)
    pick = lambda x: x[:, idx].reshape(x.shape[0], B, N).transpose(1, 0, 2)
    a = mxq(f64(xT), 1, "e4m3").transpose(0, 2, 1) @ mxq(pick(f64(wT)), 1, "e4m3")
    e = np.exp(a - a.max(-1, keepdims=True))
    g = f64(wt) * (e / e.sum(-1, keepdims=True) - f64(y))
    dw = mxq(f64(xm), 1, "e4m3").transpose(0, 2, 1) @ mxq(g, 1, "e5m2")
    dp = mxq(f64(pm), 0, "e4m3").T @ mxq(dw, 1, "e4m3")
    gw = np.zeros((K, T))
    gw[:, idx] = dp.transpose(1, 0, 2).reshape(K, B * N)
    return gw

@@ -1,0 +1,327 @@
+from contextlib import ExitStack
+
+import concourse.mybir as mybir
+from concourse.masks import make_identity
+
+B, N, T, D, R, K = 2, 512, 2048, 512, 512, 128
+FLOPS = 2 * B * (R * D * N + R * D * N + D * K * N)
+
+F32 = mybir.dt.float32
+BF16 = mybir.dt.bfloat16
+U32 = mybir.dt.uint32
+U16 = mybir.dt.uint16
+U8 = mybir.dt.uint8
+E4M3 = mybir.dt.float8_e4m3fn_x4
+E5M2 = mybir.dt.float8_e5m2_x4
+ALU = mybir.AluOpType
+ACT = mybir.ActivationFunctionType
+
+P = 128
+PACK = 4
+HALF = N // 2
+LIST_COLS = N // 16
+PIECE = 32
+
+W_CHUNKS = [(0, 0, 1024, 960), (0, 1024, 2048, 1664), (1, 0, 1024, 192), (1, 1024, 1536, 1152), (1, 1536, 2048, 1856)]
+
+
+def tile_attend_gkl_w_prj_kernel(tc, xT, wT, y, wt, xm, pm, offs, out):
+    nc = tc.nc
+    with ExitStack() as ctx:
+        sb = ctx.enter_context(tc.tile_pool(name="sb", bufs=1))
+        ps_a = ctx.enter_context(tc.psum_pool(name="ps_a", bufs=3))
+        ps_dw = ctx.enter_context(tc.psum_pool(name="ps_dw", bufs=2))
+        ps_tr = ctx.enter_context(tc.psum_pool(name="ps_tr", bufs=2))
+        ps_dp = ctx.enter_context(tc.psum_pool(name="ps_dp", bufs=1))
+        held = {}
+
+        def tile(name, shape, dtype):
+            if name not in held:
+                held[name] = sb.tile(shape, dtype, name=name, align_bytes=64)
+            return held[name]
+
+        def mx(name, width):
+            return tile(name + "_codes", [P, width], U32), tile(name + "_scales", [P, width], U8)
+
+        def quantise(name, width, fmt, first, count):
+            codes, scales = mx(name, width)
+            src = held[name + "_packed"]
+            nc.vector.quantize_mx(out=codes[:, first : first + count].bitcast(fmt), scales=scales[:, first : first + count],
+                                  in_=src[:, PACK * first : PACK * (first + count)])
+
+        def matmul(dst, lhs, lhs_fmt, cols, rhs):
+            nc.tensor.matmul_mx(out=dst, lhsT=held[lhs + "_codes"][:, cols].bitcast(lhs_fmt), lhsT_scale=held[lhs + "_scales"][:, cols],
+                                rhs=held[rhs + "_codes"][:].bitcast(E4M3), rhs_scale=held[rhs + "_scales"][:], start=True, stop=True)
+
+        def copy(dst, src, engine):
+            if engine == "vector":
+                nc.vector.tensor_copy(out=dst, in_=src)
+            elif engine == "scalar":
+                nc.scalar.copy(out=dst, in_=src)
+            else:
+                nc.gpsimd.tensor_scalar(dst, src, 1.0, 0.0, ALU.mult, ALU.add)
+
+        offsets = sb.tile([P, B * LIST_COLS], U16, name="offsets")
+        nc.sync.dma_start(offsets[:], offs)
+        w_rows = wT.rearrange("(p u e) c -> p u e c", u=2, e=2)
+        wt_sb = tile("wt", [P, B, PACK], F32)
+
+        def load_w(k):
+            u, c0, c1, split = W_CHUNKS[k]
+            nc.sync.dma_start(out=tile("w_raw%d" % k, [P, 2, c1 - c0], F32)[:], in_=w_rows[:, u, :, c0:c1])
+
+        def load_wt():
+            nc.sync.dma_start(out=wt_sb[:], in_=wt.rearrange("b (p t) o -> p b (t o)", t=PACK))
+
+        def load(name, src):
+            raw = tile(name, [P, PACK, src.shape[1]], F32)
+            nc.sync.dma_start(out=raw[:], in_=src.rearrange("(p j) c -> p j c", j=PACK))
+
+        load_w(0)
+        load_w(1)
+        load_w(2)
+        load_w(3)
+        load_w(4)
+        load("xT0", xT[0])
+        load_wt()
+        load("xT1", xT[1])
+        load("xm1", xm[1])
+        load("y0", y[0])
+        load("xm0", xm[0])
+        load("y1", y[1])
+        load("pm", pm)
+
+        window = sb.tile([P, T], F32, name="window")
+        nc.gpsimd.memset(window[:], 0.0)
+        ident = tile("ident", [P, P], F32)
+        make_identity(nc, ident[:])
+        warm = tile("warm", [P, 8], F32)
+        nc.vector.memset(warm[:], 0.0)
+        nc.scalar.activation(tile("warm_out", [P, 8], F32)[:], warm[:], ACT.Exp)
+
+        def w_views(k):
+            u, c0, c1, split = W_CHUNKS[k]
+            dst = tile("w_pairs%d" % u, [P, T], U32)[:].bitcast(BF16).rearrange("p (c e) -> p c e", e=2)[:, c0:c1]
+            return dst, held["w_raw%d" % k][:].rearrange("p e c -> p c e"), split - c0, c1 - c0
+
+        def cast_w_vector(k):
+            dst, src, split, end = w_views(k)
+            nc.vector.tensor_copy(out=dst[:, 0:split], in_=src[:, 0:split])
+
+        def cast_w_scalar(k):
+            dst, src, split, end = w_views(k)
+            nc.scalar.activation(dst[:, split:end], src[:, split:end], ACT.Copy)
+
+        def gather_w(u, b, h):
+            first, count = (0, N) if h == 2 else (h * HALF, HALF)
+            words = tile("w%d_packed" % b, [P, N * PACK], BF16)[:].bitcast(U32).rearrange("p (c u) -> p c u", u=2)
+            col = b * LIST_COLS + first // 16
+            nc.vector.tensor_copy(out=words[:, first : first + count, u],
+                                  in_=held["w_pairs%d" % u][:].indirect(offsets[:, col : col + count // 16]))
+
+        def quantise_w(b):
+            quantise("w%d" % b, N, E4M3, 0, N)
+
+        def pack_xT(b, i, engine):
+            packed = tile("xT%d_packed" % b, [P, R * PACK], BF16)
+            part = slice(i * PIECE, (i + 1) * PIECE)
+            copy(packed[:].rearrange("p (t m j) -> p m t j", t=PACK, j=PACK)[:, part],
+                 held["xT%d" % b][:].rearrange("p j (m t) -> p m t j", t=PACK)[:, part], engine)
+
+        def quantise_xT(b, c):
+            quantise("xT%d" % b, R, E4M3, c * (R // 2), R // 2)
+
+        def pack_xm(b, i, engine):
+            packed = tile("xm%d_packed" % b, [P, D * PACK], BF16)
+            part = slice(i * PIECE, (i + 1) * PIECE)
+            copy(packed[:].rearrange("p (u m e j) -> p m u e j", u=2, e=2, j=PACK)[:, part],
+                 held["xm%d" % b][:].rearrange("p j (m u e) -> p m u e j", u=2, e=2)[:, part], engine)
+
+        def quantise_xm(b):
+            quantise("xm%d" % b, D, E4M3, 0, D)
+
+        def pack_pm(engine):
+            packed = tile("pm_packed", [P, K * PACK], BF16)
+            copy(packed[:].rearrange("p (f j) -> p f j", j=PACK), held["pm"][:].rearrange("p j f -> p f j"), engine)
+
+        def quantise_pm():
+            quantise("pm", K, E4M3, 0, K)
+
+        def weigh_y(b, t, engine):
+            plane = held["y%d" % b][:, t, :]
+            weight = wt_sb[:, b, t : t + 1]
+            if engine == "vector":
+                nc.vector.tensor_scalar(plane, plane, weight, None, ALU.mult)
+            elif engine == "scalar":
+                nc.scalar.activation(plane, plane, ACT.Copy, scale=weight)
+            else:
+                nc.gpsimd.tensor_scalar(plane, plane, weight, 0.0, ALU.mult, ALU.add)
+
+        def scores(b, t):
+            neg_max = tile("neg_max%d" % b, [P, PACK], F32)[:, t : t + 1]
+            a = ps_a.tile([P, N], F32, name="a")
+            matmul(a[:], "xT%d" % b, E4M3, slice(t * P, (t + 1) * P), "w%d" % b)
+            nc.vector.tensor_reduce(neg_max, a[:], mybir.AxisListType.X, ALU.max, negate=True)
+            nc.scalar.activation(tile("e%d" % b, [P, PACK, N], F32)[:, t, :], a[:], ACT.Exp, bias=neg_max,
+                                 accum_out=tile("sums%d" % b, [P, PACK], F32)[:, t : t + 1])
+
+        def coefficients(b, pair):
+            two = slice(2 * pair, 2 * pair + 2)
+            inv = tile("inv%d" % b, [P, PACK], F32)
+            nc.vector.reciprocal(inv[:, two], held["sums%d" % b][:, two])
+            nc.vector.tensor_tensor(tile("coef%d" % b, [P, PACK], F32)[:, two], inv[:, two], wt_sb[:, b, two], ALU.mult)
+
+        def gradient(b, h, t):
+            cols = slice(0, N) if h == 2 else slice(h * HALF, (h + 1) * HALF)
+            nc.vector.scalar_tensor_tensor(tile("g_planes%d" % b, [P, PACK, N], BF16)[:, t, cols], held["e%d" % b][:, t, cols],
+                                           held["coef%d" % b][:, t : t + 1], held["y%d" % b][:, t, cols], ALU.mult, ALU.subtract)
+
+        def pack_g(b, h, i, engine):
+            packed = tile("g%d_%d_packed" % (b, h), [P, HALF * PACK], BF16)
+            first = h * HALF + i * P
+            copy(packed[:].rearrange("p (i t) -> p i t", t=PACK)[:, i * P : (i + 1) * P],
+                 held["g_planes%d" % b][:, :, first : first + P].rearrange("p t i -> p i t"), engine)
+
+        def quantise_g(b, h):
+            quantise("g%d_%d" % (b, h), HALF, E5M2, 0, HALF)
+
+        def table_gradient(b, h, q, engine):
+            if q == 0:
+                held["turned%d_%d" % (b, h)] = ps_tr.tile([P, 2, 2, P], F32, name="turned")
+            turned = held["turned%d_%d" % (b, h)]
+            dw = ps_dw.tile([P, D], F32, name="dw")
+            matmul(dw[:], "g%d_%d" % (b, h), E5M2, slice(q * P, (q + 1) * P), "xm%d" % b)
+            rounded = tile("dw_rounded%d_%d_%d" % (b, h, q), [P, D], BF16)
+            copy(rounded[:], dw[:], engine)
+            words = rounded[:].bitcast(F32)
+            for u in range(2):
+                nc.tensor.transpose(turned[:, q, u, :], words[:, u * P : (u + 1) * P], ident[:])
+
+        def pack_dw(b, h, engine):
+            packed = tile("dw%d_%d_packed" % (b, h), [P, HALF * PACK], BF16)
+            copy(packed[:].bitcast(F32).rearrange("p (q i u) -> p q i u", q=2, u=2),
+                 held["turned%d_%d" % (b, h)][:].rearrange("p q u i -> p q i u"), engine)
+
+        def quantise_dw(b, h):
+            quantise("dw%d_%d" % (b, h), HALF, E4M3, 0, HALF)
+
+        def project(b, h, engine):
+            dp = ps_dp.tile([P, HALF], F32, name="dp")
+            matmul(dp[:], "pm", E4M3, slice(0, K), "dw%d_%d" % (b, h))
+            copy(tile("dense%d_%d" % (b, h), [P, HALF], F32)[:], dp[:], engine)
+
+        def scatter(b, h):
+            first = b * LIST_COLS + h * (LIST_COLS // 2)
+            nc.vector.tensor_copy(out=window[:].indirect(offsets[:, first : first + LIST_COLS // 2]),
+                                  in_=held["dense%d_%d" % (b, h)][:])
+
+        cast_w_vector(3)
+        pack_pm("vector")
+        cast_w_scalar(0)
+        pack_xT(0, 3, "scalar")
+        cast_w_scalar(2)
+        cast_w_scalar(4)
+        cast_w_vector(4)
+        pack_xT(0, 1, "scalar")
+        pack_xT(0, 0, "scalar")
+        cast_w_vector(2)
+        cast_w_scalar(3)
+        weigh_y(0, 3, "scalar")
+        pack_xT(1, 1, "scalar")
+        cast_w_vector(0)
+        cast_w_vector(1)
+        gather_w(1, 1, 0)
+        pack_xm(0, 1, "vector")
+        pack_xm(0, 2, "scalar")
+        weigh_y(1, 3, "scalar")
+        gather_w(1, 0, 2)
+        pack_xT(0, 2, "scalar")
+        cast_w_scalar(1)
+        gather_w(0, 0, 2)
+        pack_xm(1, 1, "scalar")
+        quantise_w(0)
+        pack_xm(0, 3, "scalar")
+        quantise_xT(0, 0)
+        scores(0, 0)
+        pack_xT(1, 3, "vector")
+        weigh_y(0, 2, "vector")
+        pack_xm(1, 2, "vector")
+        pack_xT(1, 2, "scalar")
+        scores(0, 1)
+        quantise_xT(0, 1)
+        gather_w(1, 1, 1)
+        weigh_y(0, 1, "scalar")
+        gather_w(0, 1, 2)
+        weigh_y(0, 0, "vector")
+        pack_xm(0, 0, "scalar")
+        scores(0, 2)
+        pack_xT(1, 0, "vector")
+        quantise_xT(1, 0)
+        scores(0, 3)
+        quantise_w(1)
+        quantise_xT(1, 1)
+        weigh_y(1, 0, "scalar")
+        coefficients(0, 0)
+        coefficients(0, 1)
+        scores(1, 0)
+        scores(1, 1)
+        weigh_y(1, 1, "scalar")
+        scores(1, 2)
+        gradient(0, 2, 2)
+        gradient(0, 2, 0)
+        gradient(0, 2, 1)
+        gradient(0, 2, 3)
+        pack_g(0, 0, 1, "vector")
+        pack_g(0, 1, 1, "vector")
+        coefficients(1, 0)
+        pack_g(0, 0, 0, "vector")
+        quantise_g(0, 0)
+        scores(1, 3)
+        quantise_xm(0)
+        gradient(1, 0, 1)
+        gradient(1, 0, 0)
+        coefficients(1, 1)
+        pack_xm(1, 3, "scalar")
+        weigh_y(1, 2, "scalar")
+        gradient(1, 0, 2)
+        gradient(1, 1, 2)
+        gradient(1, 1, 3)
+        pack_xm(1, 0, "vector")
+        quantise_xm(1)
+        pack_g(0, 1, 0, "scalar")
+        quantise_g(0, 1)
+        gradient(1, 1, 1)
+        gradient(1, 0, 3)
+        pack_g(1, 0, 0, "vector")
+        table_gradient(0, 0, 0, "scalar")
+        table_gradient(0, 0, 1, "scalar")
+        gradient(1, 1, 0)
+        pack_g(1, 0, 1, "vector")
+        quantise_g(1, 0)
+        pack_dw(0, 0, "scalar")
+        pack_g(1, 1, 0, "scalar")
+        table_gradient(0, 1, 0, "vector")
+        table_gradient(0, 1, 1, "scalar")
+        pack_g(1, 1, 1, "scalar")
+        table_gradient(1, 0, 0, "scalar")
+        table_gradient(1, 0, 1, "vector")
+        quantise_pm()
+        quantise_dw(0, 0)
+        quantise_g(1, 1)
+        pack_dw(0, 1, "scalar")
+        pack_dw(1, 0, "scalar")
+        quantise_dw(0, 1)
+        table_gradient(1, 1, 0, "scalar")
+        table_gradient(1, 1, 1, "vector")
+        project(0, 0, "scalar")
+        project(0, 1, "scalar")
+        scatter(0, 0)
+        quantise_dw(1, 0)
+        project(1, 0, "scalar")
+        pack_dw(1, 1, "scalar")
+        scatter(0, 1)
+        quantise_dw(1, 1)
+        project(1, 1, "scalar")
+        scatter(1, 0)
+        scatter(1, 1)
+        nc.sync.dma_start(out=out, in_=window[:])

@@ -20,9 +20,8 @@ P = 128
 PACK = 4
 HALF = N // 2
 LIST_COLS = N // 16
-PIECE = 32
 
-W_CHUNKS = [(0, 0, 1024, 960), (0, 1024, 2048, 1664), (1, 0, 1024, 192), (1, 1024, 1536, 1152), (1, 1536, 2048, 1856)]
+W_CHUNKS = [(0, 0, 1024, 960), (0, 1024, 2048, 1792), (1, 0, 1024, 256), (1, 1024, 1536, 1344), (1, 1536, 2048, 1984)]
 
 
 def tile_attend_gkl_w_prj_kernel(tc, xT, wT, y, wt, xm, pm, offs, out):
@@ -80,24 +79,21 @@ def tile_attend_gkl_w_prj_kernel(tc, xT, wT, y, wt, xm, pm, offs, out):
         load_w(0)
         load_w(1)
         load_w(2)
-        load_w(3)
         load_w(4)
-        load("xT0", xT[0])
-        load_wt()
+        load_w(3)
         load("xT1", xT[1])
-        load("xm1", xm[1])
-        load("y0", y[0])
+        load("xT0", xT[0])
         load("xm0", xm[0])
+        load("y0", y[0])
+        load_wt()
         load("y1", y[1])
         load("pm", pm)
+        load("xm1", xm[1])
 
         window = sb.tile([P, T], F32, name="window")
         nc.gpsimd.memset(window[:], 0.0)
         ident = tile("ident", [P, P], F32)
         make_identity(nc, ident[:])
-        warm = tile("warm", [P, 8], F32)
-        nc.vector.memset(warm[:], 0.0)
-        nc.scalar.activation(tile("warm_out", [P, 8], F32)[:], warm[:], ACT.Exp)
 
         def w_views(k):
             u, c0, c1, split = W_CHUNKS[k]
@@ -114,35 +110,42 @@ def tile_attend_gkl_w_prj_kernel(tc, xT, wT, y, wt, xm, pm, offs, out):
 
         def gather_w(u, b, h):
             first, count = (0, N) if h == 2 else (h * HALF, HALF)
-            words = tile("w%d_packed" % b, [P, N * PACK], BF16)[:].bitcast(U32).rearrange("p (c u) -> p c u", u=2)
+            words = tile("w%d_words" % b, [P, 2, N], U32)
             col = b * LIST_COLS + first // 16
-            nc.vector.tensor_copy(out=words[:, first : first + count, u],
+            nc.vector.tensor_copy(out=words[:, u, first : first + count],
                                   in_=held["w_pairs%d" % u][:].indirect(offsets[:, col : col + count // 16]))
+
+        def pack_w(b, h, engine):
+            packed = tile("w%d_packed" % b, [P, N * PACK], BF16)
+            pairs = held["w%d_words" % b][:].rearrange("p u c -> p (u c)").bitcast(BF16)
+            part = slice(h * HALF, (h + 1) * HALF)
+            copy(packed[:].rearrange("p (c u e) -> p c u e", u=2, e=2)[:, part],
+                 pairs.rearrange("p (u c e) -> p c u e", u=2, e=2)[:, part], engine)
 
         def quantise_w(b):
             quantise("w%d" % b, N, E4M3, 0, N)
 
-        def pack_xT(b, i, engine):
+        def pack_xT(b, first, count, engine):
             packed = tile("xT%d_packed" % b, [P, R * PACK], BF16)
-            part = slice(i * PIECE, (i + 1) * PIECE)
-            copy(packed[:].rearrange("p (t m j) -> p m t j", t=PACK, j=PACK)[:, part],
-                 held["xT%d" % b][:].rearrange("p j (m t) -> p m t j", t=PACK)[:, part], engine)
+            part = slice(first, first + count)
+            copy(packed[:].rearrange("p (t m j) -> p m j t", t=PACK, j=PACK)[:, part],
+                 held["xT%d" % b][:].rearrange("p j (m t) -> p m j t", t=PACK)[:, part], engine)
 
-        def quantise_xT(b, c):
-            quantise("xT%d" % b, R, E4M3, c * (R // 2), R // 2)
+        def quantise_xT(b, first, count):
+            quantise("xT%d" % b, R, E4M3, first, count)
 
-        def pack_xm(b, i, engine):
+        def pack_xm(b, first, count, engine):
             packed = tile("xm%d_packed" % b, [P, D * PACK], BF16)
-            part = slice(i * PIECE, (i + 1) * PIECE)
-            copy(packed[:].rearrange("p (u m e j) -> p m u e j", u=2, e=2, j=PACK)[:, part],
-                 held["xm%d" % b][:].rearrange("p j (m u e) -> p m u e j", u=2, e=2)[:, part], engine)
+            part = slice(first, first + count)
+            copy(packed[:].rearrange("p (u m e j) -> p m j u e", u=2, e=2, j=PACK)[:, part],
+                 held["xm%d" % b][:].rearrange("p j (m u e) -> p m j u e", u=2, e=2)[:, part], engine)
 
         def quantise_xm(b):
             quantise("xm%d" % b, D, E4M3, 0, D)
 
         def pack_pm(engine):
             packed = tile("pm_packed", [P, K * PACK], BF16)
-            copy(packed[:].rearrange("p (f j) -> p f j", j=PACK), held["pm"][:].rearrange("p j f -> p f j"), engine)
+            copy(packed[:].rearrange("p (c i j) -> p c j i", i=PACK, j=PACK), held["pm"][:].rearrange("p j (c i) -> p c j i", i=PACK), engine)
 
         def quantise_pm():
             quantise("pm", K, E4M3, 0, K)
@@ -176,11 +179,11 @@ def tile_attend_gkl_w_prj_kernel(tc, xT, wT, y, wt, xm, pm, offs, out):
             nc.vector.scalar_tensor_tensor(tile("g_planes%d" % b, [P, PACK, N], BF16)[:, t, cols], held["e%d" % b][:, t, cols],
                                            held["coef%d" % b][:, t : t + 1], held["y%d" % b][:, t, cols], ALU.mult, ALU.subtract)
 
-        def pack_g(b, h, i, engine):
+        def pack_g(b, h, first, count, engine):
             packed = tile("g%d_%d_packed" % (b, h), [P, HALF * PACK], BF16)
-            first = h * HALF + i * P
-            copy(packed[:].rearrange("p (i t) -> p i t", t=PACK)[:, i * P : (i + 1) * P],
-                 held["g_planes%d" % b][:, :, first : first + P].rearrange("p t i -> p i t"), engine)
+            slot = h * HALF + first
+            copy(packed[:, first * PACK : (first + count) * PACK].rearrange("p (c s t) -> p c t s", s=PACK, t=PACK),
+                 held["g_planes%d" % b][:, :, slot : slot + count].rearrange("p t (c s) -> p c t s", s=PACK), engine)
 
         def quantise_g(b, h):
             quantise("g%d_%d" % (b, h), HALF, E5M2, 0, HALF)
@@ -215,113 +218,99 @@ def tile_attend_gkl_w_prj_kernel(tc, xT, wT, y, wt, xm, pm, offs, out):
             nc.vector.tensor_copy(out=window[:].indirect(offsets[:, first : first + LIST_COLS // 2]),
                                   in_=held["dense%d_%d" % (b, h)][:])
 
-        cast_w_vector(3)
-        pack_pm("vector")
-        cast_w_scalar(0)
-        pack_xT(0, 3, "scalar")
-        cast_w_scalar(2)
-        cast_w_scalar(4)
-        cast_w_vector(4)
-        pack_xT(0, 1, "scalar")
-        pack_xT(0, 0, "scalar")
-        cast_w_vector(2)
-        cast_w_scalar(3)
-        weigh_y(0, 3, "scalar")
-        pack_xT(1, 1, "scalar")
         cast_w_vector(0)
-        cast_w_vector(1)
-        gather_w(1, 1, 0)
-        pack_xm(0, 1, "vector")
-        pack_xm(0, 2, "scalar")
-        weigh_y(1, 3, "scalar")
-        gather_w(1, 0, 2)
-        pack_xT(0, 2, "scalar")
         cast_w_scalar(1)
+        cast_w_scalar(0)
+        cast_w_vector(1)
+        cast_w_vector(2)
+        cast_w_vector(3)
+        cast_w_scalar(2)
+        cast_w_scalar(3)
+        cast_w_vector(4)
+        cast_w_scalar(4)
         gather_w(0, 0, 2)
-        pack_xm(1, 1, "scalar")
-        quantise_w(0)
-        pack_xm(0, 3, "scalar")
-        quantise_xT(0, 0)
-        scores(0, 0)
-        pack_xT(1, 3, "vector")
-        weigh_y(0, 2, "vector")
-        pack_xm(1, 2, "vector")
-        pack_xT(1, 2, "scalar")
-        scores(0, 1)
-        quantise_xT(0, 1)
-        gather_w(1, 1, 1)
-        weigh_y(0, 1, "scalar")
         gather_w(0, 1, 2)
-        weigh_y(0, 0, "vector")
-        pack_xm(0, 0, "scalar")
-        scores(0, 2)
-        pack_xT(1, 0, "vector")
-        quantise_xT(1, 0)
-        scores(0, 3)
+        gather_w(1, 0, 2)
+        pack_w(0, 0, "scalar")
+        pack_xT(0, 0, 128, "vector")
+        pack_w(0, 1, "scalar")
+        quantise_w(0)
+        quantise_xT(0, 0, 256)
+        quantise_xT(0, 256, 256)
+        gather_w(1, 1, 2)
+        pack_w(1, 1, "scalar")
+        pack_xT(1, 0, 16, "scalar")
+        pack_w(1, 0, "scalar")
+        scores(0, 0)
         quantise_w(1)
-        quantise_xT(1, 1)
-        weigh_y(1, 0, "scalar")
+        scores(0, 1)
+        scores(0, 2)
+        pack_xT(1, 16, 80, "vector")
+        pack_xT(1, 96, 32, "scalar")
+        quantise_xT(1, 0, 512)
+        weigh_y(0, 1, "vector")
+        weigh_y(0, 0, "vector")
+        weigh_y(0, 2, "vector")
+        scores(0, 3)
         coefficients(0, 0)
         coefficients(0, 1)
-        scores(1, 0)
-        scores(1, 1)
-        weigh_y(1, 1, "scalar")
-        scores(1, 2)
+        weigh_y(0, 3, "scalar")
+        gradient(0, 2, 1)
         gradient(0, 2, 2)
         gradient(0, 2, 0)
-        gradient(0, 2, 1)
-        gradient(0, 2, 3)
-        pack_g(0, 0, 1, "vector")
-        pack_g(0, 1, 1, "vector")
+        gradient(0, 0, 3)
+        scores(1, 0)
+        gradient(0, 1, 3)
+        scores(1, 1)
         coefficients(1, 0)
-        pack_g(0, 0, 0, "vector")
-        quantise_g(0, 0)
+        scores(1, 2)
         scores(1, 3)
-        quantise_xm(0)
-        gradient(1, 0, 1)
-        gradient(1, 0, 0)
+        pack_xm(0, 0, 128, "scalar")
         coefficients(1, 1)
-        pack_xm(1, 3, "scalar")
-        weigh_y(1, 2, "scalar")
-        gradient(1, 0, 2)
-        gradient(1, 1, 2)
-        gradient(1, 1, 3)
-        pack_xm(1, 0, "vector")
-        quantise_xm(1)
-        pack_g(0, 1, 0, "scalar")
+        pack_pm("scalar")
+        quantise_xm(0)
+        quantise_pm()
+        pack_g(0, 0, 0, 256, "scalar")
+        weigh_y(1, 2, "vector")
+        quantise_g(0, 0)
+        pack_g(0, 1, 0, 256, "vector")
+        weigh_y(1, 1, "scalar")
         quantise_g(0, 1)
-        gradient(1, 1, 1)
-        gradient(1, 0, 3)
-        pack_g(1, 0, 0, "vector")
+        weigh_y(1, 0, "scalar")
+        gradient(1, 2, 0)
+        weigh_y(1, 3, "scalar")
+        gradient(1, 2, 3)
+        gradient(1, 2, 1)
+        gradient(1, 2, 2)
+        pack_xm(1, 0, 64, "vector")
         table_gradient(0, 0, 0, "scalar")
         table_gradient(0, 0, 1, "scalar")
-        gradient(1, 1, 0)
-        pack_g(1, 0, 1, "vector")
-        quantise_g(1, 0)
-        pack_dw(0, 0, "scalar")
-        pack_g(1, 1, 0, "scalar")
-        table_gradient(0, 1, 0, "vector")
+        pack_xm(1, 64, 64, "scalar")
+        quantise_xm(1)
+        table_gradient(0, 1, 0, "scalar")
         table_gradient(0, 1, 1, "scalar")
-        pack_g(1, 1, 1, "scalar")
-        table_gradient(1, 0, 0, "scalar")
-        table_gradient(1, 0, 1, "vector")
-        quantise_pm()
-        quantise_dw(0, 0)
-        quantise_g(1, 1)
+        pack_dw(0, 0, "scalar")
+        pack_g(1, 0, 0, 256, "vector")
+        quantise_g(1, 0)
         pack_dw(0, 1, "scalar")
-        pack_dw(1, 0, "scalar")
+        pack_g(1, 1, 0, 256, "vector")
+        quantise_g(1, 1)
+        quantise_dw(0, 0)
+        project(0, 0, "vector")
+        table_gradient(1, 0, 0, "scalar")
         quantise_dw(0, 1)
-        table_gradient(1, 1, 0, "scalar")
-        table_gradient(1, 1, 1, "vector")
-        project(0, 0, "scalar")
+        table_gradient(1, 0, 1, "scalar")
+        pack_dw(1, 0, "scalar")
         project(0, 1, "scalar")
-        scatter(0, 0)
         quantise_dw(1, 0)
         project(1, 0, "scalar")
+        table_gradient(1, 1, 0, "scalar")
+        table_gradient(1, 1, 1, "vector")
         pack_dw(1, 1, "scalar")
-        scatter(0, 1)
         quantise_dw(1, 1)
         project(1, 1, "scalar")
+        scatter(0, 0)
+        scatter(0, 1)
         scatter(1, 0)
         scatter(1, 1)
         nc.sync.dma_start(out=out, in_=window[:])

@@ -19,18 +19,21 @@ ACT = mybir.ActivationFunctionType
 P = 128
 PACK = 4
 HALF = N // 2
-LIST_COLS = N // 16
+PER_COLUMN = 16
+VECTOR, SCALAR = "vector", "scalar"
 
-W_CHUNKS = [(0, 0, 1024, 960), (0, 1024, 2048, 1792), (1, 0, 1024, 256), (1, 1024, 1536, 1344), (1, 1536, 2048, 1984)]
+TABLE_CHUNKS = [(0, 0, 1024, 1024), (0, 1024, 2048, 1792), (1, 0, 512, 128), (1, 512, 1536, 1088), (1, 1536, 2048, 1920)]
+XM_ON_VECTOR = 32
+G1_ON_SCALAR = [64, 128]
 
 
 def tile_attend_gkl_w_prj_kernel(tc, xT, wT, y, wt, xm, pm, offs, out):
     nc = tc.nc
     with ExitStack() as ctx:
         sb = ctx.enter_context(tc.tile_pool(name="sb", bufs=1))
-        ps_a = ctx.enter_context(tc.psum_pool(name="ps_a", bufs=3))
-        ps_dw = ctx.enter_context(tc.psum_pool(name="ps_dw", bufs=2))
-        ps_tr = ctx.enter_context(tc.psum_pool(name="ps_tr", bufs=2))
+        ps_scores = ctx.enter_context(tc.psum_pool(name="ps_scores", bufs=3))
+        ps_dw = ctx.enter_context(tc.psum_pool(name="ps_dw", bufs=3))
+        ps_turned = ctx.enter_context(tc.psum_pool(name="ps_turned", bufs=1))
         ps_dp = ctx.enter_context(tc.psum_pool(name="ps_dp", bufs=1))
         held = {}
 
@@ -39,55 +42,50 @@ def tile_attend_gkl_w_prj_kernel(tc, xT, wT, y, wt, xm, pm, offs, out):
                 held[name] = sb.tile(shape, dtype, name=name, align_bytes=64)
             return held[name]
 
-        def mx(name, width):
-            return tile(name + "_codes", [P, width], U32), tile(name + "_scales", [P, width], U8)
+        def copy(dst, src, engine):
+            if engine == VECTOR:
+                nc.vector.tensor_copy(out=dst, in_=src)
+            else:
+                nc.scalar.copy(out=dst, in_=src)
 
         def quantise(name, width, fmt, first, count):
-            codes, scales = mx(name, width)
-            src = held[name + "_packed"]
-            nc.vector.quantize_mx(out=codes[:, first : first + count].bitcast(fmt), scales=scales[:, first : first + count],
-                                  in_=src[:, PACK * first : PACK * (first + count)])
+            codes = tile(name + "_codes", [P, width], U32)
+            scales = tile(name + "_scales", [P, width], U8)
+            nc.vector.quantize_mx(
+                out=codes[:, first : first + count].bitcast(fmt),
+                scales=scales[:, first : first + count],
+                in_=held[name + "_packed"][:, PACK * first : PACK * (first + count)],
+            )
 
-        def matmul(dst, lhs, lhs_fmt, cols, rhs):
-            nc.tensor.matmul_mx(out=dst, lhsT=held[lhs + "_codes"][:, cols].bitcast(lhs_fmt), lhsT_scale=held[lhs + "_scales"][:, cols],
-                                rhs=held[rhs + "_codes"][:].bitcast(E4M3), rhs_scale=held[rhs + "_scales"][:], start=True, stop=True)
-
-        def copy(dst, src, engine):
-            if engine == "vector":
-                nc.vector.tensor_copy(out=dst, in_=src)
-            elif engine == "scalar":
-                nc.scalar.copy(out=dst, in_=src)
-            else:
-                nc.gpsimd.tensor_scalar(dst, src, 1.0, 0.0, ALU.mult, ALU.add)
-
-        offsets = sb.tile([P, B * LIST_COLS], U16, name="offsets")
-        nc.sync.dma_start(offsets[:], offs)
-        w_rows = wT.rearrange("(p u e) c -> p u e c", u=2, e=2)
-        wt_sb = tile("wt", [P, B, PACK], F32)
-
-        def load_w(k):
-            u, c0, c1, split = W_CHUNKS[k]
-            nc.sync.dma_start(out=tile("w_raw%d" % k, [P, 2, c1 - c0], F32)[:], in_=w_rows[:, u, :, c0:c1])
-
-        def load_wt():
-            nc.sync.dma_start(out=wt_sb[:], in_=wt.rearrange("b (p t) o -> p b (t o)", t=PACK))
+        def matmul(dst, stationary, fmt, cols, moving):
+            nc.tensor.matmul_mx(
+                out=dst,
+                lhsT=held[stationary + "_codes"][:, cols].bitcast(fmt),
+                lhsT_scale=held[stationary + "_scales"][:, cols],
+                rhs=held[moving + "_codes"][:].bitcast(E4M3),
+                rhs_scale=held[moving + "_scales"][:],
+                start=True,
+                stop=True,
+            )
 
         def load(name, src):
             raw = tile(name, [P, PACK, src.shape[1]], F32)
             nc.sync.dma_start(out=raw[:], in_=src.rearrange("(p j) c -> p j c", j=PACK))
 
-        load_w(0)
-        load_w(1)
-        load_w(2)
-        load_w(4)
-        load_w(3)
-        load("xT1", xT[1])
-        load("xT0", xT[0])
-        load("xm0", xm[0])
-        load("y0", y[0])
-        load_wt()
-        load("y1", y[1])
+        offsets = sb.tile([P, B * N // PER_COLUMN], U16, name="offsets")
+        nc.sync.dma_start(offsets[:], offs)
+        table_rows = wT.rearrange("(p u e) c -> p u e c", u=2, e=2)
+        for chunk, (u, first, end, split) in enumerate(TABLE_CHUNKS):
+            raw = tile("table%d" % chunk, [P, 2, end - first], F32)
+            nc.sync.dma_start(out=raw[:], in_=table_rows[:, u, :, first:end])
         load("pm", pm)
+        load("xT0", xT[0])
+        load("xT1", xT[1])
+        load("y0", y[0])
+        weights = tile("wt", [P, B, PACK], F32)
+        nc.sync.dma_start(out=weights[:], in_=wt.rearrange("b (p t) o -> p b (t o)", t=PACK))
+        load("xm0", xm[0])
+        load("y1", y[1])
         load("xm1", xm[1])
 
         window = sb.tile([P, T], F32, name="window")
@@ -95,222 +93,205 @@ def tile_attend_gkl_w_prj_kernel(tc, xT, wT, y, wt, xm, pm, offs, out):
         ident = tile("ident", [P, P], F32)
         make_identity(nc, ident[:])
 
-        def w_views(k):
-            u, c0, c1, split = W_CHUNKS[k]
-            dst = tile("w_pairs%d" % u, [P, T], U32)[:].bitcast(BF16).rearrange("p (c e) -> p c e", e=2)[:, c0:c1]
-            return dst, held["w_raw%d" % k][:].rearrange("p e c -> p c e"), split - c0, c1 - c0
+        def listed(b, first, count):
+            col = (b * N + first) // PER_COLUMN
+            return offsets[:, col : col + count // PER_COLUMN]
 
-        def cast_w_vector(k):
-            dst, src, split, end = w_views(k)
-            nc.vector.tensor_copy(out=dst[:, 0:split], in_=src[:, 0:split])
+        def round_table(chunk):
+            u, first, end, split = TABLE_CHUNKS[chunk]
+            pairs = tile("pairs%d" % u, [P, T], U32)[:].bitcast(BF16).rearrange("p (c e) -> p c e", e=2)
+            raw = held["table%d" % chunk][:].rearrange("p e c -> p c e")
+            nc.vector.tensor_copy(out=pairs[:, first:split], in_=raw[:, 0 : split - first])
+            if split < end:
+                nc.scalar.activation(pairs[:, split:end], raw[:, split - first : end - first], ACT.Copy)
 
-        def cast_w_scalar(k):
-            dst, src, split, end = w_views(k)
-            nc.scalar.activation(dst[:, split:end], src[:, split:end], ACT.Copy)
+        def gather(u, b, first, count):
+            words = tile("picked%d" % b, [P, 2, N], U32)
+            nc.vector.tensor_copy(
+                out=words[:, u, first : first + count], in_=held["pairs%d" % u][:].indirect(listed(b, first, count))
+            )
 
-        def gather_w(u, b, h):
-            first, count = (0, N) if h == 2 else (h * HALF, HALF)
-            words = tile("w%d_words" % b, [P, 2, N], U32)
-            col = b * LIST_COLS + first // 16
-            nc.vector.tensor_copy(out=words[:, u, first : first + count],
-                                  in_=held["w_pairs%d" % u][:].indirect(offsets[:, col : col + count // 16]))
+        def pack_table(b):
+            packed = tile("w%d_packed" % b, [P, N * PACK], BF16)[:].rearrange("p (c u e) -> p c u e", u=2, e=2)
+            picked = held["picked%d" % b][:].rearrange("p u c -> p (u c)").bitcast(BF16)
+            picked = picked.rearrange("p (u c e) -> p c u e", u=2, e=2)
+            for h in range(2):
+                part = slice(h * HALF, (h + 1) * HALF)
+                copy(packed[:, part], picked[:, part], SCALAR)
 
-        def pack_w(b, h, engine):
-            packed = tile("w%d_packed" % b, [P, N * PACK], BF16)
-            pairs = held["w%d_words" % b][:].rearrange("p u c -> p (u c)").bitcast(BF16)
-            part = slice(h * HALF, (h + 1) * HALF)
-            copy(packed[:].rearrange("p (c u e) -> p c u e", u=2, e=2)[:, part],
-                 pairs.rearrange("p (u c e) -> p c u e", u=2, e=2)[:, part], engine)
-
-        def quantise_w(b):
-            quantise("w%d" % b, N, E4M3, 0, N)
-
-        def pack_xT(b, first, count, engine):
+        def pack_xT(b, engine):
             packed = tile("xT%d_packed" % b, [P, R * PACK], BF16)
-            part = slice(first, first + count)
-            copy(packed[:].rearrange("p (t m j) -> p m j t", t=PACK, j=PACK)[:, part],
-                 held["xT%d" % b][:].rearrange("p j (m t) -> p m j t", t=PACK)[:, part], engine)
+            copy(
+                packed[:].rearrange("p (t m j) -> p m j t", t=PACK, j=PACK),
+                held["xT%d" % b][:].rearrange("p j (m t) -> p m j t", t=PACK),
+                engine,
+            )
 
-        def quantise_xT(b, first, count):
-            quantise("xT%d" % b, R, E4M3, first, count)
+        def pack_xm(b):
+            packed = tile("xm%d_packed" % b, [P, D * PACK], BF16)[:].rearrange("p (u m e j) -> p m j u e", u=2, e=2, j=PACK)
+            raw = held["xm%d" % b][:].rearrange("p j (m u e) -> p m j u e", u=2, e=2)
+            copy(packed[:, 0:XM_ON_VECTOR], raw[:, 0:XM_ON_VECTOR], VECTOR)
+            copy(packed[:, XM_ON_VECTOR:P], raw[:, XM_ON_VECTOR:P], SCALAR)
 
-        def pack_xm(b, first, count, engine):
-            packed = tile("xm%d_packed" % b, [P, D * PACK], BF16)
-            part = slice(first, first + count)
-            copy(packed[:].rearrange("p (u m e j) -> p m j u e", u=2, e=2, j=PACK)[:, part],
-                 held["xm%d" % b][:].rearrange("p j (m u e) -> p m j u e", u=2, e=2)[:, part], engine)
-
-        def quantise_xm(b):
-            quantise("xm%d" % b, D, E4M3, 0, D)
-
-        def pack_pm(engine):
+        def pack_pm():
             packed = tile("pm_packed", [P, K * PACK], BF16)
-            copy(packed[:].rearrange("p (c i j) -> p c j i", i=PACK, j=PACK), held["pm"][:].rearrange("p j (c i) -> p c j i", i=PACK), engine)
+            copy(
+                packed[:].rearrange("p (c i j) -> p c j i", i=PACK, j=PACK),
+                held["pm"][:].rearrange("p j (c i) -> p c j i", i=PACK),
+                SCALAR,
+            )
 
-        def quantise_pm():
-            quantise("pm", K, E4M3, 0, K)
-
-        def weigh_y(b, t, engine):
-            plane = held["y%d" % b][:, t, :]
-            weight = wt_sb[:, b, t : t + 1]
-            if engine == "vector":
-                nc.vector.tensor_scalar(plane, plane, weight, None, ALU.mult)
-            elif engine == "scalar":
-                nc.scalar.activation(plane, plane, ACT.Copy, scale=weight)
-            else:
-                nc.gpsimd.tensor_scalar(plane, plane, weight, 0.0, ALU.mult, ALU.add)
+        def pack_g(b, h, first, end, engine):
+            packed = tile("g%d_%d_packed" % (b, h), [P, HALF * PACK], BF16)
+            slots = slice(h * HALF + first, h * HALF + end)
+            copy(
+                packed[:, first * PACK : end * PACK].rearrange("p (c s t) -> p c t s", s=PACK, t=PACK),
+                held["g_tiles%d" % b][:, :, slots].rearrange("p t (c s) -> p c t s", s=PACK),
+                engine,
+            )
 
         def scores(b, t):
             neg_max = tile("neg_max%d" % b, [P, PACK], F32)[:, t : t + 1]
-            a = ps_a.tile([P, N], F32, name="a")
+            a = ps_scores.tile([P, N], F32, name="a")
             matmul(a[:], "xT%d" % b, E4M3, slice(t * P, (t + 1) * P), "w%d" % b)
             nc.vector.tensor_reduce(neg_max, a[:], mybir.AxisListType.X, ALU.max, negate=True)
-            nc.scalar.activation(tile("e%d" % b, [P, PACK, N], F32)[:, t, :], a[:], ACT.Exp, bias=neg_max,
-                                 accum_out=tile("sums%d" % b, [P, PACK], F32)[:, t : t + 1])
+            nc.scalar.activation(
+                tile("e%d" % b, [P, PACK, N], F32)[:, t, :],
+                a[:],
+                ACT.Exp,
+                bias=neg_max,
+                accum_out=tile("sums%d" % b, [P, PACK], F32)[:, t : t + 1],
+            )
 
-        def coefficients(b, pair):
-            two = slice(2 * pair, 2 * pair + 2)
-            inv = tile("inv%d" % b, [P, PACK], F32)
-            nc.vector.reciprocal(inv[:, two], held["sums%d" % b][:, two])
-            nc.vector.tensor_tensor(tile("coef%d" % b, [P, PACK], F32)[:, two], inv[:, two], wt_sb[:, b, two], ALU.mult)
+        def row_factors(b):
+            inverse = tile("inverse%d" % b, [P, PACK], F32)
+            factor = tile("factor%d" % b, [P, PACK], F32)
+            for t in range(0, PACK, 2):
+                nc.vector.reciprocal(inverse[:, t : t + 2], held["sums%d" % b][:, t : t + 2])
+                nc.vector.tensor_tensor(factor[:, t : t + 2], inverse[:, t : t + 2], weights[:, b, t : t + 2], ALU.mult)
 
-        def gradient(b, h, t):
-            cols = slice(0, N) if h == 2 else slice(h * HALF, (h + 1) * HALF)
-            nc.vector.scalar_tensor_tensor(tile("g_planes%d" % b, [P, PACK, N], BF16)[:, t, cols], held["e%d" % b][:, t, cols],
-                                           held["coef%d" % b][:, t : t + 1], held["y%d" % b][:, t, cols], ALU.mult, ALU.subtract)
+        def weigh_targets(b, engines):
+            for t, engine in enumerate(engines):
+                targets = held["y%d" % b][:, t, :]
+                weight = weights[:, b, t : t + 1]
+                if engine == VECTOR:
+                    nc.vector.tensor_scalar(targets, targets, weight, None, ALU.mult)
+                else:
+                    nc.scalar.activation(targets, targets, ACT.Copy, scale=weight)
 
-        def pack_g(b, h, first, count, engine):
-            packed = tile("g%d_%d_packed" % (b, h), [P, HALF * PACK], BF16)
-            slot = h * HALF + first
-            copy(packed[:, first * PACK : (first + count) * PACK].rearrange("p (c s t) -> p c t s", s=PACK, t=PACK),
-                 held["g_planes%d" % b][:, :, slot : slot + count].rearrange("p t (c s) -> p c t s", s=PACK), engine)
+        def gradient(b, t, first, end):
+            nc.vector.scalar_tensor_tensor(
+                tile("g_tiles%d" % b, [P, PACK, N], BF16)[:, t, first:end],
+                held["e%d" % b][:, t, first:end],
+                held["factor%d" % b][:, t : t + 1],
+                held["y%d" % b][:, t, first:end],
+                ALU.mult,
+                ALU.subtract,
+            )
 
-        def quantise_g(b, h):
-            quantise("g%d_%d" % (b, h), HALF, E5M2, 0, HALF)
-
-        def table_gradient(b, h, q, engine):
+        def table_gradient(b, h, q):
             if q == 0:
-                held["turned%d_%d" % (b, h)] = ps_tr.tile([P, 2, 2, P], F32, name="turned")
+                held["turned%d_%d" % (b, h)] = ps_turned.tile([P, 2, 2, P], F32, name="turned")
             turned = held["turned%d_%d" % (b, h)]
             dw = ps_dw.tile([P, D], F32, name="dw")
             matmul(dw[:], "g%d_%d" % (b, h), E5M2, slice(q * P, (q + 1) * P), "xm%d" % b)
             rounded = tile("dw_rounded%d_%d_%d" % (b, h, q), [P, D], BF16)
-            copy(rounded[:], dw[:], engine)
+            copy(rounded[:], dw[:], SCALAR)
             words = rounded[:].bitcast(F32)
             for u in range(2):
                 nc.tensor.transpose(turned[:, q, u, :], words[:, u * P : (u + 1) * P], ident[:])
 
         def pack_dw(b, h, engine):
             packed = tile("dw%d_%d_packed" % (b, h), [P, HALF * PACK], BF16)
-            copy(packed[:].bitcast(F32).rearrange("p (q i u) -> p q i u", q=2, u=2),
-                 held["turned%d_%d" % (b, h)][:].rearrange("p q u i -> p q i u"), engine)
+            copy(
+                packed[:].bitcast(F32).rearrange("p (q i u) -> p q i u", q=2, u=2),
+                held["turned%d_%d" % (b, h)][:].rearrange("p q u i -> p q i u"),
+                engine,
+            )
 
-        def quantise_dw(b, h):
-            quantise("dw%d_%d" % (b, h), HALF, E4M3, 0, HALF)
+        def quantise_half(name, b, h, fmt):
+            quantise("%s%d_%d" % (name, b, h), HALF, fmt, 0, HALF)
 
         def project(b, h, engine):
             dp = ps_dp.tile([P, HALF], F32, name="dp")
             matmul(dp[:], "pm", E4M3, slice(0, K), "dw%d_%d" % (b, h))
             copy(tile("dense%d_%d" % (b, h), [P, HALF], F32)[:], dp[:], engine)
 
-        def scatter(b, h):
-            first = b * LIST_COLS + h * (LIST_COLS // 2)
-            nc.vector.tensor_copy(out=window[:].indirect(offsets[:, first : first + LIST_COLS // 2]),
-                                  in_=held["dense%d_%d" % (b, h)][:])
+        for chunk in range(len(TABLE_CHUNKS)):
+            round_table(chunk)
+        pack_pm()
+        quantise("pm", K, E4M3, 0, K)
+        for b in range(B):
+            gather(0, b, 0, N)
 
-        cast_w_vector(0)
-        cast_w_scalar(1)
-        cast_w_scalar(0)
-        cast_w_vector(1)
-        cast_w_vector(2)
-        cast_w_vector(3)
-        cast_w_scalar(2)
-        cast_w_scalar(3)
-        cast_w_vector(4)
-        cast_w_scalar(4)
-        gather_w(0, 0, 2)
-        gather_w(0, 1, 2)
-        gather_w(1, 0, 2)
-        pack_w(0, 0, "scalar")
-        pack_xT(0, 0, 128, "vector")
-        pack_w(0, 1, "scalar")
-        quantise_w(0)
-        quantise_xT(0, 0, 256)
-        quantise_xT(0, 256, 256)
-        gather_w(1, 1, 2)
-        pack_w(1, 1, "scalar")
-        pack_xT(1, 0, 16, "scalar")
-        pack_w(1, 0, "scalar")
-        scores(0, 0)
-        quantise_w(1)
-        scores(0, 1)
-        scores(0, 2)
-        pack_xT(1, 16, 80, "vector")
-        pack_xT(1, 96, 32, "scalar")
-        quantise_xT(1, 0, 512)
-        weigh_y(0, 1, "vector")
-        weigh_y(0, 0, "vector")
-        weigh_y(0, 2, "vector")
-        scores(0, 3)
-        coefficients(0, 0)
-        coefficients(0, 1)
-        weigh_y(0, 3, "scalar")
-        gradient(0, 2, 1)
-        gradient(0, 2, 2)
-        gradient(0, 2, 0)
-        gradient(0, 0, 3)
+        gather(1, 0, 0, HALF)
+        gather(1, 0, HALF, HALF)
+        pack_table(0)
+        pack_xT(0, VECTOR)
+        quantise("w0", N, E4M3, 0, N)
+        quantise("xT0", R, E4M3, 0, R // 2)
+        quantise("xT0", R, E4M3, R // 2, R // 2)
+        gather(1, 1, 0, N)
+        pack_table(1)
+        quantise("w1", N, E4M3, 0, N)
+
+        for t in range(PACK):
+            scores(0, t)
+        row_factors(0)
+        pack_xT(1, SCALAR)
+        quantise("xT1", R, E4M3, 0, R)
+        weigh_targets(0, [VECTOR, SCALAR, VECTOR, SCALAR])
+        for t in range(PACK):
+            gradient(0, t, 0, N)
+
         scores(1, 0)
-        gradient(0, 1, 3)
         scores(1, 1)
-        coefficients(1, 0)
+        pack_xm(0)
         scores(1, 2)
         scores(1, 3)
-        pack_xm(0, 0, 128, "scalar")
-        coefficients(1, 1)
-        pack_pm("scalar")
-        quantise_xm(0)
-        quantise_pm()
-        pack_g(0, 0, 0, 256, "scalar")
-        weigh_y(1, 2, "vector")
-        quantise_g(0, 0)
-        pack_g(0, 1, 0, 256, "vector")
-        weigh_y(1, 1, "scalar")
-        quantise_g(0, 1)
-        weigh_y(1, 0, "scalar")
-        gradient(1, 2, 0)
-        weigh_y(1, 3, "scalar")
-        gradient(1, 2, 3)
-        gradient(1, 2, 1)
-        gradient(1, 2, 2)
-        pack_xm(1, 0, 64, "vector")
-        table_gradient(0, 0, 0, "scalar")
-        table_gradient(0, 0, 1, "scalar")
-        pack_xm(1, 64, 64, "scalar")
-        quantise_xm(1)
-        table_gradient(0, 1, 0, "scalar")
-        table_gradient(0, 1, 1, "scalar")
-        pack_dw(0, 0, "scalar")
-        pack_g(1, 0, 0, 256, "vector")
-        quantise_g(1, 0)
-        pack_dw(0, 1, "scalar")
-        pack_g(1, 1, 0, 256, "vector")
-        quantise_g(1, 1)
-        quantise_dw(0, 0)
-        project(0, 0, "vector")
-        table_gradient(1, 0, 0, "scalar")
-        quantise_dw(0, 1)
-        table_gradient(1, 0, 1, "scalar")
-        pack_dw(1, 0, "scalar")
-        project(0, 1, "scalar")
-        quantise_dw(1, 0)
-        project(1, 0, "scalar")
-        table_gradient(1, 1, 0, "scalar")
-        table_gradient(1, 1, 1, "vector")
-        pack_dw(1, 1, "scalar")
-        quantise_dw(1, 1)
-        project(1, 1, "scalar")
-        scatter(0, 0)
-        scatter(0, 1)
-        scatter(1, 0)
-        scatter(1, 1)
+        row_factors(1)
+        quantise("xm0", D, E4M3, 0, D)
+        for h in range(2):
+            pack_g(0, h, 0, HALF, VECTOR)
+            quantise_half("g", 0, h, E5M2)
+
+        weigh_targets(1, [SCALAR, VECTOR, SCALAR, SCALAR])
+        for t in range(PACK):
+            gradient(1, t, 0, N if t % 2 else HALF)
+        pack_xm(1)
+        quantise("xm1", D, E4M3, 0, D)
+        for h in range(2):
+            if h == 1:
+                gradient(1, 0, HALF, N)
+                gradient(1, 2, HALF, N)
+            pack_g(1, h, 0, G1_ON_SCALAR[h], SCALAR)
+            pack_g(1, h, G1_ON_SCALAR[h], HALF, VECTOR)
+            quantise_half("g", 1, h, E5M2)
+
+        table_gradient(0, 0, 0)
+        table_gradient(0, 0, 1)
+        pack_dw(0, 0, VECTOR)
+        quantise_half("dw", 0, 0, E4M3)
+        table_gradient(0, 1, 0)
+        table_gradient(0, 1, 1)
+        pack_dw(0, 1, VECTOR)
+        project(0, 0, VECTOR)
+        quantise_half("dw", 0, 1, E4M3)
+        table_gradient(1, 0, 0)
+        table_gradient(1, 0, 1)
+        pack_dw(1, 0, SCALAR)
+        table_gradient(1, 1, 0)
+        project(0, 1, SCALAR)
+        quantise_half("dw", 1, 0, E4M3)
+        table_gradient(1, 1, 1)
+        project(1, 0, SCALAR)
+        pack_dw(1, 1, SCALAR)
+        quantise_half("dw", 1, 1, E4M3)
+        project(1, 1, SCALAR)
+
+        for b in range(B):
+            for h in range(2):
+                nc.vector.tensor_copy(
+                    out=window[:].indirect(listed(b, h * HALF, HALF)), in_=held["dense%d_%d" % (b, h)][:]
+                )
         nc.sync.dma_start(out=out, in_=window[:])

@@ -20,26 +20,28 @@ P = 128
 PACK = 4
 HALF = N // 2
 PER_COLUMN = 16
-VECTOR, SCALAR = "vector", "scalar"
+VECTOR, SCALAR, GPSIMD = "vector", "scalar", "gpsimd"
 
-TABLE_CHUNKS = [(0, 0, 1024, 1024), (0, 1024, 2048, 1792), (1, 0, 512, 128), (1, 512, 1536, 1088), (1, 1536, 2048, 1920)]
-XM_ON_VECTOR = 32
-G1_ON_SCALAR = [64, 128]
+TABLE_CHUNKS = [(0, 0, 1024), (0, 1024, 2048), (1, 0, 1024), (1, 1024, 1536), (1, 1536, 2048)]
+SCORE_BANK = [[0, 1, 2, 3], [4, 5, 6, 7]]
+DW_BANK = [[0, 1, 2, 3], [3, 4, 5, 4]]
+TURNED_BANK = [[4, 5], [0, 1]]
+DP_BANK = [[6, 3], [6, 7]]
+XT0_ON_SCALAR = 32
+REUSES = {"dw_rounded0": "xm1", "w1_codes": "xT0_packed"}
 
 
 def tile_attend_gkl_w_prj_kernel(tc, xT, wT, y, wt, xm, pm, offs, out):
     nc = tc.nc
     with ExitStack() as ctx:
         sb = ctx.enter_context(tc.tile_pool(name="sb", bufs=1))
-        ps_scores = ctx.enter_context(tc.psum_pool(name="ps_scores", bufs=3))
-        ps_dw = ctx.enter_context(tc.psum_pool(name="ps_dw", bufs=3))
-        ps_turned = ctx.enter_context(tc.psum_pool(name="ps_turned", bufs=1))
-        ps_dp = ctx.enter_context(tc.psum_pool(name="ps_dp", bufs=1))
+        ps = ctx.enter_context(tc.psum_pool(name="ps", bufs=1))
+        banks = [ps.tile([P, N], F32, name="bank%d" % i) for i in range(8)]
         held = {}
 
         def tile(name, shape, dtype):
             if name not in held:
-                held[name] = sb.tile(shape, dtype, name=name, align_bytes=64)
+                held[name] = sb.tile(shape, dtype, name=name, tag=REUSES.get(name, name), align_bytes=64)
             return held[name]
 
         def copy(dst, src, engine):
@@ -73,19 +75,33 @@ def tile_attend_gkl_w_prj_kernel(tc, xT, wT, y, wt, xm, pm, offs, out):
             nc.sync.dma_start(out=raw[:], in_=src.rearrange("(p j) c -> p j c", j=PACK))
 
         offsets = sb.tile([P, B * N // PER_COLUMN], U16, name="offsets")
-        nc.sync.dma_start(offsets[:], offs)
         table_rows = wT.rearrange("(p u e) c -> p u e c", u=2, e=2)
-        for chunk, (u, first, end, split) in enumerate(TABLE_CHUNKS):
+
+        def load_table(chunk):
+            u, first, end = TABLE_CHUNKS[chunk]
             raw = tile("table%d" % chunk, [P, 2, end - first], F32)
             nc.sync.dma_start(out=raw[:], in_=table_rows[:, u, :, first:end])
-        load("pm", pm)
-        load("xT0", xT[0])
-        load("xT1", xT[1])
-        load("y0", y[0])
+
         weights = tile("wt", [P, B, PACK], F32)
-        nc.sync.dma_start(out=weights[:], in_=wt.rearrange("b (p t) o -> p b (t o)", t=PACK))
-        load("xm0", xm[0])
+
+        def load_weights():
+            nc.sync.dma_start(out=weights[:], in_=wt.rearrange("b (p t) o -> p b (t o)", t=PACK))
+
+        load_table(0)
+        nc.sync.dma_start(offsets[:], offs)
+        for chunk in range(1, len(TABLE_CHUNKS)):
+            load_table(chunk)
+        split = R - PACK * XT0_ON_SCALAR
+        xT0_rows = xT[0].rearrange("(p j) c -> p j c", j=PACK)
+        xT0_end = tile("w0_packed", [P, N * PACK], BF16)[:, HALF * PACK :].bitcast(F32).rearrange("p (j c) -> p j c", j=PACK)
+        nc.sync.dma_start(out=xT0_end, in_=xT0_rows[:, :, split:])
+        nc.sync.dma_start(out=tile("xT0", [P, PACK, split], F32)[:], in_=xT0_rows[:, :, 0:split])
+        load("xT1", xT[1])
+        load_weights()
+        load("y0", y[0])
         load("y1", y[1])
+        load("pm", pm)
+        load("xm0", xm[0])
         load("xm1", xm[1])
 
         window = sb.tile([P, T], F32, name="window")
@@ -97,48 +113,55 @@ def tile_attend_gkl_w_prj_kernel(tc, xT, wT, y, wt, xm, pm, offs, out):
             col = (b * N + first) // PER_COLUMN
             return offsets[:, col : col + count // PER_COLUMN]
 
-        def round_table(chunk):
-            u, first, end, split = TABLE_CHUNKS[chunk]
+        def round_table(chunk, on_vector):
+            u, first, end = TABLE_CHUNKS[chunk]
+            split = first + on_vector
             pairs = tile("pairs%d" % u, [P, T], U32)[:].bitcast(BF16).rearrange("p (c e) -> p c e", e=2)
             raw = held["table%d" % chunk][:].rearrange("p e c -> p c e")
-            nc.vector.tensor_copy(out=pairs[:, first:split], in_=raw[:, 0 : split - first])
+            if on_vector > 0:
+                nc.vector.tensor_copy(out=pairs[:, first:split], in_=raw[:, 0:on_vector])
             if split < end:
-                nc.scalar.activation(pairs[:, split:end], raw[:, split - first : end - first], ACT.Copy)
+                nc.scalar.activation(pairs[:, split:end], raw[:, on_vector : end - first], ACT.Copy)
 
-        def gather(u, b, first, count):
+        def gather(u, b, first=0, count=N):
             words = tile("picked%d" % b, [P, 2, N], U32)
             nc.vector.tensor_copy(
                 out=words[:, u, first : first + count], in_=held["pairs%d" % u][:].indirect(listed(b, first, count))
             )
 
-        def pack_table(b):
-            packed = tile("w%d_packed" % b, [P, N * PACK], BF16)[:].rearrange("p (c u e) -> p c u e", u=2, e=2)
-            picked = held["picked%d" % b][:].rearrange("p u c -> p (u c)").bitcast(BF16)
-            picked = picked.rearrange("p (u c e) -> p c u e", u=2, e=2)
-            for h in range(2):
-                part = slice(h * HALF, (h + 1) * HALF)
-                copy(packed[:, part], picked[:, part], SCALAR)
+        def pack_table(b, first=0, end=N):
+            packed = tile("w%d_packed" % b, [P, N * PACK], BF16)[:].bitcast(U32).rearrange("p (c u) -> p c u", u=2)
+            picked = held["picked%d" % b][:].rearrange("p u c -> p c u")
+            nc.scalar.copy(out=packed[:, first:end], in_=picked[:, first:end])
 
-        def pack_xT(b, engine):
+        def shared(dst, src, on_vector):
+            if on_vector > 0:
+                copy(dst[:, 0:on_vector], src[:, 0:on_vector], VECTOR)
+            if on_vector < P:
+                copy(dst[:, on_vector:P], src[:, on_vector:P], SCALAR)
+
+        def pack_xT(b, on_vector):
             packed = tile("xT%d_packed" % b, [P, R * PACK], BF16)
-            copy(
+            shared(
                 packed[:].rearrange("p (t m j) -> p m j t", t=PACK, j=PACK),
                 held["xT%d" % b][:].rearrange("p j (m t) -> p m j t", t=PACK),
-                engine,
+                on_vector,
             )
 
-        def pack_xm(b):
-            packed = tile("xm%d_packed" % b, [P, D * PACK], BF16)[:].rearrange("p (u m e j) -> p m j u e", u=2, e=2, j=PACK)
-            raw = held["xm%d" % b][:].rearrange("p j (m u e) -> p m j u e", u=2, e=2)
-            copy(packed[:, 0:XM_ON_VECTOR], raw[:, 0:XM_ON_VECTOR], VECTOR)
-            copy(packed[:, XM_ON_VECTOR:P], raw[:, XM_ON_VECTOR:P], SCALAR)
+        def pack_xm(b, on_vector):
+            packed = tile("xm%d_packed" % b, [P, D * PACK], BF16)
+            shared(
+                packed[:].rearrange("p (u m e j) -> p m j u e", u=2, e=2, j=PACK),
+                held["xm%d" % b][:].rearrange("p j (m u e) -> p m j u e", u=2, e=2),
+                on_vector,
+            )
 
-        def pack_pm():
+        def pack_pm(engine):
             packed = tile("pm_packed", [P, K * PACK], BF16)
             copy(
                 packed[:].rearrange("p (c i j) -> p c j i", i=PACK, j=PACK),
                 held["pm"][:].rearrange("p j (c i) -> p c j i", i=PACK),
-                SCALAR,
+                engine,
             )
 
         def pack_g(b, h, first, end, engine):
@@ -152,7 +175,9 @@ def tile_attend_gkl_w_prj_kernel(tc, xT, wT, y, wt, xm, pm, offs, out):
 
         def scores(b, t):
             neg_max = tile("neg_max%d" % b, [P, PACK], F32)[:, t : t + 1]
-            a = ps_scores.tile([P, N], F32, name="a")
+            if b == 0 and t >= 2:
+                neg_max = held["xT1_packed"][:, (t - 2) * 2 * R : (t - 2) * 2 * R + 2].bitcast(F32)
+            a = banks[SCORE_BANK[b][t]]
             matmul(a[:], "xT%d" % b, E4M3, slice(t * P, (t + 1) * P), "w%d" % b)
             nc.vector.tensor_reduce(neg_max, a[:], mybir.AxisListType.X, ALU.max, negate=True)
             nc.scalar.activation(
@@ -163,23 +188,24 @@ def tile_attend_gkl_w_prj_kernel(tc, xT, wT, y, wt, xm, pm, offs, out):
                 accum_out=tile("sums%d" % b, [P, PACK], F32)[:, t : t + 1],
             )
 
-        def row_factors(b):
-            inverse = tile("inverse%d" % b, [P, PACK], F32)
+        def invert_sums(b, first, end):
+            nc.vector.reciprocal(tile("inverse%d" % b, [P, PACK], F32)[:, first:end], held["sums%d" % b][:, first:end])
+
+        def row_factors(b, first, end):
             factor = tile("factor%d" % b, [P, PACK], F32)
-            for t in range(0, PACK, 2):
-                nc.vector.reciprocal(inverse[:, t : t + 2], held["sums%d" % b][:, t : t + 2])
-                nc.vector.tensor_tensor(factor[:, t : t + 2], inverse[:, t : t + 2], weights[:, b, t : t + 2], ALU.mult)
+            nc.vector.tensor_tensor(factor[:, first:end], held["inverse%d" % b][:, first:end], weights[:, b, first:end], ALU.mult)
 
-        def weigh_targets(b, engines):
-            for t, engine in enumerate(engines):
-                targets = held["y%d" % b][:, t, :]
-                weight = weights[:, b, t : t + 1]
-                if engine == VECTOR:
-                    nc.vector.tensor_scalar(targets, targets, weight, None, ALU.mult)
-                else:
-                    nc.scalar.activation(targets, targets, ACT.Copy, scale=weight)
+        def weigh_targets(b, t, engine):
+            targets = held["y%d" % b][:, t, :]
+            weight = weights[:, b, t : t + 1]
+            if engine == VECTOR:
+                nc.vector.tensor_scalar(targets, targets, weight, None, ALU.mult)
+            elif engine == SCALAR:
+                nc.scalar.activation(targets, targets, ACT.Copy, scale=weight)
+            else:
+                nc.gpsimd.tensor_scalar(targets, targets, weight, 0.0, ALU.mult, ALU.add)
 
-        def gradient(b, t, first, end):
+        def gradient(b, t, first=0, end=N):
             nc.vector.scalar_tensor_tensor(
                 tile("g_tiles%d" % b, [P, PACK, N], BF16)[:, t, first:end],
                 held["e%d" % b][:, t, first:end],
@@ -189,109 +215,122 @@ def tile_attend_gkl_w_prj_kernel(tc, xT, wT, y, wt, xm, pm, offs, out):
                 ALU.subtract,
             )
 
-        def table_gradient(b, h, q):
-            if q == 0:
-                held["turned%d_%d" % (b, h)] = ps_turned.tile([P, 2, 2, P], F32, name="turned")
-            turned = held["turned%d_%d" % (b, h)]
-            dw = ps_dw.tile([P, D], F32, name="dw")
+        def table_gradient(b, h, q, engine=SCALAR):
+            turned = banks[TURNED_BANK[b][h]][:].rearrange("p (q u i) -> p q u i", q=2, u=2)
+            dw = banks[DW_BANK[b][2 * h + q]]
             matmul(dw[:], "g%d_%d" % (b, h), E5M2, slice(q * P, (q + 1) * P), "xm%d" % b)
-            rounded = tile("dw_rounded%d_%d_%d" % (b, h, q), [P, D], BF16)
-            copy(rounded[:], dw[:], SCALAR)
-            words = rounded[:].bitcast(F32)
+            first = (2 * h + q) * D
+            rounded = tile("dw_rounded%d" % b, [P, PACK * D], BF16)[:, first : first + D]
+            copy(rounded, dw[:], engine)
+            words = rounded.bitcast(F32)
             for u in range(2):
                 nc.tensor.transpose(turned[:, q, u, :], words[:, u * P : (u + 1) * P], ident[:])
 
-        def pack_dw(b, h, engine):
+        def pack_dw(b, h, engine=SCALAR):
             packed = tile("dw%d_%d_packed" % (b, h), [P, HALF * PACK], BF16)
             copy(
                 packed[:].bitcast(F32).rearrange("p (q i u) -> p q i u", q=2, u=2),
-                held["turned%d_%d" % (b, h)][:].rearrange("p q u i -> p q i u"),
+                banks[TURNED_BANK[b][h]][:].rearrange("p (q u i) -> p q i u", q=2, u=2),
                 engine,
             )
 
         def quantise_half(name, b, h, fmt):
             quantise("%s%d_%d" % (name, b, h), HALF, fmt, 0, HALF)
 
-        def project(b, h, engine):
-            dp = ps_dp.tile([P, HALF], F32, name="dp")
-            matmul(dp[:], "pm", E4M3, slice(0, K), "dw%d_%d" % (b, h))
-            copy(tile("dense%d_%d" % (b, h), [P, HALF], F32)[:], dp[:], engine)
+        def project(b, h, engine=SCALAR):
+            dp = banks[DP_BANK[b][h]][:, 0:HALF]
+            matmul(dp, "pm", E4M3, slice(0, K), "dw%d_%d" % (b, h))
+            copy(tile("dense%d_%d" % (b, h), [P, HALF], F32)[:], dp, engine)
 
-        for chunk in range(len(TABLE_CHUNKS)):
-            round_table(chunk)
-        pack_pm()
-        quantise("pm", K, E4M3, 0, K)
+        def scatter(b, h):
+            nc.vector.tensor_copy(out=window[:].indirect(listed(b, h * HALF, HALF)), in_=held["dense%d_%d" % (b, h)][:])
+
+        def vector_share(chunk):
+            u, first, end = TABLE_CHUNKS[chunk]
+            return (end - first) * 5 // 8
+
+        round_table(0, vector_share(0))
+        round_table(1, vector_share(1))
         for b in range(B):
-            gather(0, b, 0, N)
-
-        gather(1, 0, 0, HALF)
-        gather(1, 0, HALF, HALF)
-        pack_table(0)
-        pack_xT(0, VECTOR)
+            gather(0, b)
+        for chunk in range(2, len(TABLE_CHUNKS)):
+            round_table(chunk, vector_share(chunk))
+        for h in range(2):
+            gather(1, 0, h * HALF, HALF)
+        gather(1, 1)
+        pack_table(0, 0, HALF)
+        xT0_packed = tile("xT0_packed", [P, R * PACK], BF16)[:].rearrange("p (t m j) -> p m j t", t=PACK, j=PACK)
+        copy(xT0_packed[:, P - XT0_ON_SCALAR :], xT0_end.rearrange("p j (m t) -> p m j t", t=PACK), SCALAR)
+        copy(xT0_packed[:, 0 : P - XT0_ON_SCALAR], held["xT0"][:].rearrange("p j (m t) -> p m j t", t=PACK), VECTOR)
+        pack_table(0, HALF, N)
         quantise("w0", N, E4M3, 0, N)
         quantise("xT0", R, E4M3, 0, R // 2)
         quantise("xT0", R, E4M3, R // 2, R // 2)
-        gather(1, 1, 0, N)
         pack_table(1)
         quantise("w1", N, E4M3, 0, N)
-
-        for t in range(PACK):
-            scores(0, t)
-        row_factors(0)
-        pack_xT(1, SCALAR)
-        quantise("xT1", R, E4M3, 0, R)
-        weigh_targets(0, [VECTOR, SCALAR, VECTOR, SCALAR])
-        for t in range(PACK):
-            gradient(0, t, 0, N)
-
+        pack_xT(1, 0)
+        scores(0, 0)
+        scores(0, 1)
+        quantise("xT1", R, E4M3, 0, R // 2)
+        scores(0, 2)
+        quantise("xT1", R, E4M3, R // 2, R // 2)
+        scores(0, 3)
+        pack_pm(SCALAR)
+        for b in range(B):
+            for t in range(PACK):
+                weigh_targets(b, t, GPSIMD)
         scores(1, 0)
+        invert_sums(0, 0, PACK)
         scores(1, 1)
-        pack_xm(0)
+        row_factors(0, 0, PACK)
         scores(1, 2)
         scores(1, 3)
-        row_factors(1)
-        quantise("xm0", D, E4M3, 0, D)
-        for h in range(2):
-            pack_g(0, h, 0, HALF, VECTOR)
-            quantise_half("g", 0, h, E5M2)
-
-        weigh_targets(1, [SCALAR, VECTOR, SCALAR, SCALAR])
         for t in range(PACK):
-            gradient(1, t, 0, N if t % 2 else HALF)
-        pack_xm(1)
-        quantise("xm1", D, E4M3, 0, D)
+            gradient(0, t)
+        quantise("pm", K, E4M3, 0, K)
+        invert_sums(1, 0, PACK)
+        pack_xm(0, 0)
+        pack_g(0, 0, 0, HALF, VECTOR)
+        row_factors(1, 0, PACK)
+        pack_g(0, 1, 0, HALF, VECTOR)
         for h in range(2):
-            if h == 1:
-                gradient(1, 0, HALF, N)
-                gradient(1, 2, HALF, N)
-            pack_g(1, h, 0, G1_ON_SCALAR[h], SCALAR)
-            pack_g(1, h, G1_ON_SCALAR[h], HALF, VECTOR)
-            quantise_half("g", 1, h, E5M2)
-
-        table_gradient(0, 0, 0)
-        table_gradient(0, 0, 1)
-        pack_dw(0, 0, VECTOR)
+            quantise_half("g", 0, h, E5M2)
+        quantise("xm0", D, E4M3, 0, D)
+        held["g_tiles1"] = held["xm0_packed"][:].rearrange("p (t c) -> p t c", t=PACK)
+        pack_xm(1, 32)
+        for t in range(PACK):
+            gradient(1, t, 0, HALF)
+        for h in range(2):
+            for q in range(2):
+                table_gradient(0, h, q)
+        for h in range(2):
+            pack_dw(0, h)
+        quantise("xm1", D, E4M3, 0, D)
+        pack_g(1, 0, 0, HALF, VECTOR)
+        gradient(1, 0, HALF, N)
+        quantise_half("g", 1, 0, E5M2)
+        for t in range(1, PACK):
+            gradient(1, t, HALF, N)
         quantise_half("dw", 0, 0, E4M3)
-        table_gradient(0, 1, 0)
-        table_gradient(0, 1, 1)
-        pack_dw(0, 1, VECTOR)
-        project(0, 0, VECTOR)
+        held["g1_1_packed"] = held["dw0_0_packed"]
+        pack_g(1, 1, 0, HALF, VECTOR)
         quantise_half("dw", 0, 1, E4M3)
+        quantise_half("g", 1, 1, E5M2)
         table_gradient(1, 0, 0)
+        project(0, 0)
         table_gradient(1, 0, 1)
-        pack_dw(1, 0, SCALAR)
-        table_gradient(1, 1, 0)
-        project(0, 1, SCALAR)
+        pack_dw(1, 0)
         quantise_half("dw", 1, 0, E4M3)
+        held["dense0_1"] = held["dw_rounded1"][:, D : 2 * D].bitcast(F32)
+        project(0, 1)
+        table_gradient(1, 1, 0)
         table_gradient(1, 1, 1)
-        project(1, 0, SCALAR)
-        pack_dw(1, 1, SCALAR)
+        pack_dw(1, 1)
         quantise_half("dw", 1, 1, E4M3)
-        project(1, 1, SCALAR)
-
+        held["dense1_0"] = held["dw_rounded1"][:, 3 * D : 4 * D].bitcast(F32)
+        project(1, 0)
+        project(1, 1)
         for b in range(B):
             for h in range(2):
-                nc.vector.tensor_copy(
-                    out=window[:].indirect(listed(b, h * HALF, HALF)), in_=held["dense%d_%d" % (b, h)][:]
-                )
+                scatter(b, h)
         nc.sync.dma_start(out=out, in_=window[:])

@@ -27,7 +27,7 @@ SCORE_BANK = [[0, 1, 2, 3], [4, 5, 6, 7]]
 DW_BANK = [[0, 1, 2, 3], [3, 4, 5, 4]]
 TURNED_BANK = [[4, 5], [0, 1]]
 DP_BANK = [[6, 3], [6, 7]]
-XT0_ON_SCALAR = 32
+XT0_ON_SCALAR = 48
 REUSES = {"dw_rounded0": "xm1", "w1_codes": "xT0_packed"}
 
 
@@ -93,14 +93,16 @@ def tile_attend_gkl_w_prj_kernel(tc, xT, wT, y, wt, xm, pm, offs, out):
             load_table(chunk)
         split = R - PACK * XT0_ON_SCALAR
         xT0_rows = xT[0].rearrange("(p j) c -> p j c", j=PACK)
-        xT0_end = tile("w0_packed", [P, N * PACK], BF16)[:, HALF * PACK :].bitcast(F32).rearrange("p (j c) -> p j c", j=PACK)
+        xT0_end = tile("w0_packed", [P, N * PACK], BF16)[:, 0 : 2 * PACK * PACK * XT0_ON_SCALAR].bitcast(F32).rearrange("p (j c) -> p j c", j=PACK)
         nc.sync.dma_start(out=xT0_end, in_=xT0_rows[:, :, split:])
         nc.sync.dma_start(out=tile("xT0", [P, PACK, split], F32)[:], in_=xT0_rows[:, :, 0:split])
         load("xT1", xT[1])
         load_weights()
-        load("y0", y[0])
-        load("y1", y[1])
+        y0_rows = y[0].rearrange("(p t) c -> p t c", t=PACK)
+        for t in range(0, PACK, 2):
+            nc.sync.dma_start(out=tile("y0", [P, PACK, N], F32)[:, t : t + 2], in_=y0_rows[:, t : t + 2])
         load("pm", pm)
+        load("y1", y[1])
         load("xm0", xm[0])
         load("xm1", xm[1])
 
@@ -124,15 +126,13 @@ def tile_attend_gkl_w_prj_kernel(tc, xT, wT, y, wt, xm, pm, offs, out):
                 nc.scalar.activation(pairs[:, split:end], raw[:, on_vector : end - first], ACT.Copy)
 
         def gather(u, b, first=0, count=N):
-            words = tile("picked%d" % b, [P, 2, N], U32)
-            nc.vector.tensor_copy(
-                out=words[:, u, first : first + count], in_=held["pairs%d" % u][:].indirect(listed(b, first, count))
-            )
+            words = held["picked%d_%d" % (b, first // count)][:, u * count : (u + 1) * count]
+            nc.vector.tensor_copy(out=words, in_=held["pairs%d" % u][:].indirect(listed(b, first, count)))
 
         def pack_table(b, first=0, end=N):
             packed = tile("w%d_packed" % b, [P, N * PACK], BF16)[:].bitcast(U32).rearrange("p (c u) -> p c u", u=2)
-            picked = held["picked%d" % b][:].rearrange("p u c -> p c u")
-            nc.scalar.copy(out=packed[:, first:end], in_=picked[:, first:end])
+            picked = held["picked%d_%d" % (b, first // (end - first))].rearrange("p (u c) -> p c u", u=2)
+            nc.scalar.copy(out=packed[:, first:end], in_=picked)
 
         def shared(dst, src, on_vector):
             if on_vector > 0:
@@ -175,8 +175,8 @@ def tile_attend_gkl_w_prj_kernel(tc, xT, wT, y, wt, xm, pm, offs, out):
 
         def scores(b, t):
             neg_max = tile("neg_max%d" % b, [P, PACK], F32)[:, t : t + 1]
-            if b == 0 and t >= 2:
-                neg_max = held["xT1_packed"][:, (t - 2) * 2 * R : (t - 2) * 2 * R + 2].bitcast(F32)
+            if (b, t) == (0, 3):
+                neg_max = held["xT1_packed"][:, 0:2].bitcast(F32)
             a = banks[SCORE_BANK[b][t]]
             matmul(a[:], "xT%d" % b, E4M3, slice(t * P, (t + 1) * P), "w%d" % b)
             nc.vector.tensor_reduce(neg_max, a[:], mybir.AxisListType.X, ALU.max, negate=True)
@@ -197,20 +197,21 @@ def tile_attend_gkl_w_prj_kernel(tc, xT, wT, y, wt, xm, pm, offs, out):
 
         def weigh_targets(b, t, engine):
             targets = held["y%d" % b][:, t, :]
+            weighed = held.setdefault("weighed%d_%d" % (b, t), targets)
             weight = weights[:, b, t : t + 1]
             if engine == VECTOR:
-                nc.vector.tensor_scalar(targets, targets, weight, None, ALU.mult)
+                nc.vector.tensor_scalar(weighed, targets, weight, None, ALU.mult)
             elif engine == SCALAR:
-                nc.scalar.activation(targets, targets, ACT.Copy, scale=weight)
+                nc.scalar.activation(weighed, targets, ACT.Copy, scale=weight)
             else:
-                nc.gpsimd.tensor_scalar(targets, targets, weight, 0.0, ALU.mult, ALU.add)
+                nc.gpsimd.tensor_scalar(weighed, targets, weight, 0.0, ALU.mult, ALU.add)
 
         def gradient(b, t, first=0, end=N):
             nc.vector.scalar_tensor_tensor(
                 tile("g_tiles%d" % b, [P, PACK, N], BF16)[:, t, first:end],
                 held["e%d" % b][:, t, first:end],
                 held["factor%d" % b][:, t : t + 1],
-                held["y%d" % b][:, t, first:end],
+                held["weighed%d_%d" % (b, t)][:, first:end],
                 ALU.mult,
                 ALU.subtract,
             )
@@ -245,23 +246,29 @@ def tile_attend_gkl_w_prj_kernel(tc, xT, wT, y, wt, xm, pm, offs, out):
         def scatter(b, h):
             nc.vector.tensor_copy(out=window[:].indirect(listed(b, h * HALF, HALF)), in_=held["dense%d_%d" % (b, h)][:])
 
+        w1_bytes = tile("w1_bytes", [P, N * PACK], BF16)
+        held["w1_packed"] = w1_bytes[:]
+        held["picked0_0"] = w1_bytes[:, 0 : 2 * N].bitcast(U32)
+        held["picked0_1"] = tile("picked0_end", [P, N], U32)[:]
+        held["picked1_0"] = tile("picked1", [P, 2 * N], U32)[:]
         def vector_share(chunk):
             u, first, end = TABLE_CHUNKS[chunk]
             return (end - first) * 5 // 8
 
         round_table(0, vector_share(0))
         round_table(1, vector_share(1))
-        for b in range(B):
-            gather(0, b)
+        for h in range(2):
+            gather(0, 0, h * HALF, HALF)
+        gather(0, 1)
         for chunk in range(2, len(TABLE_CHUNKS)):
             round_table(chunk, vector_share(chunk))
         for h in range(2):
             gather(1, 0, h * HALF, HALF)
         gather(1, 1)
-        pack_table(0, 0, HALF)
         xT0_packed = tile("xT0_packed", [P, R * PACK], BF16)[:].rearrange("p (t m j) -> p m j t", t=PACK, j=PACK)
         copy(xT0_packed[:, P - XT0_ON_SCALAR :], xT0_end.rearrange("p j (m t) -> p m j t", t=PACK), SCALAR)
         copy(xT0_packed[:, 0 : P - XT0_ON_SCALAR], held["xT0"][:].rearrange("p j (m t) -> p m j t", t=PACK), VECTOR)
+        pack_table(0, 0, HALF)
         pack_table(0, HALF, N)
         quantise("w0", N, E4M3, 0, N)
         quantise("xT0", R, E4M3, 0, R // 2)
@@ -271,14 +278,15 @@ def tile_attend_gkl_w_prj_kernel(tc, xT, wT, y, wt, xm, pm, offs, out):
         pack_xT(1, 0)
         scores(0, 0)
         scores(0, 1)
-        quantise("xT1", R, E4M3, 0, R // 2)
         scores(0, 2)
+        quantise("xT1", R, E4M3, 0, R // 2)
         quantise("xT1", R, E4M3, R // 2, R // 2)
         scores(0, 3)
-        pack_pm(SCALAR)
+        held["weighed0_0"] = held["w1_packed"][:, 0 : 2 * N].bitcast(F32)
+        held["weighed0_2"] = held["xT1_packed"][:, 2 * N :].bitcast(F32)
         for b in range(B):
             for t in range(PACK):
-                weigh_targets(b, t, GPSIMD)
+                weigh_targets(b, t, GPSIMD if b == 0 or t < 2 else SCALAR)
         scores(1, 0)
         invert_sums(0, 0, PACK)
         scores(1, 1)
@@ -287,6 +295,7 @@ def tile_attend_gkl_w_prj_kernel(tc, xT, wT, y, wt, xm, pm, offs, out):
         scores(1, 3)
         for t in range(PACK):
             gradient(0, t)
+        pack_pm(VECTOR)
         quantise("pm", K, E4M3, 0, K)
         invert_sums(1, 0, PACK)
         pack_xm(0, 0)

@@ -20,15 +20,16 @@ P = 128
 PACK = 4
 HALF = N // 2
 PER_COLUMN = 16
-VECTOR, SCALAR, GPSIMD = "vector", "scalar", "gpsimd"
 
-TABLE_CHUNKS = [(0, 0, 1024), (0, 1024, 2048), (1, 0, 1024), (1, 1024, 1536), (1, 1536, 2048)]
-SCORE_BANK = [[0, 1, 2, 3], [4, 5, 6, 7]]
-DW_BANK = [[0, 1, 2, 3], [3, 4, 5, 4]]
-TURNED_BANK = [[4, 5], [0, 1]]
-DP_BANK = [[6, 3], [6, 7]]
+TABLE_LOADS = [(0, 0, 1024, 5), (0, 1024, 2048, 5), (1, 0, 1024, 3), (1, 1024, 1536, 4), (1, 1536, 2048, 5)]
 XT0_ON_SCALAR = 48
-REUSES = {"dw_rounded0": "xm1", "w1_codes": "xT0_packed"}
+XM1_ON_VECTOR = 32
+Y1_ON_GPSIMD = 2
+
+SCORE_BANK = [[0, 1, 2, 3], [4, 5, 6, 7]]
+DW_BANK = [[0, 1, 2, 3], [3, 4, 4, 6]]
+TURNED_BANK = [[4, 4, 5, 5], [0, 0, 1, 2]]
+DP_BANK = [[6, 3], [6, 7]]
 
 
 def tile_attend_gkl_w_prj_kernel(tc, xT, wT, y, wt, xm, pm, offs, out):
@@ -39,24 +40,24 @@ def tile_attend_gkl_w_prj_kernel(tc, xT, wT, y, wt, xm, pm, offs, out):
         banks = [ps.tile([P, N], F32, name="bank%d" % i) for i in range(8)]
         held = {}
 
-        def tile(name, shape, dtype):
+        def tile(name, shape, dtype, tag=None):
             if name not in held:
-                held[name] = sb.tile(shape, dtype, name=name, tag=REUSES.get(name, name), align_bytes=64)
+                held[name] = sb.tile(shape, dtype, name=name, tag=tag or name, align_bytes=64)[:]
             return held[name]
 
-        def copy(dst, src, engine):
-            if engine == VECTOR:
-                nc.vector.tensor_copy(out=dst, in_=src)
-            else:
-                nc.scalar.copy(out=dst, in_=src)
+        def on_vector(dst, src):
+            nc.vector.tensor_copy(out=dst, in_=src)
 
-        def quantise(name, width, fmt, first, count):
-            codes = tile(name + "_codes", [P, width], U32)
-            scales = tile(name + "_scales", [P, width], U8)
+        def on_scalar(dst, src):
+            nc.scalar.copy(out=dst, in_=src)
+
+        def quantise(name, fmt, first, count):
+            packed = held[name + "_packed"]
+            width = packed.shape[1] // PACK
             nc.vector.quantize_mx(
-                out=codes[:, first : first + count].bitcast(fmt),
-                scales=scales[:, first : first + count],
-                in_=held[name + "_packed"][:, PACK * first : PACK * (first + count)],
+                out=tile(name + "_codes", [P, width], U32)[:, first : first + count].bitcast(fmt),
+                scales=tile(name + "_scales", [P, width], U8)[:, first : first + count],
+                in_=packed[:, PACK * first : PACK * (first + count)],
             )
 
         def matmul(dst, stationary, fmt, cols, moving):
@@ -64,43 +65,34 @@ def tile_attend_gkl_w_prj_kernel(tc, xT, wT, y, wt, xm, pm, offs, out):
                 out=dst,
                 lhsT=held[stationary + "_codes"][:, cols].bitcast(fmt),
                 lhsT_scale=held[stationary + "_scales"][:, cols],
-                rhs=held[moving + "_codes"][:].bitcast(E4M3),
-                rhs_scale=held[moving + "_scales"][:],
+                rhs=held[moving + "_codes"].bitcast(E4M3),
+                rhs_scale=held[moving + "_scales"],
                 start=True,
                 stop=True,
             )
 
+        def rows(src):
+            return src.rearrange("(p j) c -> p j c", j=PACK)
+
         def load(name, src):
-            raw = tile(name, [P, PACK, src.shape[1]], F32)
-            nc.sync.dma_start(out=raw[:], in_=src.rearrange("(p j) c -> p j c", j=PACK))
+            nc.sync.dma_start(out=tile(name, [P, PACK, src.shape[1]], F32), in_=rows(src))
 
         offsets = sb.tile([P, B * N // PER_COLUMN], U16, name="offsets")
         table_rows = wT.rearrange("(p u e) c -> p u e c", u=2, e=2)
-
-        def load_table(chunk):
-            u, first, end = TABLE_CHUNKS[chunk]
-            raw = tile("table%d" % chunk, [P, 2, end - first], F32)
-            nc.sync.dma_start(out=raw[:], in_=table_rows[:, u, :, first:end])
-
-        weights = tile("wt", [P, B, PACK], F32)
-
-        def load_weights():
-            nc.sync.dma_start(out=weights[:], in_=wt.rearrange("b (p t) o -> p b (t o)", t=PACK))
-
-        load_table(0)
-        nc.sync.dma_start(offsets[:], offs)
-        for chunk in range(1, len(TABLE_CHUNKS)):
-            load_table(chunk)
+        for part, (u, first, end, eighths) in enumerate(TABLE_LOADS):
+            nc.sync.dma_start(out=tile("table%d" % part, [P, 2, end - first], F32), in_=table_rows[:, u, :, first:end])
+            if part == 0:
+                nc.sync.dma_start(offsets[:], offs)
         split = R - PACK * XT0_ON_SCALAR
-        xT0_rows = xT[0].rearrange("(p j) c -> p j c", j=PACK)
-        xT0_end = tile("w0_packed", [P, N * PACK], BF16)[:, 0 : 2 * PACK * PACK * XT0_ON_SCALAR].bitcast(F32).rearrange("p (j c) -> p j c", j=PACK)
-        nc.sync.dma_start(out=xT0_end, in_=xT0_rows[:, :, split:])
-        nc.sync.dma_start(out=tile("xT0", [P, PACK, split], F32)[:], in_=xT0_rows[:, :, 0:split])
+        xT0_end = tile("w0_packed", [P, N * PACK], BF16)[:, 0 : 2 * PACK * (R - split)].bitcast(F32)
+        xT0_end = xT0_end.rearrange("p (j c) -> p j c", j=PACK)
+        nc.sync.dma_start(out=xT0_end, in_=rows(xT[0])[:, :, split:])
+        nc.sync.dma_start(out=tile("xT0_start", [P, PACK, split], F32), in_=rows(xT[0])[:, :, 0:split])
         load("xT1", xT[1])
-        load_weights()
-        y0_rows = y[0].rearrange("(p t) c -> p t c", t=PACK)
+        weights = tile("wt", [P, B, PACK], F32)
+        nc.sync.dma_start(out=weights, in_=wt.rearrange("b (p t) o -> p b (t o)", t=PACK))
         for t in range(0, PACK, 2):
-            nc.sync.dma_start(out=tile("y0", [P, PACK, N], F32)[:, t : t + 2], in_=y0_rows[:, t : t + 2])
+            nc.sync.dma_start(out=tile("y0", [P, PACK, N], F32)[:, t : t + 2], in_=rows(y[0])[:, t : t + 2])
         load("pm", pm)
         load("y1", y[1])
         load("xm0", xm[0])
@@ -109,237 +101,206 @@ def tile_attend_gkl_w_prj_kernel(tc, xT, wT, y, wt, xm, pm, offs, out):
         window = sb.tile([P, T], F32, name="window")
         nc.gpsimd.memset(window[:], 0.0)
         ident = tile("ident", [P, P], F32)
-        make_identity(nc, ident[:])
+        make_identity(nc, ident)
 
         def listed(b, first, count):
             col = (b * N + first) // PER_COLUMN
             return offsets[:, col : col + count // PER_COLUMN]
 
-        def round_table(chunk, on_vector):
-            u, first, end = TABLE_CHUNKS[chunk]
-            split = first + on_vector
-            pairs = tile("pairs%d" % u, [P, T], U32)[:].bitcast(BF16).rearrange("p (c e) -> p c e", e=2)
-            raw = held["table%d" % chunk][:].rearrange("p e c -> p c e")
-            if on_vector > 0:
-                nc.vector.tensor_copy(out=pairs[:, first:split], in_=raw[:, 0:on_vector])
-            if split < end:
-                nc.scalar.activation(pairs[:, split:end], raw[:, on_vector : end - first], ACT.Copy)
+        def round_table(part):
+            u, first, end, eighths = TABLE_LOADS[part]
+            share = (end - first) * eighths // 8
+            pairs = tile("pairs%d" % u, [P, T], U32).bitcast(BF16).rearrange("p (c e) -> p c e", e=2)[:, first:end]
+            raw = held["table%d" % part].rearrange("p e c -> p c e")
+            on_vector(pairs[:, 0:share], raw[:, 0:share])
+            nc.scalar.activation(pairs[:, share:], raw[:, share:], ACT.Copy)
 
-        def gather(u, b, first=0, count=N):
-            words = held["picked%d_%d" % (b, first // count)][:, u * count : (u + 1) * count]
-            nc.vector.tensor_copy(out=words, in_=held["pairs%d" % u][:].indirect(listed(b, first, count)))
+        runs = [(0, 0, HALF), (0, HALF, HALF), (1, 0, N)]
+        picked = [
+            tile("w1_packed", [P, N * PACK], BF16)[:, 0 : 4 * HALF].bitcast(U32),
+            tile("picked0_end", [P, 2 * HALF], U32),
+            tile("picked1", [P, 2 * N], U32),
+        ]
 
-        def pack_table(b, first=0, end=N):
-            packed = tile("w%d_packed" % b, [P, N * PACK], BF16)[:].bitcast(U32).rearrange("p (c u) -> p c u", u=2)
-            picked = held["picked%d_%d" % (b, first // (end - first))].rearrange("p (u c) -> p c u", u=2)
-            nc.scalar.copy(out=packed[:, first:end], in_=picked)
+        def gather(u):
+            for (b, first, count), words in zip(runs, picked):
+                on_vector(words[:, u * count : (u + 1) * count], held["pairs%d" % u].indirect(listed(b, first, count)))
 
-        def shared(dst, src, on_vector):
-            if on_vector > 0:
-                copy(dst[:, 0:on_vector], src[:, 0:on_vector], VECTOR)
-            if on_vector < P:
-                copy(dst[:, on_vector:P], src[:, on_vector:P], SCALAR)
+        def pack_table(run):
+            b, first, count = runs[run]
+            packed = held["w%d_packed" % b].bitcast(U32).rearrange("p (c u) -> p c u", u=2)
+            on_scalar(packed[:, first : first + count], picked[run].rearrange("p (u c) -> p c u", u=2))
 
-        def pack_xT(b, on_vector):
-            packed = tile("xT%d_packed" % b, [P, R * PACK], BF16)
-            shared(
-                packed[:].rearrange("p (t m j) -> p m j t", t=PACK, j=PACK),
-                held["xT%d" % b][:].rearrange("p j (m t) -> p m j t", t=PACK),
-                on_vector,
-            )
+        def pack_xT(b, raw, first, copy):
+            packed = tile("xT%d_packed" % b, [P, R * PACK], BF16).rearrange("p (t n l j) -> p n j l t", t=PACK, l=2, j=PACK)
+            raw = raw.rearrange("p j (n l t) -> p n j l t", l=2, t=PACK)
+            copy(packed[:, first // 2 : first // 2 + raw.shape[1]], raw)
 
-        def pack_xm(b, on_vector):
-            packed = tile("xm%d_packed" % b, [P, D * PACK], BF16)
-            shared(
-                packed[:].rearrange("p (u m e j) -> p m j u e", u=2, e=2, j=PACK),
-                held["xm%d" % b][:].rearrange("p j (m u e) -> p m j u e", u=2, e=2),
-                on_vector,
-            )
+        def pack_xm(b, first, end, copy):
+            packed = tile("xm%d_packed" % b, [P, D * PACK], BF16).rearrange("p (u m e j) -> p m j u e", u=2, e=2, j=PACK)
+            raw = held["xm%d" % b].rearrange("p j (m u e) -> p m j u e", u=2, e=2)
+            copy(packed[:, first:end], raw[:, first:end])
 
-        def pack_pm(engine):
-            packed = tile("pm_packed", [P, K * PACK], BF16)
-            copy(
-                packed[:].rearrange("p (c i j) -> p c j i", i=PACK, j=PACK),
-                held["pm"][:].rearrange("p j (c i) -> p c j i", i=PACK),
-                engine,
-            )
+        def pack_pm():
+            packed = tile("pm_packed", [P, K * PACK], BF16).rearrange("p (c i j) -> p c j i", i=PACK, j=PACK)
+            on_vector(packed, held["pm"].rearrange("p j (c i) -> p c j i", i=PACK))
 
-        def pack_g(b, h, first, end, engine):
+        def pack_g(b, h):
             packed = tile("g%d_%d_packed" % (b, h), [P, HALF * PACK], BF16)
-            slots = slice(h * HALF + first, h * HALF + end)
-            copy(
-                packed[:, first * PACK : end * PACK].rearrange("p (c s t) -> p c t s", s=PACK, t=PACK),
-                held["g_tiles%d" % b][:, :, slots].rearrange("p t (c s) -> p c t s", s=PACK),
-                engine,
+            on_vector(
+                packed.rearrange("p (c s t) -> p c t s", s=PACK, t=PACK),
+                held["g_tiles%d" % b][:, :, h * HALF : (h + 1) * HALF].rearrange("p t (c s) -> p c t s", s=PACK),
             )
 
-        def scores(b, t):
-            neg_max = tile("neg_max%d" % b, [P, PACK], F32)[:, t : t + 1]
-            if (b, t) == (0, 3):
-                neg_max = held["xT1_packed"][:, 0:2].bitcast(F32)
-            a = banks[SCORE_BANK[b][t]]
-            matmul(a[:], "xT%d" % b, E4M3, slice(t * P, (t + 1) * P), "w%d" % b)
-            nc.vector.tensor_reduce(neg_max, a[:], mybir.AxisListType.X, ALU.max, negate=True)
+        def scores(b, t, neg_max):
+            a = banks[SCORE_BANK[b][t]][:]
+            matmul(a, "xT%d" % b, E4M3, slice(t * P, (t + 1) * P), "w%d" % b)
+            nc.vector.tensor_reduce(neg_max, a, mybir.AxisListType.X, ALU.max, negate=True)
             nc.scalar.activation(
                 tile("e%d" % b, [P, PACK, N], F32)[:, t, :],
-                a[:],
+                a,
                 ACT.Exp,
                 bias=neg_max,
                 accum_out=tile("sums%d" % b, [P, PACK], F32)[:, t : t + 1],
             )
 
-        def invert_sums(b, first, end):
-            nc.vector.reciprocal(tile("inverse%d" % b, [P, PACK], F32)[:, first:end], held["sums%d" % b][:, first:end])
+        def invert_sums(b):
+            nc.vector.reciprocal(tile("inverse%d" % b, [P, PACK], F32), held["sums%d" % b])
 
-        def row_factors(b, first, end):
-            factor = tile("factor%d" % b, [P, PACK], F32)
-            nc.vector.tensor_tensor(factor[:, first:end], held["inverse%d" % b][:, first:end], weights[:, b, first:end], ALU.mult)
+        def row_factors(b):
+            nc.vector.tensor_tensor(tile("factor%d" % b, [P, PACK], F32), held["inverse%d" % b], weights[:, b, :], ALU.mult)
 
-        def weigh_targets(b, t, engine):
-            targets = held["y%d" % b][:, t, :]
-            weighed = held.setdefault("weighed%d_%d" % (b, t), targets)
-            weight = weights[:, b, t : t + 1]
-            if engine == VECTOR:
-                nc.vector.tensor_scalar(weighed, targets, weight, None, ALU.mult)
-            elif engine == SCALAR:
-                nc.scalar.activation(weighed, targets, ACT.Copy, scale=weight)
-            else:
-                nc.gpsimd.tensor_scalar(weighed, targets, weight, 0.0, ALU.mult, ALU.add)
-
-        def gradient(b, t, first=0, end=N):
+        def gradient(b, t, first, end):
             nc.vector.scalar_tensor_tensor(
                 tile("g_tiles%d" % b, [P, PACK, N], BF16)[:, t, first:end],
                 held["e%d" % b][:, t, first:end],
                 held["factor%d" % b][:, t : t + 1],
-                held["weighed%d_%d" % (b, t)][:, first:end],
+                weighed[b][t][:, first:end],
                 ALU.mult,
                 ALU.subtract,
             )
 
-        def table_gradient(b, h, q, engine=SCALAR):
-            turned = banks[TURNED_BANK[b][h]][:].rearrange("p (q u i) -> p q u i", q=2, u=2)
-            dw = banks[DW_BANK[b][2 * h + q]]
-            matmul(dw[:], "g%d_%d" % (b, h), E5M2, slice(q * P, (q + 1) * P), "xm%d" % b)
-            first = (2 * h + q) * D
-            rounded = tile("dw_rounded%d" % b, [P, PACK * D], BF16)[:, first : first + D]
-            copy(rounded, dw[:], engine)
-            words = rounded.bitcast(F32)
-            for u in range(2):
-                nc.tensor.transpose(turned[:, q, u, :], words[:, u * P : (u + 1) * P], ident[:])
+        def rounded(b, block):
+            return tile("dw_rounded%d" % b, [P, N // P * D], BF16)[:, block * D : (block + 1) * D]
 
-        def pack_dw(b, h, engine=SCALAR):
-            packed = tile("dw%d_%d_packed" % (b, h), [P, HALF * PACK], BF16)
-            copy(
-                packed[:].bitcast(F32).rearrange("p (q i u) -> p q i u", q=2, u=2),
-                banks[TURNED_BANK[b][h]][:].rearrange("p (q u i) -> p q i u", q=2, u=2),
-                engine,
+        def turned(b, block):
+            return banks[TURNED_BANK[b][block]][:].rearrange("p (q u i) -> p q u i", q=2, u=2)
+
+        def table_gradient(b, block):
+            h, q = divmod(block, 2)
+            dw = banks[DW_BANK[b][block]][:]
+            matmul(dw, "g%d_%d" % (b, h), E5M2, slice(q * P, (q + 1) * P), "xm%d" % b)
+            on_scalar(rounded(b, block), dw)
+            words = rounded(b, block).bitcast(F32)
+            for u in range(2):
+                nc.tensor.transpose(turned(b, block)[:, q, u, :], words[:, u * P : (u + 1) * P], ident)
+
+        def pack_dw(b, block, count):
+            h, q = divmod(block, 2)
+            packed = tile("dw%d_%d_packed" % (b, h), [P, HALF * PACK], BF16).bitcast(F32)
+            on_scalar(
+                packed.rearrange("p (q i u) -> p q i u", q=2, u=2)[:, q : q + count],
+                turned(b, block).rearrange("p q u i -> p q i u")[:, q : q + count],
             )
 
-        def quantise_half(name, b, h, fmt):
-            quantise("%s%d_%d" % (name, b, h), HALF, fmt, 0, HALF)
-
-        def project(b, h, engine=SCALAR):
+        def project(b, h):
             dp = banks[DP_BANK[b][h]][:, 0:HALF]
             matmul(dp, "pm", E4M3, slice(0, K), "dw%d_%d" % (b, h))
-            copy(tile("dense%d_%d" % (b, h), [P, HALF], F32)[:], dp, engine)
+            on_scalar(tile("dense%d_%d" % (b, h), [P, HALF], F32), dp)
 
-        def scatter(b, h):
-            nc.vector.tensor_copy(out=window[:].indirect(listed(b, h * HALF, HALF)), in_=held["dense%d_%d" % (b, h)][:])
+        for u in range(2):
+            for part in range(len(TABLE_LOADS)):
+                if TABLE_LOADS[part][0] == u:
+                    round_table(part)
+            gather(u)
 
-        w1_bytes = tile("w1_bytes", [P, N * PACK], BF16)
-        held["w1_packed"] = w1_bytes[:]
-        held["picked0_0"] = w1_bytes[:, 0 : 2 * N].bitcast(U32)
-        held["picked0_1"] = tile("picked0_end", [P, N], U32)[:]
-        held["picked1_0"] = tile("picked1", [P, 2 * N], U32)[:]
-        def vector_share(chunk):
-            u, first, end = TABLE_CHUNKS[chunk]
-            return (end - first) * 5 // 8
-
-        round_table(0, vector_share(0))
-        round_table(1, vector_share(1))
-        for h in range(2):
-            gather(0, 0, h * HALF, HALF)
-        gather(0, 1)
-        for chunk in range(2, len(TABLE_CHUNKS)):
-            round_table(chunk, vector_share(chunk))
-        for h in range(2):
-            gather(1, 0, h * HALF, HALF)
-        gather(1, 1)
-        xT0_packed = tile("xT0_packed", [P, R * PACK], BF16)[:].rearrange("p (t m j) -> p m j t", t=PACK, j=PACK)
-        copy(xT0_packed[:, P - XT0_ON_SCALAR :], xT0_end.rearrange("p j (m t) -> p m j t", t=PACK), SCALAR)
-        copy(xT0_packed[:, 0 : P - XT0_ON_SCALAR], held["xT0"][:].rearrange("p j (m t) -> p m j t", t=PACK), VECTOR)
-        pack_table(0, 0, HALF)
-        pack_table(0, HALF, N)
-        quantise("w0", N, E4M3, 0, N)
-        quantise("xT0", R, E4M3, 0, R // 2)
-        quantise("xT0", R, E4M3, R // 2, R // 2)
+        pack_xT(0, xT0_end, P - XT0_ON_SCALAR, on_scalar)
+        pack_xT(0, held["xT0_start"], 0, on_vector)
+        pack_table(0)
         pack_table(1)
-        quantise("w1", N, E4M3, 0, N)
-        pack_xT(1, 0)
-        scores(0, 0)
-        scores(0, 1)
-        scores(0, 2)
-        quantise("xT1", R, E4M3, 0, R // 2)
-        quantise("xT1", R, E4M3, R // 2, R // 2)
-        scores(0, 3)
-        held["weighed0_0"] = held["w1_packed"][:, 0 : 2 * N].bitcast(F32)
-        held["weighed0_2"] = held["xT1_packed"][:, 2 * N :].bitcast(F32)
+        quantise("w0", E4M3, 0, N)
+        quantise("xT0", E4M3, 0, R // 2)
+        quantise("xT0", E4M3, R // 2, R // 2)
+        pack_table(2)
+        tile("w1_codes", [P, N], U32, tag="xT0_packed")
+        quantise("w1", E4M3, 0, N)
+        pack_xT(1, held["xT1"], 0, on_scalar)
+
+        neg_max = [tile("neg_max%d" % b, [P, PACK], F32) for b in range(B)]
+        for t in range(PACK - 1):
+            scores(0, t, neg_max[0][:, t : t + 1])
+        quantise("xT1", E4M3, 0, R // 2)
+        quantise("xT1", E4M3, R // 2, R // 2)
+        scores(0, PACK - 1, held["xT1_packed"][:, 0:2].bitcast(F32))
+
+        weighed = [[held["y%d" % b][:, t, :] for t in range(PACK)] for b in range(B)]
+        weighed[0][0] = held["w1_packed"][:, 0 : 2 * N].bitcast(F32)
+        weighed[0][2] = held["xT1_packed"][:, 2 * N :].bitcast(F32)
         for b in range(B):
             for t in range(PACK):
-                weigh_targets(b, t, GPSIMD if b == 0 or t < 2 else SCALAR)
-        scores(1, 0)
-        invert_sums(0, 0, PACK)
-        scores(1, 1)
-        row_factors(0, 0, PACK)
-        scores(1, 2)
-        scores(1, 3)
+                targets, weight = held["y%d" % b][:, t, :], weights[:, b, t : t + 1]
+                if b == 0 or t < Y1_ON_GPSIMD:
+                    nc.gpsimd.tensor_scalar(weighed[b][t], targets, weight, 0.0, ALU.mult, ALU.add)
+                else:
+                    nc.scalar.activation(weighed[b][t], targets, ACT.Copy, scale=weight)
+
+        scores(1, 0, neg_max[1][:, 0:1])
+        invert_sums(0)
+        scores(1, 1, neg_max[1][:, 1:2])
+        row_factors(0)
+        for t in range(2, PACK):
+            scores(1, t, neg_max[1][:, t : t + 1])
         for t in range(PACK):
-            gradient(0, t)
-        pack_pm(VECTOR)
-        quantise("pm", K, E4M3, 0, K)
-        invert_sums(1, 0, PACK)
-        pack_xm(0, 0)
-        pack_g(0, 0, 0, HALF, VECTOR)
-        row_factors(1, 0, PACK)
-        pack_g(0, 1, 0, HALF, VECTOR)
+            gradient(0, t, 0, N)
+        pack_pm()
+        quantise("pm", E4M3, 0, K)
+        invert_sums(1)
+        pack_xm(0, 0, P, on_scalar)
+        pack_g(0, 0)
+        row_factors(1)
+        pack_g(0, 1)
         for h in range(2):
-            quantise_half("g", 0, h, E5M2)
-        quantise("xm0", D, E4M3, 0, D)
-        held["g_tiles1"] = held["xm0_packed"][:].rearrange("p (t c) -> p t c", t=PACK)
-        pack_xm(1, 32)
+            quantise("g0_%d" % h, E5M2, 0, HALF)
+        quantise("xm0", E4M3, 0, D)
+
+        held["g_tiles1"] = held["xm0_packed"].rearrange("p (t c) -> p t c", t=PACK)
+        pack_xm(1, 0, XM1_ON_VECTOR, on_vector)
+        pack_xm(1, XM1_ON_VECTOR, P, on_scalar)
         for t in range(PACK):
             gradient(1, t, 0, HALF)
+        for block in range(N // P):
+            table_gradient(0, block)
         for h in range(2):
-            for q in range(2):
-                table_gradient(0, h, q)
-        for h in range(2):
-            pack_dw(0, h)
-        quantise("xm1", D, E4M3, 0, D)
-        pack_g(1, 0, 0, HALF, VECTOR)
+            pack_dw(0, 2 * h, 2)
+        quantise("xm1", E4M3, 0, D)
+        pack_g(1, 0)
         gradient(1, 0, HALF, N)
-        quantise_half("g", 1, 0, E5M2)
+        quantise("g1_0", E5M2, 0, HALF)
         for t in range(1, PACK):
             gradient(1, t, HALF, N)
-        quantise_half("dw", 0, 0, E4M3)
+        quantise("dw0_0", E4M3, 0, HALF)
         held["g1_1_packed"] = held["dw0_0_packed"]
-        pack_g(1, 1, 0, HALF, VECTOR)
-        quantise_half("dw", 0, 1, E4M3)
-        quantise_half("g", 1, 1, E5M2)
-        table_gradient(1, 0, 0)
+        pack_g(1, 1)
+        quantise("dw0_1", E4M3, 0, HALF)
+        quantise("g1_1", E5M2, 0, HALF)
+
+        table_gradient(1, 0)
+        table_gradient(1, 1)
         project(0, 0)
-        table_gradient(1, 0, 1)
-        pack_dw(1, 0)
-        quantise_half("dw", 1, 0, E4M3)
-        held["dense0_1"] = held["dw_rounded1"][:, D : 2 * D].bitcast(F32)
+        pack_dw(1, 0, 2)
+        quantise("dw1_0", E4M3, 0, HALF)
+        held["dense0_1"] = rounded(1, 1).bitcast(F32)
         project(0, 1)
-        table_gradient(1, 1, 0)
-        table_gradient(1, 1, 1)
-        pack_dw(1, 1)
-        quantise_half("dw", 1, 1, E4M3)
-        held["dense1_0"] = held["dw_rounded1"][:, 3 * D : 4 * D].bitcast(F32)
+        table_gradient(1, 2)
+        table_gradient(1, 3)
+        for q in range(2):
+            pack_dw(1, 2 + q, 1)
+            quantise("dw1_1", E4M3, q * P, P)
+        held["dense1_0"] = rounded(1, 3).bitcast(F32)
         project(1, 0)
         project(1, 1)
+
         for b in range(B):
             for h in range(2):
-                scatter(b, h)
+                on_vector(window[:].indirect(listed(b, h * HALF, HALF)), held["dense%d_%d" % (b, h)])
         nc.sync.dma_start(out=out, in_=window[:])

@@ -21,7 +21,7 @@ PACK = 4
 HALF = N // 2
 PER_COLUMN = 16
 
-TABLE_LOADS = [(0, 0, 1024, 5), (0, 1024, 2048, 5), (1, 0, 1024, 3), (1, 1024, 1536, 4), (1, 1536, 2048, 5)]
+TABLE_LOADS = [(0, 0, 2048, 5), (1, 0, 1024, 1), (1, 1024, 2048, 5)]
 XT0_ON_SCALAR = 48
 XM1_ON_VECTOR = 32
 Y1_ON_GPSIMD = 2

@@ -90,7 +90,7 @@ def tile_attend_gkl_w_prj_kernel(tc, xT, wT, y, wt, xm, pm, offs, out):
         nc.sync.dma_start(out=tile("xT0_start", [P, PACK, split], F32), in_=rows(xT[0])[:, :, 0:split])
         load("xT1", xT[1])
         weights = tile("wt", [P, B, PACK], F32)
-        nc.sync.dma_start(out=weights, in_=wt.rearrange("b (p t) o -> p b (t o)", t=PACK))
+        nc.scalar.dma_start(out=weights, in_=wt.rearrange("b (p t) o -> p b (t o)", t=PACK))
         for t in range(0, PACK, 2):
             nc.sync.dma_start(out=tile("y0", [P, PACK, N], F32)[:, t : t + 2], in_=rows(y[0])[:, t : t + 2])
         load("pm", pm)

@@ -27,9 +27,9 @@ XM1_ON_VECTOR = 32
 Y1_ON_GPSIMD = 2
 
 SCORE_BANK = [[0, 1, 2, 3], [4, 5, 6, 7]]
-DW_BANK = [[0, 1, 2, 3], [3, 4, 4, 6]]
-TURNED_BANK = [[4, 4, 5, 5], [0, 0, 1, 2]]
-DP_BANK = [[6, 3], [6, 7]]
+DW_BANK = [[0, 1, 2, 3], [3, 4, 3, 4]]
+TURNED_BANK = [[4, 4, 5, 5], [0, 1, 2, 5]]
+DP_BANK = [[6, 1], [6, 7]]
 
 
 def tile_attend_gkl_w_prj_kernel(tc, xT, wT, y, wt, xm, pm, offs, out):
@@ -94,7 +94,8 @@ def tile_attend_gkl_w_prj_kernel(tc, xT, wT, y, wt, xm, pm, offs, out):
         for t in range(0, PACK, 2):
             nc.sync.dma_start(out=tile("y0", [P, PACK, N], F32)[:, t : t + 2], in_=rows(y[0])[:, t : t + 2])
         load("pm", pm)
-        load("y1", y[1])
+        for t in range(0, PACK, 2):
+            nc.sync.dma_start(out=tile("y1", [P, PACK, N], F32)[:, t : t + 2], in_=rows(y[1])[:, t : t + 2])
         load("xm0", xm[0])
         load("xm1", xm[1])
 
@@ -134,7 +135,8 @@ def tile_attend_gkl_w_prj_kernel(tc, xT, wT, y, wt, xm, pm, offs, out):
         def pack_xT(b, raw, first, copy):
             packed = tile("xT%d_packed" % b, [P, R * PACK], BF16).rearrange("p (t n l j) -> p n j l t", t=PACK, l=2, j=PACK)
             raw = raw.rearrange("p j (n l t) -> p n j l t", l=2, t=PACK)
-            copy(packed[:, first // 2 : first // 2 + raw.shape[1]], raw)
+            for t in range(2):
+                copy(packed[:, first // 2 : first // 2 + raw.shape[1], :, :, t::2], raw[:, :, :, :, t::2])
 
         def pack_xm(b, first, end, copy):
             packed = tile("xm%d_packed" % b, [P, D * PACK], BF16).rearrange("p (u m e j) -> p m j u e", u=2, e=2, j=PACK)
@@ -204,9 +206,10 @@ def tile_attend_gkl_w_prj_kernel(tc, xT, wT, y, wt, xm, pm, offs, out):
             )
 
         def project(b, h):
-            dp = banks[DP_BANK[b][h]][:, 0:HALF]
-            matmul(dp, "pm", E4M3, slice(0, K), "dw%d_%d" % (b, h))
-            on_scalar(tile("dense%d_%d" % (b, h), [P, HALF], F32), dp)
+            matmul(banks[DP_BANK[b][h]][:, 0:HALF], "pm", E4M3, slice(0, K), "dw%d_%d" % (b, h))
+
+        def empty(b, h, copy):
+            copy(tile("dense%d_%d" % (b, h), [P, HALF], F32), banks[DP_BANK[b][h]][:, 0:HALF])
 
         for u in range(2):
             for part in range(len(TABLE_LOADS)):
@@ -237,35 +240,36 @@ def tile_attend_gkl_w_prj_kernel(tc, xT, wT, y, wt, xm, pm, offs, out):
         weighed[0][0] = held["w1_packed"][:, 0 : 2 * N].bitcast(F32)
         weighed[0][2] = held["xT1_packed"][:, 2 * N :].bitcast(F32)
         for b in range(B):
-            for t in range(PACK):
-                targets, weight = held["y%d" % b][:, t, :], weights[:, b, t : t + 1]
-                if b == 0 or t < Y1_ON_GPSIMD:
-                    nc.gpsimd.tensor_scalar(weighed[b][t], targets, weight, 0.0, ALU.mult, ALU.add)
-                else:
-                    nc.scalar.activation(weighed[b][t], targets, ACT.Copy, scale=weight)
+            for t in range(PACK if b == 0 else Y1_ON_GPSIMD):
+                nc.gpsimd.tensor_scalar(
+                    weighed[b][t], held["y%d" % b][:, t, :], weights[:, b, t : t + 1], 0.0, ALU.mult, ALU.add
+                )
 
         scores(1, 0, neg_max[1][:, 0:1])
         invert_sums(0)
-        scores(1, 1, neg_max[1][:, 1:2])
-        row_factors(0)
-        for t in range(2, PACK):
+        for t in range(1, PACK):
             scores(1, t, neg_max[1][:, t : t + 1])
+        row_factors(0)
         for t in range(PACK):
             gradient(0, t, 0, N)
         pack_pm()
         quantise("pm", E4M3, 0, K)
         invert_sums(1)
         pack_xm(0, 0, P, on_scalar)
+        for t in range(Y1_ON_GPSIMD, PACK):
+            weighed[1][t] = held["xm0"][:, t, :]
+            nc.scalar.activation(weighed[1][t], held["y1"][:, t, :], ACT.Copy, scale=weights[:, 1, t : t + 1])
+        held["g0_1_packed"] = held["xm0"][:, 0, :].bitcast(BF16)
         pack_g(0, 0)
         row_factors(1)
-        pack_g(0, 1)
-        for h in range(2):
-            quantise("g0_%d" % h, E5M2, 0, HALF)
+        quantise("g0_0", E5M2, 0, HALF)
         quantise("xm0", E4M3, 0, D)
+        pack_g(0, 1)
 
         held["g_tiles1"] = held["xm0_packed"].rearrange("p (t c) -> p t c", t=PACK)
         pack_xm(1, 0, XM1_ON_VECTOR, on_vector)
         pack_xm(1, XM1_ON_VECTOR, P, on_scalar)
+        quantise("g0_1", E5M2, 0, HALF)
         for t in range(PACK):
             gradient(1, t, 0, HALF)
         for block in range(N // P):
@@ -282,23 +286,26 @@ def tile_attend_gkl_w_prj_kernel(tc, xT, wT, y, wt, xm, pm, offs, out):
         held["g1_1_packed"] = held["dw0_0_packed"]
         pack_g(1, 1)
         quantise("dw0_1", E4M3, 0, HALF)
+        project(0, 0)
+        empty(0, 0, on_vector)
         quantise("g1_1", E5M2, 0, HALF)
 
         table_gradient(1, 0)
         table_gradient(1, 1)
-        project(0, 0)
-        pack_dw(1, 0, 2)
-        quantise("dw1_0", E4M3, 0, HALF)
-        held["dense0_1"] = rounded(1, 1).bitcast(F32)
         project(0, 1)
+        pack_dw(1, 0, 1)
+        pack_dw(1, 1, 1)
+        quantise("dw1_0", E4M3, 0, HALF)
+        empty(0, 1, on_scalar)
         table_gradient(1, 2)
         table_gradient(1, 3)
         for q in range(2):
             pack_dw(1, 2 + q, 1)
             quantise("dw1_1", E4M3, q * P, P)
         held["dense1_0"] = rounded(1, 3).bitcast(F32)
-        project(1, 0)
-        project(1, 1)
+        for h in range(2):
+            project(1, h)
+            empty(1, h, on_scalar)
 
         for b in range(B):
             for h in range(2):

@@ -23,13 +23,14 @@ PER_COLUMN = 16
 
 TABLE_LOADS = [(0, 0, 2048, 5), (1, 0, 1024, 1), (1, 1024, 2048, 5)]
 XT0_ON_SCALAR = 48
-XM1_ON_VECTOR = 32
+XM1_ON_VECTOR = 16
+XM0_ON_GPSIMD = 64
 Y1_ON_GPSIMD = 2
 
 SCORE_BANK = [[0, 1, 2, 3], [4, 5, 6, 7]]
-DW_BANK = [[0, 1, 2, 3], [3, 4, 3, 4]]
-TURNED_BANK = [[4, 4, 5, 5], [0, 1, 2, 5]]
-DP_BANK = [[6, 1], [6, 7]]
+DW_BANK = [[0, 1, 2, 3], [3, 4, 3, 7]]
+TURNED_BANK = [[4, 4, 5, 5], [0, 0, 2, 5]]
+DP_BANK = [[6, 4], [3, 6]]
 
 
 def tile_attend_gkl_w_prj_kernel(tc, xT, wT, y, wt, xm, pm, offs, out):
@@ -94,10 +95,10 @@ def tile_attend_gkl_w_prj_kernel(tc, xT, wT, y, wt, xm, pm, offs, out):
         for t in range(0, PACK, 2):
             nc.sync.dma_start(out=tile("y0", [P, PACK, N], F32)[:, t : t + 2], in_=rows(y[0])[:, t : t + 2])
         load("pm", pm)
-        for t in range(0, PACK, 2):
-            nc.sync.dma_start(out=tile("y1", [P, PACK, N], F32)[:, t : t + 2], in_=rows(y[1])[:, t : t + 2])
         load("xm0", xm[0])
+        nc.sync.dma_start(out=tile("y1", [P, PACK, N], F32)[:, 0:2], in_=rows(y[1])[:, 0:2])
         load("xm1", xm[1])
+        nc.sync.dma_start(out=held["y1"][:, 2:], in_=rows(y[1])[:, 2:])
 
         window = sb.tile([P, T], F32, name="window")
         nc.gpsimd.memset(window[:], 0.0)
@@ -147,9 +148,9 @@ def tile_attend_gkl_w_prj_kernel(tc, xT, wT, y, wt, xm, pm, offs, out):
             packed = tile("pm_packed", [P, K * PACK], BF16).rearrange("p (c i j) -> p c j i", i=PACK, j=PACK)
             on_vector(packed, held["pm"].rearrange("p j (c i) -> p c j i", i=PACK))
 
-        def pack_g(b, h):
+        def pack_g(b, h, copy):
             packed = tile("g%d_%d_packed" % (b, h), [P, HALF * PACK], BF16)
-            on_vector(
+            copy(
                 packed.rearrange("p (c s t) -> p c t s", s=PACK, t=PACK),
                 held["g_tiles%d" % b][:, :, h * HALF : (h + 1) * HALF].rearrange("p t (c s) -> p c t s", s=PACK),
             )
@@ -182,8 +183,26 @@ def tile_attend_gkl_w_prj_kernel(tc, xT, wT, y, wt, xm, pm, offs, out):
                 ALU.subtract,
             )
 
+        def difference(t, first, end):
+            e = held["e1"][:, t, first:end]
+            nc.vector.scalar_tensor_tensor(
+                e, e, held["inverse1"][:, t : t + 1], held["y1"][:, t, first:end], ALU.mult, ALU.subtract
+            )
+
+        def weigh_and_pack(h):
+            packed = tile("g1_%d_packed" % h, [P, HALF * PACK], BF16)
+            weight = weights[:, 1, :].rearrange("p (c t s) -> p c t s", c=1, s=1)
+            nc.vector.tensor_tensor(
+                packed.rearrange("p (c s t) -> p c t s", s=PACK, t=PACK),
+                held["e1"][:, :, h * HALF : (h + 1) * HALF].rearrange("p t (c s) -> p c t s", s=PACK),
+                weight.to_broadcast([P, HALF // PACK, PACK, PACK]),
+                ALU.mult,
+            )
+
         def rounded(b, block):
-            return tile("dw_rounded%d" % b, [P, N // P * D], BF16)[:, block * D : (block + 1) * D]
+            if b == 0:
+                return held["xm1"][:, block, 0 : D // 2].bitcast(BF16)
+            return tile("dw_rounded1", [P, N // P * D], BF16)[:, block * D : (block + 1) * D]
 
         def turned(b, block):
             return banks[TURNED_BANK[b][block]][:].rearrange("p (q u i) -> p q u i", q=2, u=2)
@@ -236,14 +255,14 @@ def tile_attend_gkl_w_prj_kernel(tc, xT, wT, y, wt, xm, pm, offs, out):
         quantise("xT1", E4M3, R // 2, R // 2)
         scores(0, PACK - 1, held["xT1_packed"][:, 0:2].bitcast(F32))
 
-        weighed = [[held["y%d" % b][:, t, :] for t in range(PACK)] for b in range(B)]
+        weighed = [[held["y0"][:, t, :] for t in range(PACK)]]
         weighed[0][0] = held["w1_packed"][:, 0 : 2 * N].bitcast(F32)
         weighed[0][2] = held["xT1_packed"][:, 2 * N :].bitcast(F32)
-        for b in range(B):
-            for t in range(PACK if b == 0 else Y1_ON_GPSIMD):
-                nc.gpsimd.tensor_scalar(
-                    weighed[b][t], held["y%d" % b][:, t, :], weights[:, b, t : t + 1], 0.0, ALU.mult, ALU.add
-                )
+        for t in range(PACK):
+            nc.gpsimd.tensor_scalar(weighed[0][t], held["y0"][:, t, :], weights[:, 0, t : t + 1], 0.0, ALU.mult, ALU.add)
+        packed = tile("xm0_packed", [P, D * PACK], BF16).rearrange("p (u m e j) -> p u m j e", u=2, e=2, j=PACK)
+        raw = held["xm0"].rearrange("p j (m u e) -> p u m j e", u=2, e=2)
+        nc.gpsimd.tensor_scalar(packed[:, 0, 0:XM0_ON_GPSIMD], raw[:, 0, 0:XM0_ON_GPSIMD], 1.0, 0.0, ALU.mult, ALU.add)
 
         scores(1, 0, neg_max[1][:, 0:1])
         invert_sums(0)
@@ -255,36 +274,32 @@ def tile_attend_gkl_w_prj_kernel(tc, xT, wT, y, wt, xm, pm, offs, out):
         pack_pm()
         quantise("pm", E4M3, 0, K)
         invert_sums(1)
-        pack_xm(0, 0, P, on_scalar)
-        for t in range(Y1_ON_GPSIMD, PACK):
-            weighed[1][t] = held["xm0"][:, t, :]
-            nc.scalar.activation(weighed[1][t], held["y1"][:, t, :], ACT.Copy, scale=weights[:, 1, t : t + 1])
-        held["g0_1_packed"] = held["xm0"][:, 0, :].bitcast(BF16)
-        pack_g(0, 0)
-        row_factors(1)
-        quantise("g0_0", E5M2, 0, HALF)
+        on_scalar(packed[:, 1, 0:XM0_ON_GPSIMD], raw[:, 1, 0:XM0_ON_GPSIMD])
+        pack_xm(0, XM0_ON_GPSIMD, P, on_scalar)
+        pack_g(0, 0, on_vector)
         quantise("xm0", E4M3, 0, D)
-        pack_g(0, 1)
+        pack_g(0, 1, on_scalar)
+        for h in range(2):
+            quantise("g0_%d" % h, E5M2, 0, HALF)
 
-        held["g_tiles1"] = held["xm0_packed"].rearrange("p (t c) -> p t c", t=PACK)
-        pack_xm(1, 0, XM1_ON_VECTOR, on_vector)
-        pack_xm(1, XM1_ON_VECTOR, P, on_scalar)
-        quantise("g0_1", E5M2, 0, HALF)
+        pack_xm(1, 0, P // 2, on_scalar)
+        pack_xm(1, P // 2, P - XM1_ON_VECTOR, on_scalar)
+        pack_xm(1, P - XM1_ON_VECTOR, P, on_vector)
         for t in range(PACK):
-            gradient(1, t, 0, HALF)
+            difference(t, 0, HALF)
         for block in range(N // P):
             table_gradient(0, block)
         for h in range(2):
             pack_dw(0, 2 * h, 2)
         quantise("xm1", E4M3, 0, D)
-        pack_g(1, 0)
-        gradient(1, 0, HALF, N)
+        weigh_and_pack(0)
+        difference(0, HALF, N)
         quantise("g1_0", E5M2, 0, HALF)
         for t in range(1, PACK):
-            gradient(1, t, HALF, N)
+            difference(t, HALF, N)
         quantise("dw0_0", E4M3, 0, HALF)
         held["g1_1_packed"] = held["dw0_0_packed"]
-        pack_g(1, 1)
+        weigh_and_pack(1)
         quantise("dw0_1", E4M3, 0, HALF)
         project(0, 0)
         empty(0, 0, on_vector)
@@ -293,8 +308,7 @@ def tile_attend_gkl_w_prj_kernel(tc, xT, wT, y, wt, xm, pm, offs, out):
         table_gradient(1, 0)
         table_gradient(1, 1)
         project(0, 1)
-        pack_dw(1, 0, 1)
-        pack_dw(1, 1, 1)
+        pack_dw(1, 0, 2)
         quantise("dw1_0", E4M3, 0, HALF)
         empty(0, 1, on_scalar)
         table_gradient(1, 2)

@@ -21,10 +21,10 @@ PACK = 4
 HALF = N // 2
 PER_COLUMN = 16
 
-TABLE_LOADS = [(0, 0, 2048, 5), (1, 0, 1024, 1), (1, 1024, 2048, 5)]
+TABLE_LOADS = [(0, 0, 1024, 5), (0, 1024, 2048, 5), (1, 0, 1280, 3), (1, 1280, 1792, 5), (1, 1792, 2048, 5)]
 XT0_ON_SCALAR = 48
 XM1_ON_VECTOR = 16
-XM0_ON_GPSIMD = 64
+XM0_ON_GPSIMD = 96
 Y1_ON_GPSIMD = 2
 
 SCORE_BANK = [[0, 1, 2, 3], [4, 5, 6, 7]]
@@ -244,7 +244,7 @@ def tile_attend_gkl_w_prj_kernel(tc, xT, wT, y, wt, xm, pm, offs, out):
         quantise("xT0", E4M3, 0, R // 2)
         quantise("xT0", E4M3, R // 2, R // 2)
         pack_table(2)
-        tile("w1_codes", [P, N], U32, tag="xT0_packed")
+        tile("w1_codes", [P, N], U32, tag="xT0_start")
         quantise("w1", E4M3, 0, N)
         pack_xT(1, held["xT1"], 0, on_scalar)
 
@@ -269,22 +269,22 @@ def tile_attend_gkl_w_prj_kernel(tc, xT, wT, y, wt, xm, pm, offs, out):
         for t in range(1, PACK):
             scores(1, t, neg_max[1][:, t : t + 1])
         row_factors(0)
-        for t in range(PACK):
-            gradient(0, t, 0, N)
+        for first in (HALF, 0):
+            for t in range(PACK):
+                gradient(0, t, first, first + HALF)
         pack_pm()
         quantise("pm", E4M3, 0, K)
         invert_sums(1)
+        pack_g(0, 1, on_scalar)
         on_scalar(packed[:, 1, 0:XM0_ON_GPSIMD], raw[:, 1, 0:XM0_ON_GPSIMD])
         pack_xm(0, XM0_ON_GPSIMD, P, on_scalar)
         pack_g(0, 0, on_vector)
         quantise("xm0", E4M3, 0, D)
-        pack_g(0, 1, on_scalar)
         for h in range(2):
             quantise("g0_%d" % h, E5M2, 0, HALF)
 
         pack_xm(1, 0, P // 2, on_scalar)
-        pack_xm(1, P // 2, P - XM1_ON_VECTOR, on_scalar)
-        pack_xm(1, P - XM1_ON_VECTOR, P, on_vector)
+        pack_xm(1, P // 2, P, on_scalar)
         for t in range(PACK):
             difference(t, 0, HALF)
         for block in range(N // P):

@@ -21,7 +21,7 @@ PACK = 4
 HALF = N // 2
 PER_COLUMN = 16
 
-TABLE_LOADS = [(0, 0, 1024, 5), (0, 1024, 2048, 5), (1, 0, 1280, 3), (1, 1280, 1792, 5), (1, 1792, 2048, 5)]
+TABLE_LOADS = [(0, 0, 1280, 5), (0, 1280, 2048, 5), (1, 0, 1280, 4), (1, 1280, 1792, 5), (1, 1792, 2048, 5)]
 XT0_ON_SCALAR = 48
 XM1_ON_VECTOR = 16
 XM0_ON_GPSIMD = 96
@@ -136,8 +136,7 @@ def tile_attend_gkl_w_prj_kernel(tc, xT, wT, y, wt, xm, pm, offs, out):
         def pack_xT(b, raw, first, copy):
             packed = tile("xT%d_packed" % b, [P, R * PACK], BF16).rearrange("p (t n l j) -> p n j l t", t=PACK, l=2, j=PACK)
             raw = raw.rearrange("p j (n l t) -> p n j l t", l=2, t=PACK)
-            for t in range(2):
-                copy(packed[:, first // 2 : first // 2 + raw.shape[1], :, :, t::2], raw[:, :, :, :, t::2])
+            copy(packed[:, first // 2 : first // 2 + raw.shape[1]], raw)
 
         def pack_xm(b, first, end, copy):
             packed = tile("xm%d_packed" % b, [P, D * PACK], BF16).rearrange("p (u m e j) -> p m j u e", u=2, e=2, j=PACK)

@@ -61,13 +61,13 @@ def tile_attend_gkl_w_prj_kernel(tc, xT, wT, y, wt, xm, pm, offs, out):
                 in_=packed[:, PACK * first : PACK * (first + count)],
             )
 
-        def matmul(dst, stationary, fmt, cols, moving):
+        def matmul(dst, stationary, fmt, cols, moving, part=slice(None)):
             nc.tensor.matmul_mx(
                 out=dst,
                 lhsT=held[stationary + "_codes"][:, cols].bitcast(fmt),
                 lhsT_scale=held[stationary + "_scales"][:, cols],
-                rhs=held[moving + "_codes"].bitcast(E4M3),
-                rhs_scale=held[moving + "_scales"],
+                rhs=held[moving + "_codes"][:, part].bitcast(E4M3),
+                rhs_scale=held[moving + "_scales"][:, part],
                 start=True,
                 stop=True,
             )
@@ -89,11 +89,14 @@ def tile_attend_gkl_w_prj_kernel(tc, xT, wT, y, wt, xm, pm, offs, out):
         xT0_end = xT0_end.rearrange("p (j c) -> p j c", j=PACK)
         nc.sync.dma_start(out=xT0_end, in_=rows(xT[0])[:, :, split:])
         nc.sync.dma_start(out=tile("xT0_start", [P, PACK, split], F32), in_=rows(xT[0])[:, :, 0:split])
-        load("xT1", xT[1])
+        for h in range(2):
+            nc.sync.dma_start(
+                out=tile("xT1_%d" % h, [P, PACK, R // 2], F32), in_=rows(xT[1])[:, :, h * R // 2 : (h + 1) * R // 2]
+            )
+            nc.sync.dma_start(out=tile("y0", [P, PACK, N], F32)[:, h], in_=rows(y[0])[:, h])
         weights = tile("wt", [P, B, PACK], F32)
         nc.scalar.dma_start(out=weights, in_=wt.rearrange("b (p t) o -> p b (t o)", t=PACK))
-        for t in range(0, PACK, 2):
-            nc.sync.dma_start(out=tile("y0", [P, PACK, N], F32)[:, t : t + 2], in_=rows(y[0])[:, t : t + 2])
+        nc.sync.dma_start(out=held["y0"][:, 2:], in_=rows(y[0])[:, 2:])
         load("pm", pm)
         load("xm0", xm[0])
         nc.sync.dma_start(out=tile("y1", [P, PACK, N], F32)[:, 0:2], in_=rows(y[1])[:, 0:2])
@@ -156,7 +159,8 @@ def tile_attend_gkl_w_prj_kernel(tc, xT, wT, y, wt, xm, pm, offs, out):
 
         def scores(b, t, neg_max):
             a = banks[SCORE_BANK[b][t]][:]
-            matmul(a, "xT%d" % b, E4M3, slice(t * P, (t + 1) * P), "w%d" % b)
+            for part in [slice(0, HALF), slice(HALF, N)] if b == t == 0 else [slice(0, N)]:
+                matmul(a[:, part], "xT%d" % b, E4M3, slice(t * P, (t + 1) * P), "w%d" % b, part)
             nc.vector.tensor_reduce(neg_max, a, mybir.AxisListType.X, ALU.max, negate=True)
             nc.scalar.activation(
                 tile("e%d" % b, [P, PACK, N], F32)[:, t, :],
@@ -239,13 +243,14 @@ def tile_attend_gkl_w_prj_kernel(tc, xT, wT, y, wt, xm, pm, offs, out):
         pack_xT(0, held["xT0_start"], 0, on_vector)
         pack_table(0)
         pack_table(1)
-        quantise("w0", E4M3, 0, N)
-        quantise("xT0", E4M3, 0, R // 2)
-        quantise("xT0", E4M3, R // 2, R // 2)
+        for h in range(2):
+            quantise("w0", E4M3, h * HALF, HALF)
+            quantise("xT0", E4M3, h * R // 2, R // 2)
         pack_table(2)
         tile("w1_codes", [P, N], U32, tag="xT0_start")
         quantise("w1", E4M3, 0, N)
-        pack_xT(1, held["xT1"], 0, on_scalar)
+        for h in range(2):
+            pack_xT(1, held["xT1_%d" % h], h * P // 2, on_scalar)
 
         neg_max = [tile("neg_max%d" % b, [P, PACK], F32) for b in range(B)]
         for t in range(PACK - 1):

@@ -139,7 +139,8 @@ def tile_attend_gkl_w_prj_kernel(tc, xT, wT, y, wt, xm, pm, offs, out):
         def pack_xT(b, raw, first, copy):
             packed = tile("xT%d_packed" % b, [P, R * PACK], BF16).rearrange("p (t n l j) -> p n j l t", t=PACK, l=2, j=PACK)
             raw = raw.rearrange("p j (n l t) -> p n j l t", l=2, t=PACK)
-            copy(packed[:, first // 2 : first // 2 + raw.shape[1]], raw)
+            for t in range(2):
+                copy(packed[:, first // 2 : first // 2 + raw.shape[1], :, :, t::2], raw[:, :, :, :, t::2])
 
         def pack_xm(b, first, end, copy):
             packed = tile("xm%d_packed" % b, [P, D * PACK], BF16).rearrange("p (u m e j) -> p m j u e", u=2, e=2, j=PACK)

@@ -1,7 +1,6 @@
 from contextlib import ExitStack
 
 import concourse.mybir as mybir
-from concourse.masks import make_identity
 
 B, N, T, D, R, K = 2, 512, 2048, 512, 512, 128
 FLOPS = 2 * B * (R * D * N + R * D * N + D * K * N)
@@ -19,18 +18,11 @@ ACT = mybir.ActivationFunctionType
 P = 128
 PACK = 4
 HALF = N // 2
+BLOCK = 128
 PER_COLUMN = 16
 
 TABLE_LOADS = [(0, 0, 1280, 5), (0, 1280, 2048, 5), (1, 0, 1280, 4), (1, 1280, 1792, 5), (1, 1792, 2048, 5)]
 XT0_ON_SCALAR = 48
-XM1_ON_VECTOR = 16
-XM0_ON_GPSIMD = 96
-Y1_ON_GPSIMD = 2
-
-SCORE_BANK = [[0, 1, 2, 3], [4, 5, 6, 7]]
-DW_BANK = [[0, 1, 2, 3], [3, 4, 3, 7]]
-TURNED_BANK = [[4, 4, 5, 5], [0, 0, 2, 5]]
-DP_BANK = [[6, 4], [3, 6]]
 
 
 def tile_attend_gkl_w_prj_kernel(tc, xT, wT, y, wt, xm, pm, offs, out):
@@ -52,21 +44,24 @@ def tile_attend_gkl_w_prj_kernel(tc, xT, wT, y, wt, xm, pm, offs, out):
         def on_scalar(dst, src):
             nc.scalar.copy(out=dst, in_=src)
 
+        def packed(name, width=N):
+            return tile(name + "_packed", [P, width * PACK], BF16)
+
         def quantise(name, fmt, first, count):
-            packed = held[name + "_packed"]
-            width = packed.shape[1] // PACK
+            source = held[name + "_packed"]
+            width = source.shape[1] // PACK
             nc.vector.quantize_mx(
                 out=tile(name + "_codes", [P, width], U32)[:, first : first + count].bitcast(fmt),
                 scales=tile(name + "_scales", [P, width], U8)[:, first : first + count],
-                in_=packed[:, PACK * first : PACK * (first + count)],
+                in_=source[:, PACK * first : PACK * (first + count)],
             )
 
-        def matmul(dst, stationary, fmt, cols, moving, part=slice(None)):
+        def matmul(dst, stationary, cols, moving, fmt, part):
             nc.tensor.matmul_mx(
                 out=dst,
-                lhsT=held[stationary + "_codes"][:, cols].bitcast(fmt),
+                lhsT=held[stationary + "_codes"][:, cols].bitcast(E4M3),
                 lhsT_scale=held[stationary + "_scales"][:, cols],
-                rhs=held[moving + "_codes"][:, part].bitcast(E4M3),
+                rhs=held[moving + "_codes"][:, part].bitcast(fmt),
                 rhs_scale=held[moving + "_scales"][:, part],
                 start=True,
                 stop=True,
@@ -75,42 +70,26 @@ def tile_attend_gkl_w_prj_kernel(tc, xT, wT, y, wt, xm, pm, offs, out):
         def rows(src):
             return src.rearrange("(p j) c -> p j c", j=PACK)
 
-        def load(name, src):
-            nc.sync.dma_start(out=tile(name, [P, PACK, src.shape[1]], F32), in_=rows(src))
+        def load_columns(name, src, first, end):
+            nc.sync.dma_start(out=tile(name, [P, PACK, end - first], F32), in_=rows(src)[:, :, first:end])
+
+        def load_targets(b, first, end):
+            nc.sync.dma_start(out=tile("y%d" % b, [P, PACK, N], F32)[:, first:end], in_=rows(y[b])[:, first:end])
 
         offsets = sb.tile([P, B * N // PER_COLUMN], U16, name="offsets")
-        table_rows = wT.rearrange("(p u e) c -> p u e c", u=2, e=2)
-        for part, (u, first, end, eighths) in enumerate(TABLE_LOADS):
-            nc.sync.dma_start(out=tile("table%d" % part, [P, 2, end - first], F32), in_=table_rows[:, u, :, first:end])
-            if part == 0:
-                nc.sync.dma_start(offsets[:], offs)
-        split = R - PACK * XT0_ON_SCALAR
-        xT0_end = tile("w0_packed", [P, N * PACK], BF16)[:, 0 : 2 * PACK * (R - split)].bitcast(F32)
-        xT0_end = xT0_end.rearrange("p (j c) -> p j c", j=PACK)
-        nc.sync.dma_start(out=xT0_end, in_=rows(xT[0])[:, :, split:])
-        nc.sync.dma_start(out=tile("xT0_start", [P, PACK, split], F32), in_=rows(xT[0])[:, :, 0:split])
-        for h in range(2):
-            nc.sync.dma_start(
-                out=tile("xT1_%d" % h, [P, PACK, R // 2], F32), in_=rows(xT[1])[:, :, h * R // 2 : (h + 1) * R // 2]
-            )
-            nc.sync.dma_start(out=tile("y0", [P, PACK, N], F32)[:, h], in_=rows(y[0])[:, h])
-        weights = tile("wt", [P, B, PACK], F32)
-        nc.scalar.dma_start(out=weights, in_=wt.rearrange("b (p t) o -> p b (t o)", t=PACK))
-        nc.sync.dma_start(out=held["y0"][:, 2:], in_=rows(y[0])[:, 2:])
-        load("pm", pm)
-        load("xm0", xm[0])
-        nc.sync.dma_start(out=tile("y1", [P, PACK, N], F32)[:, 0:2], in_=rows(y[1])[:, 0:2])
-        load("xm1", xm[1])
-        nc.sync.dma_start(out=held["y1"][:, 2:], in_=rows(y[1])[:, 2:])
-
         window = sb.tile([P, T], F32, name="window")
-        nc.gpsimd.memset(window[:], 0.0)
-        ident = tile("ident", [P, P], F32)
-        make_identity(nc, ident)
+        weights = tile("wt", [P, B, PACK], F32)
 
         def listed(b, first, count):
             col = (b * N + first) // PER_COLUMN
             return offsets[:, col : col + count // PER_COLUMN]
+
+        def load_table():
+            table_rows = wT.rearrange("(p u e) c -> p u e c", u=2, e=2)
+            for part, (u, first, end, eighths) in enumerate(TABLE_LOADS):
+                nc.sync.dma_start(out=tile("table%d" % part, [P, 2, end - first], F32), in_=table_rows[:, u, :, first:end])
+                if part == 0:
+                    nc.sync.dma_start(offsets[:], offs)
 
         def round_table(part):
             u, first, end, eighths = TABLE_LOADS[part]
@@ -120,52 +99,33 @@ def tile_attend_gkl_w_prj_kernel(tc, xT, wT, y, wt, xm, pm, offs, out):
             on_vector(pairs[:, 0:share], raw[:, 0:share])
             nc.scalar.activation(pairs[:, share:], raw[:, share:], ACT.Copy)
 
-        runs = [(0, 0, HALF), (0, HALF, HALF), (1, 0, N)]
-        picked = [
-            tile("w1_packed", [P, N * PACK], BF16)[:, 0 : 4 * HALF].bitcast(U32),
-            tile("picked0_end", [P, 2 * HALF], U32),
-            tile("picked1", [P, 2 * N], U32),
-        ]
+        def gather(u, b, h):
+            words = tile("picked%d_%d" % (b, h), [P, 2 * HALF], U32)
+            on_vector(words[:, u * HALF : (u + 1) * HALF], held["pairs%d" % u].indirect(listed(b, h * HALF, HALF)))
 
-        def gather(u):
-            for (b, first, count), words in zip(runs, picked):
-                on_vector(words[:, u * count : (u + 1) * count], held["pairs%d" % u].indirect(listed(b, first, count)))
+        def weave(b, h, copy):
+            dst = packed("w%d" % b).bitcast(U32).rearrange("p (c u) -> p c u", u=2)
+            copy(dst[:, h * HALF : (h + 1) * HALF], held["picked%d_%d" % (b, h)].rearrange("p (u c) -> p c u", u=2))
 
-        def pack_table(run):
-            b, first, count = runs[run]
-            packed = held["w%d_packed" % b].bitcast(U32).rearrange("p (c u) -> p c u", u=2)
-            on_scalar(packed[:, first : first + count], picked[run].rearrange("p (u c) -> p c u", u=2))
+        def deal(name, raw, raw_first, first, end, copy):
+            dst = packed(name).rearrange("p (t n l j) -> p n j l t", t=PACK, l=2, j=PACK)
+            src = raw.rearrange("p j (n l t) -> p n j l t", l=2, t=PACK)
+            copy(dst[:, first // 2 : end // 2], src[:, (first - raw_first) // 2 : (end - raw_first) // 2])
 
-        def pack_xT(b, raw, first, copy):
-            packed = tile("xT%d_packed" % b, [P, R * PACK], BF16).rearrange("p (t n l j) -> p n j l t", t=PACK, l=2, j=PACK)
-            raw = raw.rearrange("p j (n l t) -> p n j l t", l=2, t=PACK)
-            for t in range(2):
-                copy(packed[:, first // 2 : first // 2 + raw.shape[1], :, :, t::2], raw[:, :, :, :, t::2])
+        def pack_pm(copy):
+            dst = packed("pm", K).rearrange("p (c i j) -> p c j i", i=PACK, j=PACK)
+            copy(dst, held["pm"].rearrange("p j (c i) -> p c j i", i=PACK))
 
-        def pack_xm(b, first, end, copy):
-            packed = tile("xm%d_packed" % b, [P, D * PACK], BF16).rearrange("p (u m e j) -> p m j u e", u=2, e=2, j=PACK)
-            raw = held["xm%d" % b].rearrange("p j (m u e) -> p m j u e", u=2, e=2)
-            copy(packed[:, first:end], raw[:, first:end])
+        def score(b, t, bank):
+            matmul(banks[bank][:], "xT%d" % b, slice(t * P, (t + 1) * P), "w%d" % b, E4M3, slice(0, N))
 
-        def pack_pm():
-            packed = tile("pm_packed", [P, K * PACK], BF16).rearrange("p (c i j) -> p c j i", i=PACK, j=PACK)
-            on_vector(packed, held["pm"].rearrange("p j (c i) -> p c j i", i=PACK))
+        def row_max(bank, neg_max):
+            nc.vector.tensor_reduce(neg_max, banks[bank][:], mybir.AxisListType.X, ALU.max, negate=True)
 
-        def pack_g(b, h, copy):
-            packed = tile("g%d_%d_packed" % (b, h), [P, HALF * PACK], BF16)
-            copy(
-                packed.rearrange("p (c s t) -> p c t s", s=PACK, t=PACK),
-                held["g_tiles%d" % b][:, :, h * HALF : (h + 1) * HALF].rearrange("p t (c s) -> p c t s", s=PACK),
-            )
-
-        def scores(b, t, neg_max):
-            a = banks[SCORE_BANK[b][t]][:]
-            for part in [slice(0, HALF), slice(HALF, N)] if b == t == 0 else [slice(0, N)]:
-                matmul(a[:, part], "xT%d" % b, E4M3, slice(t * P, (t + 1) * P), "w%d" % b, part)
-            nc.vector.tensor_reduce(neg_max, a, mybir.AxisListType.X, ALU.max, negate=True)
+        def exp(b, t, bank, neg_max):
             nc.scalar.activation(
                 tile("e%d" % b, [P, PACK, N], F32)[:, t, :],
-                a,
+                banks[bank][:],
                 ACT.Exp,
                 bias=neg_max,
                 accum_out=tile("sums%d" % b, [P, PACK], F32)[:, t : t + 1],
@@ -177,156 +137,214 @@ def tile_attend_gkl_w_prj_kernel(tc, xT, wT, y, wt, xm, pm, offs, out):
         def row_factors(b):
             nc.vector.tensor_tensor(tile("factor%d" % b, [P, PACK], F32), held["inverse%d" % b], weights[:, b, :], ALU.mult)
 
-        def gradient(b, t, first, end):
-            nc.vector.scalar_tensor_tensor(
-                tile("g_tiles%d" % b, [P, PACK, N], BF16)[:, t, first:end],
-                held["e%d" % b][:, t, first:end],
-                held["factor%d" % b][:, t : t + 1],
-                weighed[b][t][:, first:end],
-                ALU.mult,
-                ALU.subtract,
+        def weigh_on_gpsimd(b, t, dst):
+            nc.gpsimd.tensor_scalar(dst, held["y%d" % b][:, t, :], weights[:, b, t : t + 1], 0.0, ALU.mult, ALU.add)
+            weighed[b][t] = dst
+
+        def weigh_on_scalar(b, t, dst):
+            nc.scalar.activation(dst, held["y%d" % b][:, t, :], ACT.Copy, scale=weights[:, b, t : t + 1])
+            weighed[b][t] = dst
+
+        def weigh_on_vector(b, t, dst):
+            nc.vector.tensor_scalar(dst, held["y%d" % b][:, t, :], weights[:, b, t : t + 1], None, ALU.mult)
+            weighed[b][t] = dst
+
+        weighed = [[None] * PACK for b in range(B)]
+
+        def gradient(b, first, end):
+            for t in range(PACK):
+                nc.vector.scalar_tensor_tensor(
+                    tile("g_tiles%d" % b, [P, PACK, N], BF16)[:, t, first:end],
+                    held["e%d" % b][:, t, first:end],
+                    held["factor%d" % b][:, t : t + 1],
+                    weighed[b][t][:, first:end],
+                    ALU.mult,
+                    ALU.subtract,
+                )
+
+        def pack_g(b, first, end, copy):
+            dst = packed("g%d" % b)[:, PACK * first : PACK * end]
+            copy(
+                dst.rearrange("p (c s t) -> p c t s", s=PACK, t=PACK),
+                held["g_tiles%d" % b][:, :, first:end].rearrange("p t (c s) -> p c t s", s=PACK),
             )
 
-        def difference(t, first, end):
-            e = held["e1"][:, t, first:end]
-            nc.vector.scalar_tensor_tensor(
-                e, e, held["inverse1"][:, t : t + 1], held["y1"][:, t, first:end], ALU.mult, ALU.subtract
-            )
+        def table_gradient(b, block, bank):
+            for j in range(PACK):
+                matmul(
+                    banks[bank][:, j * BLOCK : (j + 1) * BLOCK],
+                    "xm%d" % b,
+                    slice(j * P, (j + 1) * P),
+                    "g%d" % b,
+                    E5M2,
+                    slice(block * BLOCK, (block + 1) * BLOCK),
+                )
 
-        def weigh_and_pack(h):
-            packed = tile("g1_%d_packed" % h, [P, HALF * PACK], BF16)
-            weight = weights[:, 1, :].rearrange("p (c t s) -> p c t s", c=1, s=1)
+        def pack_dw(b, block, bank, copy):
+            dst = packed("dw%d" % b)[:, PACK * BLOCK * block : PACK * BLOCK * (block + 1)]
+            copy(dst.rearrange("p (i j) -> p i j", j=PACK), banks[bank][:].rearrange("p (j i) -> p i j", j=PACK))
+
+        def project(b, first, count, bank):
+            matmul(banks[bank][:, 0:count], "pm", slice(0, K), "dw%d" % b, E4M3, slice(first, first + count))
+
+        def empty(b, first, count, bank, copy):
+            copy(tile("dense%d_%d" % (b, first), [P, count], F32), banks[bank][:, 0:count])
+
+        def scatter_on_scalar(b, first, count):
+            nc.scalar.activation(window[:].indirect(listed(b, first, count)), held["dense%d_%d" % (b, first)], ACT.Copy)
+
+        def scatter_on_vector(b, first, count):
+            on_vector(window[:].indirect(listed(b, first, count)), held["dense%d_%d" % (b, first)])
+
+        def scatter_short(b, first, count):
             nc.vector.tensor_tensor(
-                packed.rearrange("p (c s t) -> p c t s", s=PACK, t=PACK),
-                held["e1"][:, :, h * HALF : (h + 1) * HALF].rearrange("p t (c s) -> p c t s", s=PACK),
-                weight.to_broadcast([P, HALF // PACK, PACK, PACK]),
-                ALU.mult,
+                window[:].indirect(listed(b, first, count)), held["dense%d_%d" % (b, first)], held["zeros"], ALU.add
             )
 
-        def rounded(b, block):
-            if b == 0:
-                return held["xm1"][:, block, 0 : D // 2].bitcast(BF16)
-            return tile("dw_rounded1", [P, N // P * D], BF16)[:, block * D : (block + 1) * D]
+        load_table()
+        split = R - PACK * XT0_ON_SCALAR
+        xT0_end = packed("w0")[:, 0 : 2 * PACK * (R - split)].bitcast(F32).rearrange("p (j c) -> p j c", j=PACK)
+        nc.sync.dma_start(out=xT0_end, in_=rows(xT[0])[:, :, split:])
+        load_columns("xT0_start", xT[0], 0, split)
+        for h in range(2):
+            load_columns("xT1_%d" % h, xT[1], h * HALF, (h + 1) * HALF)
+            load_targets(0, h, h + 1)
+        nc.scalar.dma_start(out=weights, in_=wt.rearrange("b (p t) o -> p b (t o)", t=PACK))
+        load_targets(0, 2, 4)
+        load_targets(1, 0, 2)
+        load_columns("xm0", xm[0], 0, D)
+        load_targets(1, 2, 4)
+        load_columns("pm", pm, 0, K)
+        load_columns("xm1_0", xm[1], 0, HALF)
+        load_columns("xm1_1", xm[1], HALF, D)
+        nc.gpsimd.memset(window[:], 0.0)
+        nc.gpsimd.memset(tile("zeros", [P, BLOCK], F32), 0.0)
 
-        def turned(b, block):
-            return banks[TURNED_BANK[b][block]][:].rearrange("p (q u i) -> p q u i", q=2, u=2)
+        runs = [(0, 0, HALF), (0, HALF, HALF), (1, 0, N)]
+        picked = [
+            packed("w1")[:, 0 : 4 * HALF].bitcast(U32),
+            tile("picked0_end", [P, 2 * HALF], U32),
+            tile("picked1", [P, 2 * N], U32),
+        ]
 
-        def table_gradient(b, block):
-            h, q = divmod(block, 2)
-            dw = banks[DW_BANK[b][block]][:]
-            matmul(dw, "g%d_%d" % (b, h), E5M2, slice(q * P, (q + 1) * P), "xm%d" % b)
-            on_scalar(rounded(b, block), dw)
-            words = rounded(b, block).bitcast(F32)
-            for u in range(2):
-                nc.tensor.transpose(turned(b, block)[:, q, u, :], words[:, u * P : (u + 1) * P], ident)
+        def gather_runs(u):
+            for (b, first, count), words in zip(runs, picked):
+                on_vector(words[:, u * count : (u + 1) * count], held["pairs%d" % u].indirect(listed(b, first, count)))
 
-        def pack_dw(b, block, count):
-            h, q = divmod(block, 2)
-            packed = tile("dw%d_%d_packed" % (b, h), [P, HALF * PACK], BF16).bitcast(F32)
-            on_scalar(
-                packed.rearrange("p (q i u) -> p q i u", q=2, u=2)[:, q : q + count],
-                turned(b, block).rearrange("p q u i -> p q i u")[:, q : q + count],
-            )
-
-        def project(b, h):
-            matmul(banks[DP_BANK[b][h]][:, 0:HALF], "pm", E4M3, slice(0, K), "dw%d_%d" % (b, h))
-
-        def empty(b, h, copy):
-            copy(tile("dense%d_%d" % (b, h), [P, HALF], F32), banks[DP_BANK[b][h]][:, 0:HALF])
+        def pack_table(run):
+            b, first, count = runs[run]
+            dst = held["w%d_packed" % b].bitcast(U32).rearrange("p (c u) -> p c u", u=2)
+            on_scalar(dst[:, first : first + count], picked[run].rearrange("p (u c) -> p c u", u=2))
 
         for u in range(2):
             for part in range(len(TABLE_LOADS)):
                 if TABLE_LOADS[part][0] == u:
                     round_table(part)
-            gather(u)
+            gather_runs(u)
 
-        pack_xT(0, xT0_end, P - XT0_ON_SCALAR, on_scalar)
-        pack_xT(0, held["xT0_start"], 0, on_vector)
+        deal("xT0", xT0_end, P - XT0_ON_SCALAR, P - XT0_ON_SCALAR, P, on_scalar)
+        deal("xT0", held["xT0_start"], 0, 0, P - XT0_ON_SCALAR, on_vector)
         pack_table(0)
         pack_table(1)
         for h in range(2):
             quantise("w0", E4M3, h * HALF, HALF)
-            quantise("xT0", E4M3, h * R // 2, R // 2)
+            quantise("xT0", E4M3, h * HALF, HALF)
         pack_table(2)
         tile("w1_codes", [P, N], U32, tag="xT0_start")
         quantise("w1", E4M3, 0, N)
         for h in range(2):
-            pack_xT(1, held["xT1_%d" % h], h * P // 2, on_scalar)
+            deal("xT1", held["xT1_%d" % h], h * 64, h * 64, (h + 1) * 64, on_scalar)
+
+        def scores(b, t, neg_max):
+            bank = PACK * b + t
+            if b == t == 0:
+                for h in range(2):
+                    part = slice(h * HALF, (h + 1) * HALF)
+                    matmul(banks[bank][:, part], "xT0", slice(0, P), "w0", E4M3, part)
+            else:
+                score(b, t, bank)
+            row_max(bank, neg_max)
+            exp(b, t, bank, neg_max)
 
         neg_max = [tile("neg_max%d" % b, [P, PACK], F32) for b in range(B)]
         for t in range(PACK - 1):
             scores(0, t, neg_max[0][:, t : t + 1])
-        quantise("xT1", E4M3, 0, R // 2)
-        quantise("xT1", E4M3, R // 2, R // 2)
+        quantise("xT1", E4M3, 0, HALF)
+        quantise("xT1", E4M3, HALF, HALF)
         scores(0, PACK - 1, held["xT1_packed"][:, 0:2].bitcast(F32))
-
-        weighed = [[held["y0"][:, t, :] for t in range(PACK)]]
-        weighed[0][0] = held["w1_packed"][:, 0 : 2 * N].bitcast(F32)
-        weighed[0][2] = held["xT1_packed"][:, 2 * N :].bitcast(F32)
-        for t in range(PACK):
-            nc.gpsimd.tensor_scalar(weighed[0][t], held["y0"][:, t, :], weights[:, 0, t : t + 1], 0.0, ALU.mult, ALU.add)
-        packed = tile("xm0_packed", [P, D * PACK], BF16).rearrange("p (u m e j) -> p u m j e", u=2, e=2, j=PACK)
-        raw = held["xm0"].rearrange("p j (m u e) -> p u m j e", u=2, e=2)
-        nc.gpsimd.tensor_scalar(packed[:, 0, 0:XM0_ON_GPSIMD], raw[:, 0, 0:XM0_ON_GPSIMD], 1.0, 0.0, ALU.mult, ALU.add)
-
+        weigh_on_gpsimd(0, 0, held["w1_packed"][:, 0 : 2 * N].bitcast(F32))
+        weigh_on_gpsimd(0, 1, held["w1_packed"][:, 2 * N :].bitcast(F32))
+        weigh_on_gpsimd(0, 2, held["xT1_packed"][:, 2 * N :].bitcast(F32))
+        weigh_on_gpsimd(0, 3, held["y0"][:, 2, :])
+        for t in range(2):
+            weigh_on_gpsimd(1, t, held["y1"][:, t - 1, :] if t else held["y0"][:, 3, :])
         scores(1, 0, neg_max[1][:, 0:1])
         invert_sums(0)
         for t in range(1, PACK):
             scores(1, t, neg_max[1][:, t : t + 1])
         row_factors(0)
-        for first in (HALF, 0):
-            for t in range(PACK):
-                gradient(0, t, first, first + HALF)
-        pack_pm()
-        quantise("pm", E4M3, 0, K)
+
+        gradient(0, 0, HALF)
         invert_sums(1)
-        pack_g(0, 1, on_scalar)
-        on_scalar(packed[:, 1, 0:XM0_ON_GPSIMD], raw[:, 1, 0:XM0_ON_GPSIMD])
-        pack_xm(0, XM0_ON_GPSIMD, P, on_scalar)
-        pack_g(0, 0, on_vector)
+        deal("xm0", held["xm0"], 0, 0, 64, on_scalar)
+        deal("xm0", held["xm0"], 0, 64, 128, on_vector)
+        pack_g(0, 0, HALF, on_vector)
+        row_factors(1)
         quantise("xm0", E4M3, 0, D)
-        for h in range(2):
-            quantise("g0_%d" % h, E5M2, 0, HALF)
-
-        pack_xm(1, 0, P // 2, on_scalar)
-        pack_xm(1, P // 2, P, on_scalar)
-        for t in range(PACK):
-            difference(t, 0, HALF)
-        for block in range(N // P):
-            table_gradient(0, block)
-        for h in range(2):
-            pack_dw(0, 2 * h, 2)
+        quantise("g0", E5M2, 0, HALF)
+        for t in range(2, PACK):
+            weigh_on_scalar(1, t, held["y1"][:, t, :])
+        pack_pm(on_scalar)
+        table_gradient(0, 0, 0)
+        table_gradient(0, 1, 1)
+        pack_dw(0, 0, 0, on_scalar)
+        pack_dw(0, 1, 1, on_scalar)
+        deal("xm1", held["xm1_0"], 0, 0, 64, on_scalar)
+        gradient(0, HALF, N)
+        quantise("pm", E4M3, 0, K)
+        pack_g(0, HALF, N, on_vector)
+        quantise("dw0", E4M3, 0, HALF)
+        quantise("g0", E5M2, HALF, HALF)
+        project(0, 0, HALF, 4)
+        table_gradient(0, 2, 2)
+        table_gradient(0, 3, 3)
+        empty(0, 0, HALF, 4, on_scalar)
+        pack_dw(0, 2, 2, on_scalar)
+        pack_dw(0, 3, 3, on_scalar)
+        deal("xm1", held["xm1_1"], 64, 64, 128, on_scalar)
+        scatter_on_scalar(0, 0, HALF)
+        gradient(1, 0, HALF)
         quantise("xm1", E4M3, 0, D)
-        weigh_and_pack(0)
-        difference(0, HALF, N)
-        quantise("g1_0", E5M2, 0, HALF)
-        for t in range(1, PACK):
-            difference(t, HALF, N)
-        quantise("dw0_0", E4M3, 0, HALF)
-        held["g1_1_packed"] = held["dw0_0_packed"]
-        weigh_and_pack(1)
-        quantise("dw0_1", E4M3, 0, HALF)
-        project(0, 0)
-        empty(0, 0, on_vector)
-        quantise("g1_1", E5M2, 0, HALF)
-
-        table_gradient(1, 0)
-        table_gradient(1, 1)
-        project(0, 1)
-        pack_dw(1, 0, 2)
-        quantise("dw1_0", E4M3, 0, HALF)
-        empty(0, 1, on_scalar)
-        table_gradient(1, 2)
-        table_gradient(1, 3)
-        for q in range(2):
-            pack_dw(1, 2 + q, 1)
-            quantise("dw1_1", E4M3, q * P, P)
-        held["dense1_0"] = rounded(1, 3).bitcast(F32)
-        for h in range(2):
-            project(1, h)
-            empty(1, h, on_scalar)
-
-        for b in range(B):
-            for h in range(2):
-                on_vector(window[:].indirect(listed(b, h * HALF, HALF)), held["dense%d_%d" % (b, h)])
+        pack_g(1, 0, HALF, on_vector)
+        quantise("dw0", E4M3, HALF, HALF)
+        quantise("g1", E5M2, 0, HALF)
+        project(0, HALF, HALF, 5)
+        empty(0, HALF, HALF, 5, on_scalar)
+        scatter_on_scalar(0, HALF, HALF)
+        table_gradient(1, 0, 6)
+        table_gradient(1, 1, 7)
+        gradient(1, 256, 384)
+        pack_dw(1, 0, 6, on_vector)
+        pack_dw(1, 1, 7, on_vector)
+        pack_g(1, 256, 384, on_vector)
+        quantise("dw1", E4M3, 0, HALF)
+        quantise("g1", E5M2, 256, 128)
+        project(1, 0, HALF, 0)
+        table_gradient(1, 2, 1)
+        gradient(1, 384, 512)
+        empty(1, 0, HALF, 0, on_vector)
+        pack_g(1, 384, 512, on_vector)
+        pack_dw(1, 2, 1, on_scalar)
+        scatter_on_scalar(1, 0, HALF)
+        quantise("g1", E5M2, 384, 128)
+        table_gradient(1, 3, 2)
+        quantise("dw1", E4M3, 256, 128)
+        project(1, 256, 128, 3)
+        pack_dw(1, 3, 2, on_vector)
+        empty(1, 256, 128, 3, on_vector)
+        quantise("dw1", E4M3, 384, 128)
+        project(1, 384, 128, 4)
+        scatter_short(1, 256, 128)
+        empty(1, 384, 128, 4, on_scalar)
+        scatter_short(1, 384, 128)
         nc.sync.dma_start(out=out, in_=window[:])

@@ -47,13 +47,13 @@ def tile_attend_gkl_w_prj_kernel(tc, xT, wT, y, wt, xm, pm, offs, out):
         def packed(name, width=N):
             return tile(name + "_packed", [P, width * PACK], BF16)
 
-        def quantise(name, fmt, first, count):
+        def quantise(name, fmt, first, count, apart=None):
             source = held[name + "_packed"]
             width = source.shape[1] // PACK
             nc.vector.quantize_mx(
                 out=tile(name + "_codes", [P, width], U32)[:, first : first + count].bitcast(fmt),
                 scales=tile(name + "_scales", [P, width], U8)[:, first : first + count],
-                in_=source[:, PACK * first : PACK * (first + count)],
+                in_=source[:, PACK * first : PACK * (first + count)] if apart is None else apart,
             )
 
         def matmul(dst, stationary, cols, moving, fmt, part):
@@ -112,6 +112,11 @@ def tile_attend_gkl_w_prj_kernel(tc, xT, wT, y, wt, xm, pm, offs, out):
             src = raw.rearrange("p j (n l t) -> p n j l t", l=2, t=PACK)
             copy(dst[:, first // 2 : end // 2], src[:, (first - raw_first) // 2 : (end - raw_first) // 2])
 
+        def deal_on_gpsimd(name, raw, raw_first, first, end):
+            dst = packed(name).rearrange("p (t m j) -> p m j t", t=PACK, j=PACK)
+            src = raw.rearrange("p j (m t) -> p m j t", t=PACK)
+            nc.gpsimd.tensor_scalar(dst[:, first:end], src[:, first - raw_first : end - raw_first], 1.0, 0.0, ALU.mult, ALU.add)
+
         def pack_pm(copy):
             dst = packed("pm", K).rearrange("p (c i j) -> p c j i", i=PACK, j=PACK)
             copy(dst, held["pm"].rearrange("p j (c i) -> p c j i", i=PACK))
@@ -151,10 +156,16 @@ def tile_attend_gkl_w_prj_kernel(tc, xT, wT, y, wt, xm, pm, offs, out):
 
         weighed = [[None] * PACK for b in range(B)]
 
-        def gradient(b, first, end):
-            for t in range(PACK):
+        def g_tiles(b, first, end):
+            if b == 1 and first >= HALF:
+                spare = held["xm1_packed"][:, PACK * (first - HALF) : PACK * (end - HALF)]
+                return spare.rearrange("p (t c) -> p t c", t=PACK)
+            return tile("g_tiles%d" % b, [P, PACK, N - b * HALF], BF16)[:, :, first:end]
+
+        def gradient(b, first, end, tiles):
+            for t in tiles:
                 nc.vector.scalar_tensor_tensor(
-                    tile("g_tiles%d" % b, [P, PACK, N], BF16)[:, t, first:end],
+                    g_tiles(b, first, end)[:, t, :],
                     held["e%d" % b][:, t, first:end],
                     held["factor%d" % b][:, t : t + 1],
                     weighed[b][t][:, first:end],
@@ -166,7 +177,7 @@ def tile_attend_gkl_w_prj_kernel(tc, xT, wT, y, wt, xm, pm, offs, out):
             dst = packed("g%d" % b)[:, PACK * first : PACK * end]
             copy(
                 dst.rearrange("p (c s t) -> p c t s", s=PACK, t=PACK),
-                held["g_tiles%d" % b][:, :, first:end].rearrange("p t (c s) -> p c t s", s=PACK),
+                g_tiles(b, first, end).rearrange("p t (c s) -> p c t s", s=PACK),
             )
 
         def table_gradient(b, block, bank):
@@ -182,6 +193,8 @@ def tile_attend_gkl_w_prj_kernel(tc, xT, wT, y, wt, xm, pm, offs, out):
 
         def pack_dw(b, block, bank, copy):
             dst = packed("dw%d" % b)[:, PACK * BLOCK * block : PACK * BLOCK * (block + 1)]
+            if (b, block) == (1, 2):
+                dst = held["xm1_packed"][:, PACK * BLOCK : 2 * PACK * BLOCK]
             copy(dst.rearrange("p (i j) -> p i j", j=PACK), banks[bank][:].rearrange("p (j i) -> p i j", j=PACK))
 
         def project(b, first, count, bank):
@@ -211,9 +224,10 @@ def tile_attend_gkl_w_prj_kernel(tc, xT, wT, y, wt, xm, pm, offs, out):
             load_targets(0, h, h + 1)
         nc.scalar.dma_start(out=weights, in_=wt.rearrange("b (p t) o -> p b (t o)", t=PACK))
         load_targets(0, 2, 4)
-        load_targets(1, 0, 2)
-        load_columns("xm0", xm[0], 0, D)
-        load_targets(1, 2, 4)
+        load_targets(1, 0, 1)
+        load_columns("xm0_0", xm[0], 0, HALF)
+        load_columns("xm0_1", xm[0], HALF, D)
+        load_targets(1, 1, 4)
         load_columns("pm", pm, 0, K)
         load_columns("xm1_0", xm[1], 0, HALF)
         load_columns("xm1_1", xm[1], HALF, D)
@@ -276,69 +290,74 @@ def tile_attend_gkl_w_prj_kernel(tc, xT, wT, y, wt, xm, pm, offs, out):
         weigh_on_gpsimd(0, 1, held["w1_packed"][:, 2 * N :].bitcast(F32))
         weigh_on_gpsimd(0, 2, held["xT1_packed"][:, 2 * N :].bitcast(F32))
         weigh_on_gpsimd(0, 3, held["y0"][:, 2, :])
-        for t in range(2):
-            weigh_on_gpsimd(1, t, held["y1"][:, t - 1, :] if t else held["y0"][:, 3, :])
+        weigh_on_gpsimd(1, 0, held["y0"][:, 3, :])
         scores(1, 0, neg_max[1][:, 0:1])
-        invert_sums(0)
-        for t in range(1, PACK):
+        held["inverse0"] = packed("xm0")[:, HALF : HALF + 2 * PACK].bitcast(F32)
+        for t in range(1, PACK - 1):
             scores(1, t, neg_max[1][:, t : t + 1])
+        invert_sums(0)
+        scores(1, PACK - 1, held["xm0_packed"][:, 0:2].bitcast(F32))
         row_factors(0)
-
-        gradient(0, 0, HALF)
+        deal("xm0", held["xm0_1"], 64, 64, 128, on_vector)
+        gradient(0, 0, 512, range(PACK))
+        deal("xm0", held["xm0_0"], 0, 0, 64, on_scalar)
+        weigh_on_scalar(1, 2, held["y1"][:, 2, :])
+        weigh_on_scalar(1, 3, held["y1"][:, 3, :])
         invert_sums(1)
-        deal("xm0", held["xm0"], 0, 0, 64, on_scalar)
-        deal("xm0", held["xm0"], 0, 64, 128, on_vector)
-        pack_g(0, 0, HALF, on_vector)
-        row_factors(1)
+        weigh_on_vector(1, 1, held["w1_packed"][:, 0 : 2 * N].bitcast(F32))
+        pack_g(0, 0, 256, on_vector)
         quantise("xm0", E4M3, 0, D)
-        quantise("g0", E5M2, 0, HALF)
-        for t in range(2, PACK):
-            weigh_on_scalar(1, t, held["y1"][:, t, :])
+        quantise("g0", E5M2, 0, 256)
+        row_factors(1)
+        pack_g(0, 256, 512, on_vector)
         pack_pm(on_scalar)
+        deal("xm1", held["xm1_0"], 0, 0, 64, on_scalar)
+        deal("xm1", held["xm1_1"], 64, 64, 128, on_scalar)
+        held["dw0_packed"] = held["xm1_1"].rearrange("p j c -> p (j c)").bitcast(BF16)
+        held["g1_packed"] = held["dw0_packed"]
         table_gradient(0, 0, 0)
         table_gradient(0, 1, 1)
-        pack_dw(0, 0, 0, on_scalar)
-        pack_dw(0, 1, 1, on_scalar)
-        deal("xm1", held["xm1_0"], 0, 0, 64, on_scalar)
-        gradient(0, HALF, N)
-        quantise("pm", E4M3, 0, K)
-        pack_g(0, HALF, N, on_vector)
-        quantise("dw0", E4M3, 0, HALF)
-        quantise("g0", E5M2, HALF, HALF)
-        project(0, 0, HALF, 4)
+        gradient(1, 0, 256, [0])
+        quantise("g0", E5M2, 256, 256)
         table_gradient(0, 2, 2)
         table_gradient(0, 3, 3)
-        empty(0, 0, HALF, 4, on_scalar)
+        pack_dw(0, 0, 0, on_scalar)
+        pack_dw(0, 1, 1, on_scalar)
         pack_dw(0, 2, 2, on_scalar)
         pack_dw(0, 3, 3, on_scalar)
-        deal("xm1", held["xm1_1"], 64, 64, 128, on_scalar)
-        scatter_on_scalar(0, 0, HALF)
-        gradient(1, 0, HALF)
+        gradient(1, 0, 256, [1, 2, 3])
+        quantise("pm", E4M3, 0, K)
         quantise("xm1", E4M3, 0, D)
-        pack_g(1, 0, HALF, on_vector)
-        quantise("dw0", E4M3, HALF, HALF)
-        quantise("g1", E5M2, 0, HALF)
-        project(0, HALF, HALF, 5)
-        empty(0, HALF, HALF, 5, on_scalar)
-        scatter_on_scalar(0, HALF, HALF)
+        quantise("dw0", E4M3, 0, 256)
+        project(0, 0, 256, 4)
+        empty(0, 0, 256, 4, on_scalar)
+        scatter_on_scalar(0, 0, 256)
+        pack_g(1, 0, 256, on_vector)
+        gradient(1, 256, 384, [0, 1])
+        quantise("g1", E5M2, 0, 256)
+        quantise("dw0", E4M3, 256, 256)
         table_gradient(1, 0, 6)
+        project(0, 256, 256, 5)
         table_gradient(1, 1, 7)
-        gradient(1, 256, 384)
-        pack_dw(1, 0, 6, on_vector)
-        pack_dw(1, 1, 7, on_vector)
+        gradient(1, 256, 384, [2, 3])
+        gradient(1, 384, 512, [0, 1])
+        empty(0, 256, 256, 5, on_scalar)
+        scatter_on_scalar(0, 256, 256)
         pack_g(1, 256, 384, on_vector)
-        quantise("dw1", E4M3, 0, HALF)
+        pack_dw(1, 0, 6, on_vector)
         quantise("g1", E5M2, 256, 128)
-        project(1, 0, HALF, 0)
         table_gradient(1, 2, 1)
-        gradient(1, 384, 512)
-        empty(1, 0, HALF, 0, on_vector)
+        pack_dw(1, 1, 7, on_vector)
+        gradient(1, 384, 512, [2, 3])
+        quantise("dw1", E4M3, 0, 256)
+        project(1, 0, 256, 0)
         pack_g(1, 384, 512, on_vector)
         pack_dw(1, 2, 1, on_scalar)
-        scatter_on_scalar(1, 0, HALF)
         quantise("g1", E5M2, 384, 128)
+        empty(1, 0, 256, 0, on_vector)
+        scatter_on_scalar(1, 0, 256)
         table_gradient(1, 3, 2)
-        quantise("dw1", E4M3, 256, 128)
+        quantise("dw1", E4M3, 256, 128, held["xm1_packed"][:, PACK * BLOCK : 2 * PACK * BLOCK])
         project(1, 256, 128, 3)
         pack_dw(1, 3, 2, on_vector)
         empty(1, 256, 128, 3, on_vector)

@@ -22,7 +22,7 @@ BLOCK = 128
 PER_COLUMN = 16
 
 TABLE_LOADS = [(0, 0, 1280, 5), (0, 1280, 2048, 5), (1, 0, 1280, 4), (1, 1280, 1792, 5), (1, 1792, 2048, 5)]
-XT0_ON_SCALAR = 48
+XT0_ON_SCALAR = 64
 
 
 def tile_attend_gkl_w_prj_kernel(tc, xT, wT, y, wt, xm, pm, offs, out):
@@ -112,6 +112,11 @@ def tile_attend_gkl_w_prj_kernel(tc, xT, wT, y, wt, xm, pm, offs, out):
             src = raw.rearrange("p j (n l t) -> p n j l t", l=2, t=PACK)
             copy(dst[:, first // 2 : end // 2], src[:, (first - raw_first) // 2 : (end - raw_first) // 2])
 
+        def deal_tiles(name, raw, first, end, tiles, copy):
+            dst = packed(name).rearrange("p (t n l j) -> p n j l t", t=PACK, l=2, j=PACK)
+            src = raw.rearrange("p j (n l t) -> p n j l t", l=2, t=PACK)
+            copy(dst[:, first // 2 : end // 2, :, :, tiles], src[:, first // 2 : end // 2, :, :, tiles])
+
         def deal_on_gpsimd(name, raw, raw_first, first, end):
             dst = packed(name).rearrange("p (t m j) -> p m j t", t=PACK, j=PACK)
             src = raw.rearrange("p j (m t) -> p m j t", t=PACK)
@@ -158,7 +163,7 @@ def tile_attend_gkl_w_prj_kernel(tc, xT, wT, y, wt, xm, pm, offs, out):
 
         def g_tiles(b, first, end):
             if b == 1 and first >= HALF:
-                spare = held["xm1_packed"][:, PACK * (first - HALF) : PACK * (end - HALF)]
+                spare = tile("g_tiles_end", [P, PACK * HALF], BF16, tag="dw0_0_codes")[:, PACK * (first - HALF) : PACK * (end - HALF)]
                 return spare.rearrange("p (t c) -> p t c", t=PACK)
             return tile("g_tiles%d" % b, [P, PACK, N - b * HALF], BF16)[:, :, first:end]
 
@@ -194,11 +199,14 @@ def tile_attend_gkl_w_prj_kernel(tc, xT, wT, y, wt, xm, pm, offs, out):
         def pack_dw(b, block, bank, copy):
             dst = packed("dw%d" % b)[:, PACK * BLOCK * block : PACK * BLOCK * (block + 1)]
             if (b, block) == (1, 2):
-                dst = held["xm1_packed"][:, PACK * BLOCK : 2 * PACK * BLOCK]
+                dst = held["g_tiles_end"][:, PACK * BLOCK :]
             copy(dst.rearrange("p (i j) -> p i j", j=PACK), banks[bank][:].rearrange("p (j i) -> p i j", j=PACK))
 
         def project(b, first, count, bank):
-            matmul(banks[bank][:, 0:count], "pm", slice(0, K), "dw%d" % b, E4M3, slice(first, first + count))
+            if b == 0:
+                matmul(banks[bank][:, 0:count], "pm", slice(0, K), "dw0_%d" % (first // HALF), E4M3, slice(0, count))
+            else:
+                matmul(banks[bank][:, 0:count], "pm", slice(0, K), "dw%d" % b, E4M3, slice(first, first + count))
 
         def empty(b, first, count, bank, copy):
             copy(tile("dense%d_%d" % (b, first), [P, count], F32), banks[bank][:, 0:count])
@@ -215,59 +223,40 @@ def tile_attend_gkl_w_prj_kernel(tc, xT, wT, y, wt, xm, pm, offs, out):
             )
 
         load_table()
-        split = R - PACK * XT0_ON_SCALAR
-        xT0_end = packed("w0")[:, 0 : 2 * PACK * (R - split)].bitcast(F32).rearrange("p (j c) -> p j c", j=PACK)
-        nc.sync.dma_start(out=xT0_end, in_=rows(xT[0])[:, :, split:])
-        load_columns("xT0_start", xT[0], 0, split)
-        for h in range(2):
-            load_columns("xT1_%d" % h, xT[1], h * HALF, (h + 1) * HALF)
-            load_targets(0, h, h + 1)
         nc.scalar.dma_start(out=weights, in_=wt.rearrange("b (p t) o -> p b (t o)", t=PACK))
+        load_columns("xT0", xT[0], 0, R)
+        load_columns("xT1", xT[1], 0, R)
+        load_targets(0, 0, 2)
         load_targets(0, 2, 4)
         load_targets(1, 0, 1)
-        load_columns("xm0_0", xm[0], 0, HALF)
-        load_columns("xm0_1", xm[0], HALF, D)
+        load_columns("xm0", xm[0], 0, D)
         load_targets(1, 1, 4)
         load_columns("pm", pm, 0, K)
-        load_columns("xm1_0", xm[1], 0, HALF)
-        load_columns("xm1_1", xm[1], HALF, D)
+        load_columns("xm1", xm[1], 0, D)
         nc.gpsimd.memset(window[:], 0.0)
         nc.gpsimd.memset(tile("zeros", [P, BLOCK], F32), 0.0)
-
-        runs = [(0, 0, HALF), (0, HALF, HALF), (1, 0, N)]
-        picked = [
-            packed("w1")[:, 0 : 4 * HALF].bitcast(U32),
-            tile("picked0_end", [P, 2 * HALF], U32),
-            tile("picked1", [P, 2 * N], U32),
-        ]
-
-        def gather_runs(u):
-            for (b, first, count), words in zip(runs, picked):
-                on_vector(words[:, u * count : (u + 1) * count], held["pairs%d" % u].indirect(listed(b, first, count)))
-
-        def pack_table(run):
-            b, first, count = runs[run]
-            dst = held["w%d_packed" % b].bitcast(U32).rearrange("p (c u) -> p c u", u=2)
-            on_scalar(dst[:, first : first + count], picked[run].rearrange("p (u c) -> p c u", u=2))
 
         for u in range(2):
             for part in range(len(TABLE_LOADS)):
                 if TABLE_LOADS[part][0] == u:
                     round_table(part)
-            gather_runs(u)
-
-        deal("xT0", xT0_end, P - XT0_ON_SCALAR, P - XT0_ON_SCALAR, P, on_scalar)
-        deal("xT0", held["xT0_start"], 0, 0, P - XT0_ON_SCALAR, on_vector)
-        pack_table(0)
-        pack_table(1)
-        for h in range(2):
-            quantise("w0", E4M3, h * HALF, HALF)
-            quantise("xT0", E4M3, h * HALF, HALF)
-        pack_table(2)
-        tile("w1_codes", [P, N], U32, tag="xT0_start")
-        quantise("w1", E4M3, 0, N)
-        for h in range(2):
-            deal("xT1", held["xT1_%d" % h], h * 64, h * 64, (h + 1) * 64, on_scalar)
+            for b in range(B):
+                for h in range(2):
+                    gather(u, b, h)
+        for b in range(B):
+            for h in range(2):
+                weave(b, h, on_scalar)
+        deal_tiles("xT0", held["xT0"], 0, P, slice(0, 2), on_vector)
+        deal_tiles("xT0", held["xT0"], 0, P - XT0_ON_SCALAR, slice(2, 4), on_vector)
+        deal_tiles("xT0", held["xT0"], P - XT0_ON_SCALAR, P, slice(2, 4), on_scalar)
+        quantise("w0", E4M3, 0, HALF)
+        quantise("xT0", E4M3, 0, HALF)
+        quantise("w0", E4M3, HALF, HALF)
+        tile("w1_codes", [P, N], U32, tag="xT0")
+        quantise("w1", E4M3, 0, HALF)
+        quantise("xT0", E4M3, HALF, HALF)
+        quantise("w1", E4M3, HALF, HALF)
+        deal("xT1", held["xT1"], 0, 0, P, on_scalar)
 
         def scores(b, t, neg_max):
             bank = PACK * b + t
@@ -280,40 +269,43 @@ def tile_attend_gkl_w_prj_kernel(tc, xT, wT, y, wt, xm, pm, offs, out):
             row_max(bank, neg_max)
             exp(b, t, bank, neg_max)
 
+        held["e0"] = held["xT1"]
         neg_max = [tile("neg_max%d" % b, [P, PACK], F32) for b in range(B)]
         for t in range(PACK - 1):
             scores(0, t, neg_max[0][:, t : t + 1])
         quantise("xT1", E4M3, 0, HALF)
         quantise("xT1", E4M3, HALF, HALF)
         scores(0, PACK - 1, held["xT1_packed"][:, 0:2].bitcast(F32))
-        weigh_on_gpsimd(0, 0, held["w1_packed"][:, 0 : 2 * N].bitcast(F32))
-        weigh_on_gpsimd(0, 1, held["w1_packed"][:, 2 * N :].bitcast(F32))
+        weigh_on_gpsimd(0, 0, held["w1_packed"][:, 2 * N :].bitcast(F32))
+        weigh_on_gpsimd(0, 1, held["y0"][:, 0, :])
         weigh_on_gpsimd(0, 2, held["xT1_packed"][:, 2 * N :].bitcast(F32))
         weigh_on_gpsimd(0, 3, held["y0"][:, 2, :])
         weigh_on_gpsimd(1, 0, held["y0"][:, 3, :])
-        scores(1, 0, neg_max[1][:, 0:1])
         held["inverse0"] = packed("xm0")[:, HALF : HALF + 2 * PACK].bitcast(F32)
-        for t in range(1, PACK - 1):
-            scores(1, t, neg_max[1][:, t : t + 1])
+        late = tile("weighed1", [P, 2, N], F32)
+        scores(1, 0, neg_max[1][:, 0:1])
+        scores(1, 1, late[:, 1, 0:1])
+        scores(1, 2, late[:, 0, 0:1])
         invert_sums(0)
         scores(1, PACK - 1, held["xm0_packed"][:, 0:2].bitcast(F32))
         row_factors(0)
-        deal("xm0", held["xm0_1"], 64, 64, 128, on_vector)
+        deal("xm0", held["xm0"], 0, 64, P, on_vector)
         gradient(0, 0, 512, range(PACK))
-        deal("xm0", held["xm0_0"], 0, 0, 64, on_scalar)
-        weigh_on_scalar(1, 2, held["y1"][:, 2, :])
-        weigh_on_scalar(1, 3, held["y1"][:, 3, :])
+        deal("xm0", held["xm0"], 0, 0, 64, on_scalar)
+        weigh_on_scalar(1, 2, late[:, 0, :])
+        weigh_on_scalar(1, 3, late[:, 1, :])
         invert_sums(1)
-        weigh_on_vector(1, 1, held["w1_packed"][:, 0 : 2 * N].bitcast(F32))
+        weigh_on_vector(1, 1, weighed[0][0])
         pack_g(0, 0, 256, on_vector)
         quantise("xm0", E4M3, 0, D)
         quantise("g0", E5M2, 0, 256)
         row_factors(1)
         pack_g(0, 256, 512, on_vector)
         pack_pm(on_scalar)
-        deal("xm1", held["xm1_0"], 0, 0, 64, on_scalar)
-        deal("xm1", held["xm1_1"], 64, 64, 128, on_scalar)
-        held["dw0_packed"] = held["xm1_1"].rearrange("p j c -> p (j c)").bitcast(BF16)
+        deal("xm1", held["xm1"], 0, 0, P, on_scalar)
+        held["dw0_packed"] = held["xm1"][:, 0:2, :].rearrange("p j c -> p (j c)").bitcast(BF16)
+        for h in range(2):
+            held["dw0_%d_packed" % h] = held["dw0_packed"][:, h * PACK * HALF : (h + 1) * PACK * HALF]
         held["g1_packed"] = held["dw0_packed"]
         table_gradient(0, 0, 0)
         table_gradient(0, 1, 1)
@@ -328,18 +320,17 @@ def tile_attend_gkl_w_prj_kernel(tc, xT, wT, y, wt, xm, pm, offs, out):
         gradient(1, 0, 256, [1, 2, 3])
         quantise("pm", E4M3, 0, K)
         quantise("xm1", E4M3, 0, D)
-        quantise("dw0", E4M3, 0, 256)
+        quantise("dw0_0", E4M3, 0, HALF)
         project(0, 0, 256, 4)
         empty(0, 0, 256, 4, on_scalar)
         scatter_on_scalar(0, 0, 256)
         pack_g(1, 0, 256, on_vector)
-        gradient(1, 256, 384, [0, 1])
+        quantise("dw0_1", E4M3, 0, HALF)
         quantise("g1", E5M2, 0, 256)
-        quantise("dw0", E4M3, 256, 256)
-        table_gradient(1, 0, 6)
         project(0, 256, 256, 5)
+        table_gradient(1, 0, 6)
         table_gradient(1, 1, 7)
-        gradient(1, 256, 384, [2, 3])
+        gradient(1, 256, 384, range(PACK))
         gradient(1, 384, 512, [0, 1])
         empty(0, 256, 256, 5, on_scalar)
         scatter_on_scalar(0, 256, 256)
@@ -357,7 +348,7 @@ def tile_attend_gkl_w_prj_kernel(tc, xT, wT, y, wt, xm, pm, offs, out):
         empty(1, 0, 256, 0, on_vector)
         scatter_on_scalar(1, 0, 256)
         table_gradient(1, 3, 2)
-        quantise("dw1", E4M3, 256, 128, held["xm1_packed"][:, PACK * BLOCK : 2 * PACK * BLOCK])
+        quantise("dw1", E4M3, 256, 128, held["g_tiles_end"][:, PACK * BLOCK :])
         project(1, 256, 128, 3)
         pack_dw(1, 3, 2, on_vector)
         empty(1, 256, 128, 3, on_vector)

@@ -22,7 +22,7 @@ BLOCK = 128
 PER_COLUMN = 16
 
 TABLE_LOADS = [(0, 0, 1280, 5), (0, 1280, 2048, 5), (1, 0, 1280, 4), (1, 1280, 1792, 5), (1, 1792, 2048, 5)]
-XT0_ON_SCALAR = 64
+XT0_ON_SCALAR = 48
 
 
 def tile_attend_gkl_w_prj_kernel(tc, xT, wT, y, wt, xm, pm, offs, out):
@@ -108,14 +108,14 @@ def tile_attend_gkl_w_prj_kernel(tc, xT, wT, y, wt, xm, pm, offs, out):
             copy(dst[:, h * HALF : (h + 1) * HALF], held["picked%d_%d" % (b, h)].rearrange("p (u c) -> p c u", u=2))
 
         def deal(name, raw, raw_first, first, end, copy):
-            dst = packed(name).rearrange("p (t n l j) -> p n j l t", t=PACK, l=2, j=PACK)
-            src = raw.rearrange("p j (n l t) -> p n j l t", l=2, t=PACK)
-            copy(dst[:, first // 2 : end // 2], src[:, (first - raw_first) // 2 : (end - raw_first) // 2])
+            dst = packed(name).rearrange("p (t m a e) -> p m a t e", t=PACK, a=2, e=2)
+            src = raw.rearrange("p (a e) (m t) -> p m a t e", e=2, t=PACK)
+            copy(dst[:, first:end], src[:, first - raw_first : end - raw_first])
 
         def deal_tiles(name, raw, first, end, tiles, copy):
-            dst = packed(name).rearrange("p (t n l j) -> p n j l t", t=PACK, l=2, j=PACK)
-            src = raw.rearrange("p j (n l t) -> p n j l t", l=2, t=PACK)
-            copy(dst[:, first // 2 : end // 2, :, :, tiles], src[:, first // 2 : end // 2, :, :, tiles])
+            dst = packed(name).rearrange("p (t m a e) -> p m a t e", t=PACK, a=2, e=2)
+            src = raw.rearrange("p (a e) (m t) -> p m a t e", e=2, t=PACK)
+            copy(dst[:, first:end, :, tiles], src[:, first:end, :, tiles])
 
         def deal_on_gpsimd(name, raw, raw_first, first, end):
             dst = packed(name).rearrange("p (t m j) -> p m j t", t=PACK, j=PACK)
@@ -200,7 +200,10 @@ def tile_attend_gkl_w_prj_kernel(tc, xT, wT, y, wt, xm, pm, offs, out):
             dst = packed("dw%d" % b)[:, PACK * BLOCK * block : PACK * BLOCK * (block + 1)]
             if (b, block) == (1, 2):
                 dst = held["g_tiles_end"][:, PACK * BLOCK :]
-            copy(dst.rearrange("p (i j) -> p i j", j=PACK), banks[bank][:].rearrange("p (j i) -> p i j", j=PACK))
+            copy(
+                dst.rearrange("p (c s j) -> p c j s", s=2, j=PACK),
+                banks[bank][:].rearrange("p (j c s) -> p c j s", j=PACK, s=2),
+            )
 
         def project(b, first, count, bank):
             if b == 0:
@@ -223,40 +226,59 @@ def tile_attend_gkl_w_prj_kernel(tc, xT, wT, y, wt, xm, pm, offs, out):
             )
 
         load_table()
+        split = R - PACK * XT0_ON_SCALAR
+        xT0_end = packed("w0")[:, 0 : 2 * PACK * (R - split)].bitcast(F32).rearrange("p (j c) -> p j c", j=PACK)
+        nc.sync.dma_start(out=xT0_end, in_=rows(xT[0])[:, :, split:])
+        load_columns("xT0_start", xT[0], 0, split)
+        for h in range(2):
+            load_columns("xT1_%d" % h, xT[1], h * HALF, (h + 1) * HALF)
+            load_targets(0, h, h + 1)
         nc.scalar.dma_start(out=weights, in_=wt.rearrange("b (p t) o -> p b (t o)", t=PACK))
-        load_columns("xT0", xT[0], 0, R)
-        load_columns("xT1", xT[1], 0, R)
-        load_targets(0, 0, 2)
         load_targets(0, 2, 4)
         load_targets(1, 0, 1)
-        load_columns("xm0", xm[0], 0, D)
+        load_columns("xm0_0", xm[0], 0, HALF)
+        load_columns("xm0_1", xm[0], HALF, D)
         load_targets(1, 1, 4)
         load_columns("pm", pm, 0, K)
-        load_columns("xm1", xm[1], 0, D)
+        load_columns("xm1_0", xm[1], 0, HALF)
+        load_columns("xm1_1", xm[1], HALF, D)
         nc.gpsimd.memset(window[:], 0.0)
         nc.gpsimd.memset(tile("zeros", [P, BLOCK], F32), 0.0)
+
+        runs = [(0, 0, HALF), (0, HALF, HALF), (1, 0, N)]
+        picked = [
+            packed("w1")[:, 0 : 4 * HALF].bitcast(U32),
+            tile("picked0_end", [P, 2 * HALF], U32),
+            tile("picked1", [P, 2 * N], U32),
+        ]
+
+        def gather_runs(u):
+            for (b, first, count), words in zip(runs, picked):
+                on_vector(words[:, u * count : (u + 1) * count], held["pairs%d" % u].indirect(listed(b, first, count)))
+
+        def pack_table(run):
+            b, first, count = runs[run]
+            dst = held["w%d_packed" % b].bitcast(U32).rearrange("p (c u) -> p c u", u=2)
+            on_scalar(dst[:, first : first + count], picked[run].rearrange("p (u c) -> p c u", u=2))
 
         for u in range(2):
             for part in range(len(TABLE_LOADS)):
                 if TABLE_LOADS[part][0] == u:
                     round_table(part)
-            for b in range(B):
-                for h in range(2):
-                    gather(u, b, h)
-        for b in range(B):
-            for h in range(2):
-                weave(b, h, on_scalar)
-        deal_tiles("xT0", held["xT0"], 0, P, slice(0, 2), on_vector)
-        deal_tiles("xT0", held["xT0"], 0, P - XT0_ON_SCALAR, slice(2, 4), on_vector)
-        deal_tiles("xT0", held["xT0"], P - XT0_ON_SCALAR, P, slice(2, 4), on_scalar)
-        quantise("w0", E4M3, 0, HALF)
-        quantise("xT0", E4M3, 0, HALF)
-        quantise("w0", E4M3, HALF, HALF)
-        tile("w1_codes", [P, N], U32, tag="xT0")
-        quantise("w1", E4M3, 0, HALF)
-        quantise("xT0", E4M3, HALF, HALF)
-        quantise("w1", E4M3, HALF, HALF)
-        deal("xT1", held["xT1"], 0, 0, P, on_scalar)
+            gather_runs(u)
+
+        deal("xT0", xT0_end, P - XT0_ON_SCALAR, P - XT0_ON_SCALAR, P, on_scalar)
+        deal("xT0", held["xT0_start"], 0, 0, P - XT0_ON_SCALAR, on_vector)
+        pack_table(0)
+        pack_table(1)
+        for h in range(2):
+            quantise("w0", E4M3, h * HALF, HALF)
+            quantise("xT0", E4M3, h * HALF, HALF)
+        pack_table(2)
+        tile("w1_codes", [P, N], U32, tag="xT0_start")
+        quantise("w1", E4M3, 0, N)
+        for h in range(2):
+            deal("xT1", held["xT1_%d" % h], h * 64, h * 64, (h + 1) * 64, on_scalar)
 
         def scores(b, t, neg_max):
             bank = PACK * b + t
@@ -269,29 +291,28 @@ def tile_attend_gkl_w_prj_kernel(tc, xT, wT, y, wt, xm, pm, offs, out):
             row_max(bank, neg_max)
             exp(b, t, bank, neg_max)
 
-        held["e0"] = held["xT1"]
         neg_max = [tile("neg_max%d" % b, [P, PACK], F32) for b in range(B)]
         for t in range(PACK - 1):
             scores(0, t, neg_max[0][:, t : t + 1])
         quantise("xT1", E4M3, 0, HALF)
         quantise("xT1", E4M3, HALF, HALF)
         scores(0, PACK - 1, held["xT1_packed"][:, 0:2].bitcast(F32))
-        weigh_on_gpsimd(0, 0, held["w1_packed"][:, 2 * N :].bitcast(F32))
-        weigh_on_gpsimd(0, 1, held["y0"][:, 0, :])
+        weigh_on_gpsimd(0, 0, held["w1_packed"][:, 0 : 2 * N].bitcast(F32))
+        weigh_on_gpsimd(0, 1, held["w1_packed"][:, 2 * N :].bitcast(F32))
         weigh_on_gpsimd(0, 2, held["xT1_packed"][:, 2 * N :].bitcast(F32))
         weigh_on_gpsimd(0, 3, held["y0"][:, 2, :])
         weigh_on_gpsimd(1, 0, held["y0"][:, 3, :])
-        held["inverse0"] = packed("xm0")[:, HALF : HALF + 2 * PACK].bitcast(F32)
         late = tile("weighed1", [P, 2, N], F32)
         scores(1, 0, neg_max[1][:, 0:1])
+        held["inverse0"] = packed("xm0")[:, HALF : HALF + 2 * PACK].bitcast(F32)
         scores(1, 1, late[:, 1, 0:1])
         scores(1, 2, late[:, 0, 0:1])
         invert_sums(0)
         scores(1, PACK - 1, held["xm0_packed"][:, 0:2].bitcast(F32))
         row_factors(0)
-        deal("xm0", held["xm0"], 0, 64, P, on_vector)
+        deal("xm0", held["xm0_1"], 64, 64, 128, on_vector)
         gradient(0, 0, 512, range(PACK))
-        deal("xm0", held["xm0"], 0, 0, 64, on_scalar)
+        deal("xm0", held["xm0_0"], 0, 0, 64, on_scalar)
         weigh_on_scalar(1, 2, late[:, 0, :])
         weigh_on_scalar(1, 3, late[:, 1, :])
         invert_sums(1)
@@ -302,8 +323,9 @@ def tile_attend_gkl_w_prj_kernel(tc, xT, wT, y, wt, xm, pm, offs, out):
         row_factors(1)
         pack_g(0, 256, 512, on_vector)
         pack_pm(on_scalar)
-        deal("xm1", held["xm1"], 0, 0, P, on_scalar)
-        held["dw0_packed"] = held["xm1"][:, 0:2, :].rearrange("p j c -> p (j c)").bitcast(BF16)
+        deal("xm1", held["xm1_0"], 0, 0, 64, on_scalar)
+        deal("xm1", held["xm1_1"], 64, 64, 128, on_scalar)
+        held["dw0_packed"] = held["xm1_1"].rearrange("p j c -> p (j c)").bitcast(BF16)
         for h in range(2):
             held["dw0_%d_packed" % h] = held["dw0_packed"][:, h * PACK * HALF : (h + 1) * PACK * HALF]
         held["g1_packed"] = held["dw0_packed"]

@@ -22,7 +22,7 @@ BLOCK = 128
 PER_COLUMN = 16
 
 TABLE_LOADS = [(0, 0, 1280, 5), (0, 1280, 2048, 5), (1, 0, 1280, 4), (1, 1280, 1792, 5), (1, 1792, 2048, 5)]
-XT0_ON_SCALAR = 48
+XT0_ON_SCALAR = 64
 
 
 def tile_attend_gkl_w_prj_kernel(tc, xT, wT, y, wt, xm, pm, offs, out):
@@ -122,6 +122,9 @@ def tile_attend_gkl_w_prj_kernel(tc, xT, wT, y, wt, xm, pm, offs, out):
             src = raw.rearrange("p j (m t) -> p m j t", t=PACK)
             nc.gpsimd.tensor_scalar(dst[:, first:end], src[:, first - raw_first : end - raw_first], 1.0, 0.0, ALU.mult, ALU.add)
 
+        def on_scalar_activation(dst, src):
+            nc.scalar.activation(dst, src, ACT.Copy)
+
         def pack_pm(copy):
             dst = packed("pm", K).rearrange("p (c i j) -> p c j i", i=PACK, j=PACK)
             copy(dst, held["pm"].rearrange("p j (c i) -> p c j i", i=PACK))
@@ -162,10 +165,35 @@ def tile_attend_gkl_w_prj_kernel(tc, xT, wT, y, wt, xm, pm, offs, out):
         weighed = [[None] * PACK for b in range(B)]
 
         def g_tiles(b, first, end):
-            if b == 1 and first >= HALF:
-                spare = tile("g_tiles_end", [P, PACK * HALF], BF16, tag="dw0_0_codes")[:, PACK * (first - HALF) : PACK * (end - HALF)]
-                return spare.rearrange("p (t c) -> p t c", t=PACK)
             return tile("g_tiles%d" % b, [P, PACK, N - b * HALF], BF16)[:, :, first:end]
+
+        def differences(block):
+            both = tile("differences", [P, 2, PACK, BLOCK], F32, tag="dw0_0_codes")
+            return both[:, block - 2]
+
+        def difference(block, tiles):
+            for t in tiles:
+                nc.vector.scalar_tensor_tensor(
+                    differences(block)[:, t, :],
+                    held["e1"][:, t, block * BLOCK : (block + 1) * BLOCK],
+                    held["inverse1"][:, t : t + 1],
+                    held["y1_end"][:, t, (block - 2) * BLOCK : (block - 1) * BLOCK],
+                    ALU.mult,
+                    ALU.subtract,
+                )
+
+        def weigh_and_pack(block):
+            dst = packed("g1")[:, PACK * BLOCK * block : PACK * BLOCK * (block + 1)]
+            weight = weights[:, 1, :].rearrange("p (c t s) -> p c t s", c=1, s=1)
+            nc.vector.tensor_tensor(
+                dst.rearrange("p (c s t) -> p c t s", s=PACK, t=PACK),
+                differences(block).rearrange("p t (c s) -> p c t s", s=PACK),
+                weight.to_broadcast([P, BLOCK // PACK, PACK, PACK]),
+                ALU.mult,
+            )
+
+        def spent_differences():
+            return differences(3)[:, 0:2, :].rearrange("p t c -> p (t c)").bitcast(BF16)
 
         def gradient(b, first, end, tiles):
             for t in tiles:
@@ -199,7 +227,7 @@ def tile_attend_gkl_w_prj_kernel(tc, xT, wT, y, wt, xm, pm, offs, out):
         def pack_dw(b, block, bank, copy):
             dst = packed("dw%d" % b)[:, PACK * BLOCK * block : PACK * BLOCK * (block + 1)]
             if (b, block) == (1, 2):
-                dst = held["g_tiles_end"][:, PACK * BLOCK :]
+                dst = spent_differences()
             copy(
                 dst.rearrange("p (c s j) -> p c j s", s=2, j=PACK),
                 banks[bank][:].rearrange("p (j c s) -> p c j s", j=PACK, s=2),
@@ -225,98 +253,98 @@ def tile_attend_gkl_w_prj_kernel(tc, xT, wT, y, wt, xm, pm, offs, out):
                 window[:].indirect(listed(b, first, count)), held["dense%d_%d" % (b, first)], held["zeros"], ALU.add
             )
 
-        load_table()
-        split = R - PACK * XT0_ON_SCALAR
-        xT0_end = packed("w0")[:, 0 : 2 * PACK * (R - split)].bitcast(F32).rearrange("p (j c) -> p j c", j=PACK)
-        nc.sync.dma_start(out=xT0_end, in_=rows(xT[0])[:, :, split:])
-        load_columns("xT0_start", xT[0], 0, split)
-        for h in range(2):
-            load_columns("xT1_%d" % h, xT[1], h * HALF, (h + 1) * HALF)
-            load_targets(0, h, h + 1)
+        planes = [sb.tile([P, T], F32, name="plane%d" % j) for j in range(PACK)]
+        for j in range(PACK):
+            nc.sync.dma_start(out=planes[j][:], in_=rows(wT)[:, j, :])
+            if j == 0:
+                nc.sync.dma_start(offsets[:], offs)
         nc.scalar.dma_start(out=weights, in_=wt.rearrange("b (p t) o -> p b (t o)", t=PACK))
+        load_columns("xT0", xT[0], 0, R)
+        load_columns("xT1_0", xT[1], 0, HALF)
+        load_columns("xT1_1", xT[1], HALF, R)
+        load_targets(0, 0, 2)
         load_targets(0, 2, 4)
-        load_targets(1, 0, 1)
         load_columns("xm0_0", xm[0], 0, HALF)
         load_columns("xm0_1", xm[0], HALF, D)
-        load_targets(1, 1, 4)
+        load_columns("y1", y[1], 0, HALF)
         load_columns("pm", pm, 0, K)
         load_columns("xm1_0", xm[1], 0, HALF)
         load_columns("xm1_1", xm[1], HALF, D)
+        load_columns("y1_end", y[1], HALF, N)
         nc.gpsimd.memset(window[:], 0.0)
         nc.gpsimd.memset(tile("zeros", [P, BLOCK], F32), 0.0)
 
-        runs = [(0, 0, HALF), (0, HALF, HALF), (1, 0, N)]
-        picked = [
-            packed("w1")[:, 0 : 4 * HALF].bitcast(U32),
-            tile("picked0_end", [P, 2 * HALF], U32),
-            tile("picked1", [P, 2 * N], U32),
-        ]
+        def pick(j, b, first, count):
+            dst = tile("picked%d" % b, [P, PACK, N], BF16)[:, j, first : first + count]
+            src = planes[j][:].indirect(listed(b, first, count))
+            if b == 0:
+                on_vector(dst, src)
+            else:
+                nc.scalar.activation(dst, src, ACT.Copy)
 
-        def gather_runs(u):
-            for (b, first, count), words in zip(runs, picked):
-                on_vector(words[:, u * count : (u + 1) * count], held["pairs%d" % u].indirect(listed(b, first, count)))
+        def pair_up(b, u, first, count, copy):
+            dst = packed("w%d" % b).rearrange("p (c u e) -> p c u e", u=2, e=2)[:, first : first + count, u, :]
+            copy(dst, held["picked%d" % b][:, 2 * u : 2 * u + 2, first : first + count].rearrange("p e c -> p c e"))
 
-        def pack_table(run):
-            b, first, count = runs[run]
-            dst = held["w%d_packed" % b].bitcast(U32).rearrange("p (c u) -> p c u", u=2)
-            on_scalar(dst[:, first : first + count], picked[run].rearrange("p (u c) -> p c u", u=2))
-
-        for u in range(2):
-            for part in range(len(TABLE_LOADS)):
-                if TABLE_LOADS[part][0] == u:
-                    round_table(part)
-            gather_runs(u)
-
-        deal("xT0", xT0_end, P - XT0_ON_SCALAR, P - XT0_ON_SCALAR, P, on_scalar)
-        deal("xT0", held["xT0_start"], 0, 0, P - XT0_ON_SCALAR, on_vector)
-        pack_table(0)
-        pack_table(1)
-        for h in range(2):
-            quantise("w0", E4M3, h * HALF, HALF)
-            quantise("xT0", E4M3, h * HALF, HALF)
-        pack_table(2)
-        tile("w1_codes", [P, N], U32, tag="xT0_start")
-        quantise("w1", E4M3, 0, N)
+        for j in range(2):
+            for b in range(B):
+                pick(j, b, 0, N)
+        pair_up(0, 0, 0, N, on_vector)
+        pair_up(1, 0, 0, BLOCK, on_scalar_activation)
+        pair_up(1, 0, BLOCK, N - BLOCK, on_vector)
+        for b in range(B):
+            pick(2, b, 0, N)
+        for b in range(B):
+            for h in range(2):
+                pick(3, b, h * HALF, HALF)
+            for h in range(2):
+                pair_up(b, 1, h * HALF, HALF, on_scalar if b else on_vector)
+        quantise("w0", E4M3, 0, HALF)
+        quantise("w0", E4M3, HALF, HALF)
+        deal_tiles("xT0", held["xT0"], 0, P, slice(0, 2), on_vector)
+        deal_tiles("xT0", held["xT0"], 0, P - XT0_ON_SCALAR, slice(2, 4), on_vector)
+        deal_tiles("xT0", held["xT0"], P - XT0_ON_SCALAR, P, slice(2, 4), on_scalar)
+        quantise("xT0", E4M3, 0, HALF)
+        tile("w1_codes", [P, N], U32, tag="xT0")
+        quantise("w1", E4M3, 0, HALF)
+        quantise("xT0", E4M3, HALF, HALF)
+        quantise("w1", E4M3, HALF, HALF)
         for h in range(2):
             deal("xT1", held["xT1_%d" % h], h * 64, h * 64, (h + 1) * 64, on_scalar)
 
         def scores(b, t, neg_max):
             bank = PACK * b + t
-            if b == t == 0:
-                for h in range(2):
-                    part = slice(h * HALF, (h + 1) * HALF)
-                    matmul(banks[bank][:, part], "xT0", slice(0, P), "w0", E4M3, part)
-            else:
-                score(b, t, bank)
+            score(b, t, bank)
             row_max(bank, neg_max)
             exp(b, t, bank, neg_max)
 
+        held["sums0"] = held["xT1_1"][:, 0, 0:PACK]
         neg_max = [tile("neg_max%d" % b, [P, PACK], F32) for b in range(B)]
-        for t in range(PACK - 1):
+        for t in range(2):
             scores(0, t, neg_max[0][:, t : t + 1])
+        scores(0, 2, packed("xm0")[:, 0:2].bitcast(F32))
         quantise("xT1", E4M3, 0, HALF)
         quantise("xT1", E4M3, HALF, HALF)
         scores(0, PACK - 1, held["xT1_packed"][:, 0:2].bitcast(F32))
-        weigh_on_gpsimd(0, 0, held["w1_packed"][:, 0 : 2 * N].bitcast(F32))
-        weigh_on_gpsimd(0, 1, held["w1_packed"][:, 2 * N :].bitcast(F32))
-        weigh_on_gpsimd(0, 2, held["xT1_packed"][:, 2 * N :].bitcast(F32))
-        weigh_on_gpsimd(0, 3, held["y0"][:, 2, :])
-        weigh_on_gpsimd(1, 0, held["y0"][:, 3, :])
-        late = tile("weighed1", [P, 2, N], F32)
-        scores(1, 0, neg_max[1][:, 0:1])
+        weigh_on_gpsimd(0, 0, held["xT1_packed"][:, 2 * N :].bitcast(F32))
+        weigh_on_gpsimd(0, 1, held["y0"][:, 0, :])
+        weigh_on_gpsimd(0, 2, held["y0"][:, 1, :])
+
         held["inverse0"] = packed("xm0")[:, HALF : HALF + 2 * PACK].bitcast(F32)
-        scores(1, 1, late[:, 1, 0:1])
-        scores(1, 2, late[:, 0, 0:1])
+        late = tile("weighed1", [P, PACK, HALF], F32)
+        scores(1, 0, late[:, 3, 0:1])
+        scores(1, 1, late[:, 2, 0:1])
+        scores(1, 2, late[:, 1, 0:1])
         invert_sums(0)
-        scores(1, PACK - 1, held["xm0_packed"][:, 0:2].bitcast(F32))
+        scores(1, PACK - 1, late[:, 0, 0:1])
         row_factors(0)
+        weigh_on_vector(0, 3, held["y0"][:, 2, :])
         deal("xm0", held["xm0_1"], 64, 64, 128, on_vector)
         gradient(0, 0, 512, range(PACK))
         deal("xm0", held["xm0_0"], 0, 0, 64, on_scalar)
-        weigh_on_scalar(1, 2, late[:, 0, :])
-        weigh_on_scalar(1, 3, late[:, 1, :])
+        for t in range(PACK):
+            weigh_on_scalar(1, t, late[:, t, :])
         invert_sums(1)
-        weigh_on_vector(1, 1, weighed[0][0])
         pack_g(0, 0, 256, on_vector)
         quantise("xm0", E4M3, 0, D)
         quantise("g0", E5M2, 0, 256)
@@ -352,25 +380,25 @@ def tile_attend_gkl_w_prj_kernel(tc, xT, wT, y, wt, xm, pm, offs, out):
         project(0, 256, 256, 5)
         table_gradient(1, 0, 6)
         table_gradient(1, 1, 7)
-        gradient(1, 256, 384, range(PACK))
-        gradient(1, 384, 512, [0, 1])
+        difference(2, range(PACK))
+        difference(3, range(2))
         empty(0, 256, 256, 5, on_scalar)
         scatter_on_scalar(0, 256, 256)
-        pack_g(1, 256, 384, on_vector)
+        weigh_and_pack(2)
         pack_dw(1, 0, 6, on_vector)
         quantise("g1", E5M2, 256, 128)
         table_gradient(1, 2, 1)
         pack_dw(1, 1, 7, on_vector)
-        gradient(1, 384, 512, [2, 3])
+        difference(3, range(2, PACK))
         quantise("dw1", E4M3, 0, 256)
         project(1, 0, 256, 0)
-        pack_g(1, 384, 512, on_vector)
+        weigh_and_pack(3)
         pack_dw(1, 2, 1, on_scalar)
         quantise("g1", E5M2, 384, 128)
         empty(1, 0, 256, 0, on_vector)
         scatter_on_scalar(1, 0, 256)
         table_gradient(1, 3, 2)
-        quantise("dw1", E4M3, 256, 128, held["g_tiles_end"][:, PACK * BLOCK :])
+        quantise("dw1", E4M3, 256, 128, spent_differences())
         project(1, 256, 128, 3)
         pack_dw(1, 3, 2, on_vector)
         empty(1, 256, 128, 3, on_vector)

@@ -165,35 +165,10 @@ def tile_attend_gkl_w_prj_kernel(tc, xT, wT, y, wt, xm, pm, offs, out):
         weighed = [[None] * PACK for b in range(B)]
 
         def g_tiles(b, first, end):
+            if b == 1 and first >= HALF:
+                spare = tile("g_tiles_end", [P, PACK * HALF], BF16, tag="dw0_0_codes")[:, PACK * (first - HALF) : PACK * (end - HALF)]
+                return spare.rearrange("p (t c) -> p t c", t=PACK)
             return tile("g_tiles%d" % b, [P, PACK, N - b * HALF], BF16)[:, :, first:end]
-
-        def differences(block):
-            both = tile("differences", [P, 2, PACK, BLOCK], F32, tag="dw0_0_codes")
-            return both[:, block - 2]
-
-        def difference(block, tiles):
-            for t in tiles:
-                nc.vector.scalar_tensor_tensor(
-                    differences(block)[:, t, :],
-                    held["e1"][:, t, block * BLOCK : (block + 1) * BLOCK],
-                    held["inverse1"][:, t : t + 1],
-                    held["y1_end"][:, t, (block - 2) * BLOCK : (block - 1) * BLOCK],
-                    ALU.mult,
-                    ALU.subtract,
-                )
-
-        def weigh_and_pack(block):
-            dst = packed("g1")[:, PACK * BLOCK * block : PACK * BLOCK * (block + 1)]
-            weight = weights[:, 1, :].rearrange("p (c t s) -> p c t s", c=1, s=1)
-            nc.vector.tensor_tensor(
-                dst.rearrange("p (c s t) -> p c t s", s=PACK, t=PACK),
-                differences(block).rearrange("p t (c s) -> p c t s", s=PACK),
-                weight.to_broadcast([P, BLOCK // PACK, PACK, PACK]),
-                ALU.mult,
-            )
-
-        def spent_differences():
-            return differences(3)[:, 0:2, :].rearrange("p t c -> p (t c)").bitcast(BF16)
 
         def gradient(b, first, end, tiles):
             for t in tiles:
@@ -227,7 +202,7 @@ def tile_attend_gkl_w_prj_kernel(tc, xT, wT, y, wt, xm, pm, offs, out):
         def pack_dw(b, block, bank, copy):
             dst = packed("dw%d" % b)[:, PACK * BLOCK * block : PACK * BLOCK * (block + 1)]
             if (b, block) == (1, 2):
-                dst = spent_differences()
+                dst = held["g_tiles_end"][:, PACK * BLOCK :]
             copy(
                 dst.rearrange("p (c s j) -> p c j s", s=2, j=PACK),
                 banks[bank][:].rearrange("p (j c s) -> p c j s", j=PACK, s=2),
@@ -261,16 +236,17 @@ def tile_attend_gkl_w_prj_kernel(tc, xT, wT, y, wt, xm, pm, offs, out):
         nc.scalar.dma_start(out=weights, in_=wt.rearrange("b (p t) o -> p b (t o)", t=PACK))
         load_columns("xT0", xT[0], 0, R)
         load_columns("xT1_0", xT[1], 0, HALF)
+        load_targets(0, 0, 1)
         load_columns("xT1_1", xT[1], HALF, R)
-        load_targets(0, 0, 2)
+        load_targets(0, 1, 2)
         load_targets(0, 2, 4)
+        load_targets(1, 0, 1)
         load_columns("xm0_0", xm[0], 0, HALF)
         load_columns("xm0_1", xm[0], HALF, D)
-        load_columns("y1", y[1], 0, HALF)
+        load_targets(1, 1, 4)
         load_columns("pm", pm, 0, K)
         load_columns("xm1_0", xm[1], 0, HALF)
         load_columns("xm1_1", xm[1], HALF, D)
-        load_columns("y1_end", y[1], HALF, N)
         nc.gpsimd.memset(window[:], 0.0)
         nc.gpsimd.memset(tile("zeros", [P, BLOCK], F32), 0.0)
 
@@ -302,7 +278,8 @@ def tile_attend_gkl_w_prj_kernel(tc, xT, wT, y, wt, xm, pm, offs, out):
         quantise("w0", E4M3, 0, HALF)
         quantise("w0", E4M3, HALF, HALF)
         deal_tiles("xT0", held["xT0"], 0, P, slice(0, 2), on_vector)
-        deal_tiles("xT0", held["xT0"], 0, P - XT0_ON_SCALAR, slice(2, 4), on_vector)
+        if XT0_ON_SCALAR < P:
+            deal_tiles("xT0", held["xT0"], 0, P - XT0_ON_SCALAR, slice(2, 4), on_vector)
         deal_tiles("xT0", held["xT0"], P - XT0_ON_SCALAR, P, slice(2, 4), on_scalar)
         quantise("xT0", E4M3, 0, HALF)
         tile("w1_codes", [P, N], U32, tag="xT0")
@@ -320,31 +297,31 @@ def tile_attend_gkl_w_prj_kernel(tc, xT, wT, y, wt, xm, pm, offs, out):
 
         held["sums0"] = held["xT1_1"][:, 0, 0:PACK]
         neg_max = [tile("neg_max%d" % b, [P, PACK], F32) for b in range(B)]
-        for t in range(2):
+        for t in range(PACK - 1):
             scores(0, t, neg_max[0][:, t : t + 1])
-        scores(0, 2, packed("xm0")[:, 0:2].bitcast(F32))
         quantise("xT1", E4M3, 0, HALF)
         quantise("xT1", E4M3, HALF, HALF)
         scores(0, PACK - 1, held["xT1_packed"][:, 0:2].bitcast(F32))
-        weigh_on_gpsimd(0, 0, held["xT1_packed"][:, 2 * N :].bitcast(F32))
+        weigh_on_gpsimd(0, 0, held["w1_packed"][:, 2 * N :].bitcast(F32))
         weigh_on_gpsimd(0, 1, held["y0"][:, 0, :])
-        weigh_on_gpsimd(0, 2, held["y0"][:, 1, :])
-
+        weigh_on_gpsimd(0, 2, held["xT1_packed"][:, 2 * N :].bitcast(F32))
+        weigh_on_gpsimd(0, 3, held["y0"][:, 2, :])
+        weigh_on_gpsimd(1, 0, held["y0"][:, 3, :])
         held["inverse0"] = packed("xm0")[:, HALF : HALF + 2 * PACK].bitcast(F32)
-        late = tile("weighed1", [P, PACK, HALF], F32)
-        scores(1, 0, late[:, 3, 0:1])
-        scores(1, 1, late[:, 2, 0:1])
-        scores(1, 2, late[:, 1, 0:1])
+        late = tile("weighed1", [P, 2, N], F32)
+        scores(1, 0, neg_max[1][:, 0:1])
+        scores(1, 1, late[:, 1, 0:1])
+        scores(1, 2, late[:, 0, 0:1])
         invert_sums(0)
-        scores(1, PACK - 1, late[:, 0, 0:1])
+        scores(1, PACK - 1, held["xm0_packed"][:, 0:2].bitcast(F32))
         row_factors(0)
-        weigh_on_vector(0, 3, held["y0"][:, 2, :])
         deal("xm0", held["xm0_1"], 64, 64, 128, on_vector)
         gradient(0, 0, 512, range(PACK))
         deal("xm0", held["xm0_0"], 0, 0, 64, on_scalar)
-        for t in range(PACK):
-            weigh_on_scalar(1, t, late[:, t, :])
+        weigh_on_scalar(1, 2, late[:, 0, :])
+        weigh_on_scalar(1, 3, late[:, 1, :])
         invert_sums(1)
+        weigh_on_vector(1, 1, weighed[0][0])
         pack_g(0, 0, 256, on_vector)
         quantise("xm0", E4M3, 0, D)
         quantise("g0", E5M2, 0, 256)
@@ -380,25 +357,25 @@ def tile_attend_gkl_w_prj_kernel(tc, xT, wT, y, wt, xm, pm, offs, out):
         project(0, 256, 256, 5)
         table_gradient(1, 0, 6)
         table_gradient(1, 1, 7)
-        difference(2, range(PACK))
-        difference(3, range(2))
+        gradient(1, 256, 384, range(PACK))
+        gradient(1, 384, 512, [0, 1])
         empty(0, 256, 256, 5, on_scalar)
         scatter_on_scalar(0, 256, 256)
-        weigh_and_pack(2)
+        pack_g(1, 256, 384, on_vector)
         pack_dw(1, 0, 6, on_vector)
         quantise("g1", E5M2, 256, 128)
         table_gradient(1, 2, 1)
         pack_dw(1, 1, 7, on_vector)
-        difference(3, range(2, PACK))
+        gradient(1, 384, 512, [2, 3])
         quantise("dw1", E4M3, 0, 256)
         project(1, 0, 256, 0)
-        weigh_and_pack(3)
+        pack_g(1, 384, 512, on_vector)
         pack_dw(1, 2, 1, on_scalar)
         quantise("g1", E5M2, 384, 128)
         empty(1, 0, 256, 0, on_vector)
         scatter_on_scalar(1, 0, 256)
         table_gradient(1, 3, 2)
-        quantise("dw1", E4M3, 256, 128, spent_differences())
+        quantise("dw1", E4M3, 256, 128, held["g_tiles_end"][:, PACK * BLOCK :])
         project(1, 256, 128, 3)
         pack_dw(1, 3, 2, on_vector)
         empty(1, 256, 128, 3, on_vector)

@@ -327,7 +327,6 @@ def tile_attend_gkl_w_prj_kernel(tc, xT, wT, y, wt, xm, pm, offs, out):
         quantise("g0", E5M2, 0, 256)
         row_factors(1)
         pack_g(0, 256, 512, on_vector)
-        pack_pm(on_scalar)
         deal("xm1", held["xm1_0"], 0, 0, 64, on_scalar)
         deal("xm1", held["xm1_1"], 64, 64, 128, on_scalar)
         held["dw0_packed"] = held["xm1_1"].rearrange("p j c -> p (j c)").bitcast(BF16)
@@ -336,8 +335,9 @@ def tile_attend_gkl_w_prj_kernel(tc, xT, wT, y, wt, xm, pm, offs, out):
         held["g1_packed"] = held["dw0_packed"]
         table_gradient(0, 0, 0)
         table_gradient(0, 1, 1)
-        gradient(1, 0, 256, [0])
+        pack_pm(on_vector)
         quantise("g0", E5M2, 256, 256)
+        gradient(1, 0, 256, [0])
         table_gradient(0, 2, 2)
         table_gradient(0, 3, 3)
         pack_dw(0, 0, 0, on_scalar)

@@ -201,8 +201,6 @@ def tile_attend_gkl_w_prj_kernel(tc, xT, wT, y, wt, xm, pm, offs, out):
 
         def pack_dw(b, block, bank, copy):
             dst = packed("dw%d" % b)[:, PACK * BLOCK * block : PACK * BLOCK * (block + 1)]
-            if (b, block) == (1, 2):
-                dst = held["g_tiles_end"][:, PACK * BLOCK :]
             copy(
                 dst.rearrange("p (c s j) -> p c j s", s=2, j=PACK),
                 banks[bank][:].rearrange("p (j c s) -> p c j s", j=PACK, s=2),
@@ -243,8 +241,8 @@ def tile_attend_gkl_w_prj_kernel(tc, xT, wT, y, wt, xm, pm, offs, out):
         load_targets(1, 0, 1)
         load_columns("xm0_0", xm[0], 0, HALF)
         load_columns("xm0_1", xm[0], HALF, D)
-        load_targets(1, 1, 4)
         load_columns("pm", pm, 0, K)
+        load_targets(1, 1, 4)
         load_columns("xm1_0", xm[1], 0, HALF)
         load_columns("xm1_1", xm[1], HALF, D)
         nc.gpsimd.memset(window[:], 0.0)
@@ -318,64 +316,66 @@ def tile_attend_gkl_w_prj_kernel(tc, xT, wT, y, wt, xm, pm, offs, out):
         deal("xm0", held["xm0_1"], 64, 64, 128, on_vector)
         gradient(0, 0, 512, range(PACK))
         deal("xm0", held["xm0_0"], 0, 0, 64, on_scalar)
+        weigh_on_scalar(1, 1, held["xm0_0"][:, 0:2, :].rearrange("p j c -> p (j c)"))
         weigh_on_scalar(1, 2, late[:, 0, :])
         weigh_on_scalar(1, 3, late[:, 1, :])
         invert_sums(1)
-        weigh_on_vector(1, 1, weighed[0][0])
+        pack_pm(on_vector)
         pack_g(0, 0, 256, on_vector)
         quantise("xm0", E4M3, 0, D)
         quantise("g0", E5M2, 0, 256)
         row_factors(1)
-        pack_g(0, 256, 512, on_vector)
-        deal("xm1", held["xm1_0"], 0, 0, 64, on_scalar)
-        deal("xm1", held["xm1_1"], 64, 64, 128, on_scalar)
-        held["dw0_packed"] = held["xm1_1"].rearrange("p j c -> p (j c)").bitcast(BF16)
+        pack_g(0, 256, 512, on_scalar)
+        deal("xm1", held["xm1_0"], 0, 0, 64, on_vector)
+        held["dw0_packed"] = held["g_tiles0"].rearrange("p t c -> p (t c)")
         for h in range(2):
             held["dw0_%d_packed" % h] = held["dw0_packed"][:, h * PACK * HALF : (h + 1) * PACK * HALF]
         held["g1_packed"] = held["dw0_packed"]
         table_gradient(0, 0, 0)
         table_gradient(0, 1, 1)
-        pack_pm(on_vector)
-        quantise("g0", E5M2, 256, 256)
         gradient(1, 0, 256, [0])
+        quantise("g0", E5M2, 256, 256)
         table_gradient(0, 2, 2)
         table_gradient(0, 3, 3)
         pack_dw(0, 0, 0, on_scalar)
         pack_dw(0, 1, 1, on_scalar)
         pack_dw(0, 2, 2, on_scalar)
         pack_dw(0, 3, 3, on_scalar)
-        gradient(1, 0, 256, [1, 2, 3])
+        gradient(1, 0, 256, [1])
         quantise("pm", E4M3, 0, K)
-        quantise("xm1", E4M3, 0, D)
+        deal("xm1", held["xm1_1"], 64, 64, 128, on_vector)
         quantise("dw0_0", E4M3, 0, HALF)
         project(0, 0, 256, 4)
         empty(0, 0, 256, 4, on_scalar)
         scatter_on_scalar(0, 0, 256)
+        gradient(1, 0, 256, [2, 3])
+        quantise("xm1", E4M3, 0, D)
         pack_g(1, 0, 256, on_vector)
-        quantise("dw0_1", E4M3, 0, HALF)
+        gradient(1, 256, 384, [0])
         quantise("g1", E5M2, 0, 256)
-        project(0, 256, 256, 5)
+        quantise("dw0_1", E4M3, 0, HALF)
         table_gradient(1, 0, 6)
         table_gradient(1, 1, 7)
-        gradient(1, 256, 384, range(PACK))
-        gradient(1, 384, 512, [0, 1])
-        empty(0, 256, 256, 5, on_scalar)
+        project(0, 256, 256, 5)
+        pack_dw(1, 0, 6, on_scalar)
+        pack_dw(1, 1, 7, on_scalar)
+        gradient(1, 256, 384, [1, 2, 3])
+        gradient(1, 384, 512, [0, 1, 2])
+        empty(0, 256, 256, 5, on_vector)
         scatter_on_scalar(0, 256, 256)
         pack_g(1, 256, 384, on_vector)
-        pack_dw(1, 0, 6, on_vector)
-        quantise("g1", E5M2, 256, 128)
-        table_gradient(1, 2, 1)
-        pack_dw(1, 1, 7, on_vector)
-        gradient(1, 384, 512, [2, 3])
+        gradient(1, 384, 512, [3])
         quantise("dw1", E4M3, 0, 256)
         project(1, 0, 256, 0)
+        quantise("g1", E5M2, 256, 128)
+        table_gradient(1, 2, 1)
         pack_g(1, 384, 512, on_vector)
-        pack_dw(1, 2, 1, on_scalar)
-        quantise("g1", E5M2, 384, 128)
         empty(1, 0, 256, 0, on_vector)
         scatter_on_scalar(1, 0, 256)
+        quantise("g1", E5M2, 384, 128)
         table_gradient(1, 3, 2)
-        quantise("dw1", E4M3, 256, 128, held["g_tiles_end"][:, PACK * BLOCK :])
+        pack_dw(1, 2, 1, on_vector)
+        quantise("dw1", E4M3, 256, 128)
         project(1, 256, 128, 3)
         pack_dw(1, 3, 2, on_vector)
         empty(1, 256, 128, 3, on_vector)

from contextlib import ExitStack

import concourse.mybir as mybir

B, N, T, D, R, K = 2, 512, 2048, 512, 512, 128
FLOPS = 2 * B * (R * D * N + R * D * N + D * K * N)

F32 = mybir.dt.float32
BF16 = mybir.dt.bfloat16
U32 = mybir.dt.uint32
U16 = mybir.dt.uint16
U8 = mybir.dt.uint8
E4M3 = mybir.dt.float8_e4m3fn_x4
E5M2 = mybir.dt.float8_e5m2_x4
ALU = mybir.AluOpType
ACT = mybir.ActivationFunctionType

P = 128
PACK = 4
HALF = N // 2
BLOCK = 128
PER_COLUMN = 16

TABLE_LOADS = [(0, 0, 1280, 5), (0, 1280, 2048, 5), (1, 0, 1280, 4), (1, 1280, 1792, 5), (1, 1792, 2048, 5)]
XT0_ON_SCALAR = 64


def tile_attend_gkl_w_prj_kernel(tc, xT, wT, y, wt, xm, pm, offs, out):
    nc = tc.nc
    with ExitStack() as ctx:
        sb = ctx.enter_context(tc.tile_pool(name="sb", bufs=1))
        ps = ctx.enter_context(tc.psum_pool(name="ps", bufs=1))
        banks = [ps.tile([P, N], F32, name="bank%d" % i) for i in range(8)]
        held = {}

        def tile(name, shape, dtype, tag=None):
            if name not in held:
                held[name] = sb.tile(shape, dtype, name=name, tag=tag or name, align_bytes=64)[:]
            return held[name]

        def on_vector(dst, src):
            nc.vector.tensor_copy(out=dst, in_=src)

        def on_scalar(dst, src):
            nc.scalar.copy(out=dst, in_=src)

        def packed(name, width=N):
            return tile(name + "_packed", [P, width * PACK], BF16)

        def quantise(name, fmt, first, count, apart=None):
            source = held[name + "_packed"]
            width = source.shape[1] // PACK
            nc.vector.quantize_mx(
                out=tile(name + "_codes", [P, width], U32)[:, first : first + count].bitcast(fmt),
                scales=tile(name + "_scales", [P, width], U8)[:, first : first + count],
                in_=source[:, PACK * first : PACK * (first + count)] if apart is None else apart,
            )

        def matmul(dst, stationary, cols, moving, fmt, part):
            nc.tensor.matmul_mx(
                out=dst,
                lhsT=held[stationary + "_codes"][:, cols].bitcast(E4M3),
                lhsT_scale=held[stationary + "_scales"][:, cols],
                rhs=held[moving + "_codes"][:, part].bitcast(fmt),
                rhs_scale=held[moving + "_scales"][:, part],
                start=True,
                stop=True,
            )

        def rows(src):
            return src.rearrange("(p j) c -> p j c", j=PACK)

        def load_columns(name, src, first, end):
            nc.sync.dma_start(out=tile(name, [P, PACK, end - first], F32), in_=rows(src)[:, :, first:end])

        def load_targets(b, first, end):
            nc.sync.dma_start(out=tile("y%d" % b, [P, PACK, N], F32)[:, first:end], in_=rows(y[b])[:, first:end])

        offsets = sb.tile([P, B * N // PER_COLUMN], U16, name="offsets")
        window = sb.tile([P, T], F32, name="window")
        weights = tile("wt", [P, B, PACK], F32)

        def listed(b, first, count):
            col = (b * N + first) // PER_COLUMN
            return offsets[:, col : col + count // PER_COLUMN]

        def load_table():
            table_rows = wT.rearrange("(p u e) c -> p u e c", u=2, e=2)
            for part, (u, first, end, eighths) in enumerate(TABLE_LOADS):
                nc.sync.dma_start(out=tile("table%d" % part, [P, 2, end - first], F32), in_=table_rows[:, u, :, first:end])
                if part == 0:
                    nc.sync.dma_start(offsets[:], offs)

        def round_table(part):
            u, first, end, eighths = TABLE_LOADS[part]
            share = (end - first) * eighths // 8
            pairs = tile("pairs%d" % u, [P, T], U32).bitcast(BF16).rearrange("p (c e) -> p c e", e=2)[:, first:end]
            raw = held["table%d" % part].rearrange("p e c -> p c e")
            on_vector(pairs[:, 0:share], raw[:, 0:share])
            nc.scalar.activation(pairs[:, share:], raw[:, share:], ACT.Copy)

        def gather(u, b, h):
            words = tile("picked%d_%d" % (b, h), [P, 2 * HALF], U32)
            on_vector(words[:, u * HALF : (u + 1) * HALF], held["pairs%d" % u].indirect(listed(b, h * HALF, HALF)))

        def weave(b, h, copy):
            dst = packed("w%d" % b).bitcast(U32).rearrange("p (c u) -> p c u", u=2)
            copy(dst[:, h * HALF : (h + 1) * HALF], held["picked%d_%d" % (b, h)].rearrange("p (u c) -> p c u", u=2))

        def deal(name, raw, raw_first, first, end, copy):
            dst = packed(name).rearrange("p (t m a e) -> p m a t e", t=PACK, a=2, e=2)
            src = raw.rearrange("p (a e) (m t) -> p m a t e", e=2, t=PACK)
            copy(dst[:, first:end], src[:, first - raw_first : end - raw_first])

        def deal_tiles(name, raw, first, end, tiles, copy):
            dst = packed(name).rearrange("p (t m a e) -> p m a t e", t=PACK, a=2, e=2)
            src = raw.rearrange("p (a e) (m t) -> p m a t e", e=2, t=PACK)
            copy(dst[:, first:end, :, tiles], src[:, first:end, :, tiles])

        def deal_on_gpsimd(name, raw, raw_first, first, end):
            dst = packed(name).rearrange("p (t m j) -> p m j t", t=PACK, j=PACK)
            src = raw.rearrange("p j (m t) -> p m j t", t=PACK)
            nc.gpsimd.tensor_scalar(dst[:, first:end], src[:, first - raw_first : end - raw_first], 1.0, 0.0, ALU.mult, ALU.add)

        def on_scalar_activation(dst, src):
            nc.scalar.activation(dst, src, ACT.Copy)

        def pack_pm(copy):
            dst = packed("pm", K).rearrange("p (c i j) -> p c j i", i=PACK, j=PACK)
            copy(dst, held["pm"].rearrange("p j (c i) -> p c j i", i=PACK))

        def score(b, t, bank):
            matmul(banks[bank][:], "xT%d" % b, slice(t * P, (t + 1) * P), "w%d" % b, E4M3, slice(0, N))

        def row_max(bank, neg_max):
            nc.vector.tensor_reduce(neg_max, banks[bank][:], mybir.AxisListType.X, ALU.max, negate=True)

        def exp(b, t, bank, neg_max):
            nc.scalar.activation(
                tile("e%d" % b, [P, PACK, N], F32)[:, t, :],
                banks[bank][:],
                ACT.Exp,
                bias=neg_max,
                accum_out=tile("sums%d" % b, [P, PACK], F32)[:, t : t + 1],
            )

        def invert_sums(b):
            nc.vector.reciprocal(tile("inverse%d" % b, [P, PACK], F32), held["sums%d" % b])

        def row_factors(b):
            nc.vector.tensor_tensor(tile("factor%d" % b, [P, PACK], F32), held["inverse%d" % b], weights[:, b, :], ALU.mult)

        def weigh_on_gpsimd(b, t, dst):
            nc.gpsimd.tensor_scalar(dst, held["y%d" % b][:, t, :], weights[:, b, t : t + 1], 0.0, ALU.mult, ALU.add)
            weighed[b][t] = dst

        def weigh_on_scalar(b, t, dst):
            nc.scalar.activation(dst, held["y%d" % b][:, t, :], ACT.Copy, scale=weights[:, b, t : t + 1])
            weighed[b][t] = dst

        def weigh_on_vector(b, t, dst):
            nc.vector.tensor_scalar(dst, held["y%d" % b][:, t, :], weights[:, b, t : t + 1], None, ALU.mult)
            weighed[b][t] = dst

        weighed = [[None] * PACK for b in range(B)]

        def g_tiles(b, first, end):
            if b == 1 and first >= HALF:
                spare = tile("g_tiles_end", [P, PACK * HALF], BF16, tag="dw0_0_codes")[:, PACK * (first - HALF) : PACK * (end - HALF)]
                return spare.rearrange("p (t c) -> p t c", t=PACK)
            return tile("g_tiles%d" % b, [P, PACK, N - b * HALF], BF16)[:, :, first:end]

        def gradient(b, first, end, tiles):
            for t in tiles:
                nc.vector.scalar_tensor_tensor(
                    g_tiles(b, first, end)[:, t, :],
                    held["e%d" % b][:, t, first:end],
                    held["factor%d" % b][:, t : t + 1],
                    weighed[b][t][:, first:end],
                    ALU.mult,
                    ALU.subtract,
                )

        def pack_g(b, first, end, copy):
            dst = packed("g%d" % b)[:, PACK * first : PACK * end]
            copy(
                dst.rearrange("p (c s t) -> p c t s", s=PACK, t=PACK),
                g_tiles(b, first, end).rearrange("p t (c s) -> p c t s", s=PACK),
            )

        def table_gradient(b, block, bank):
            for j in range(PACK):
                matmul(
                    banks[bank][:, j * BLOCK : (j + 1) * BLOCK],
                    "xm%d" % b,
                    slice(j * P, (j + 1) * P),
                    "g%d" % b,
                    E5M2,
                    slice(block * BLOCK, (block + 1) * BLOCK),
                )

        def pack_dw(b, block, bank, copy):
            dst = packed("dw%d" % b)[:, PACK * BLOCK * block : PACK * BLOCK * (block + 1)]
            copy(
                dst.rearrange("p (c s j) -> p c j s", s=2, j=PACK),
                banks[bank][:].rearrange("p (j c s) -> p c j s", j=PACK, s=2),
            )

        def project(b, first, count, bank):
            if b == 0:
                matmul(banks[bank][:, 0:count], "pm", slice(0, K), "dw0_%d" % (first // HALF), E4M3, slice(0, count))
            else:
                matmul(banks[bank][:, 0:count], "pm", slice(0, K), "dw%d" % b, E4M3, slice(first, first + count))

        def empty(b, first, count, bank, copy):
            copy(tile("dense%d_%d" % (b, first), [P, count], F32), banks[bank][:, 0:count])

        def scatter_on_scalar(b, first, count):
            nc.scalar.activation(window[:].indirect(listed(b, first, count)), held["dense%d_%d" % (b, first)], ACT.Copy)

        def scatter_on_vector(b, first, count):
            on_vector(window[:].indirect(listed(b, first, count)), held["dense%d_%d" % (b, first)])

        def scatter_short(b, first, count):
            nc.vector.tensor_tensor(
                window[:].indirect(listed(b, first, count)), held["dense%d_%d" % (b, first)], held["zeros"], ALU.add
            )

        planes = [sb.tile([P, T], F32, name="plane%d" % j) for j in range(PACK)]
        for j in range(PACK):
            nc.sync.dma_start(out=planes[j][:], in_=rows(wT)[:, j, :])
            if j == 0:
                nc.sync.dma_start(offsets[:], offs)
        nc.scalar.dma_start(out=weights, in_=wt.rearrange("b (p t) o -> p b (t o)", t=PACK))
        load_columns("xT0", xT[0], 0, R)
        load_columns("xT1_0", xT[1], 0, HALF)
        load_targets(0, 0, 1)
        load_columns("xT1_1", xT[1], HALF, R)
        load_targets(0, 1, 2)
        load_targets(0, 2, 4)
        load_targets(1, 0, 1)
        load_columns("xm0_0", xm[0], 0, HALF)
        load_columns("xm0_1", xm[0], HALF, D)
        load_columns("pm", pm, 0, K)
        load_targets(1, 1, 4)
        load_columns("xm1_0", xm[1], 0, HALF)
        load_columns("xm1_1", xm[1], HALF, D)
        nc.gpsimd.memset(window[:], 0.0)
        nc.gpsimd.memset(tile("zeros", [P, BLOCK], F32), 0.0)

        def pick(j, b, first, count):
            dst = tile("picked%d" % b, [P, PACK, N], BF16)[:, j, first : first + count]
            src = planes[j][:].indirect(listed(b, first, count))
            if b == 0:
                on_vector(dst, src)
            else:
                nc.scalar.activation(dst, src, ACT.Copy)

        def pair_up(b, u, first, count, copy):
            dst = packed("w%d" % b).rearrange("p (c u e) -> p c u e", u=2, e=2)[:, first : first + count, u, :]
            copy(dst, held["picked%d" % b][:, 2 * u : 2 * u + 2, first : first + count].rearrange("p e c -> p c e"))

        for j in range(2):
            for b in range(B):
                pick(j, b, 0, N)
        pair_up(0, 0, 0, N, on_vector)
        pair_up(1, 0, 0, BLOCK, on_scalar_activation)
        pair_up(1, 0, BLOCK, N - BLOCK, on_vector)
        for b in range(B):
            pick(2, b, 0, N)
        for b in range(B):
            for h in range(2):
                pick(3, b, h * HALF, HALF)
            for h in range(2):
                pair_up(b, 1, h * HALF, HALF, on_scalar if b else on_vector)
        quantise("w0", E4M3, 0, HALF)
        quantise("w0", E4M3, HALF, HALF)
        deal_tiles("xT0", held["xT0"], 0, P, slice(0, 2), on_vector)
        if XT0_ON_SCALAR < P:
            deal_tiles("xT0", held["xT0"], 0, P - XT0_ON_SCALAR, slice(2, 4), on_vector)
        deal_tiles("xT0", held["xT0"], P - XT0_ON_SCALAR, P, slice(2, 4), on_scalar)
        quantise("xT0", E4M3, 0, HALF)
        tile("w1_codes", [P, N], U32, tag="xT0")
        quantise("w1", E4M3, 0, HALF)
        quantise("xT0", E4M3, HALF, HALF)
        quantise("w1", E4M3, HALF, HALF)
        for h in range(2):
            deal("xT1", held["xT1_%d" % h], h * 64, h * 64, (h + 1) * 64, on_scalar)

        def scores(b, t, neg_max):
            bank = PACK * b + t
            score(b, t, bank)
            row_max(bank, neg_max)
            exp(b, t, bank, neg_max)

        held["sums0"] = held["xT1_1"][:, 0, 0:PACK]
        neg_max = [tile("neg_max%d" % b, [P, PACK], F32) for b in range(B)]
        for t in range(PACK - 1):
            scores(0, t, neg_max[0][:, t : t + 1])
        quantise("xT1", E4M3, 0, HALF)
        quantise("xT1", E4M3, HALF, HALF)
        scores(0, PACK - 1, held["xT1_packed"][:, 0:2].bitcast(F32))
        weigh_on_gpsimd(0, 0, held["w1_packed"][:, 2 * N :].bitcast(F32))
        weigh_on_gpsimd(0, 1, held["y0"][:, 0, :])
        weigh_on_gpsimd(0, 2, held["xT1_packed"][:, 2 * N :].bitcast(F32))
        weigh_on_gpsimd(0, 3, held["y0"][:, 2, :])
        weigh_on_gpsimd(1, 0, held["y0"][:, 3, :])
        held["inverse0"] = packed("xm0")[:, HALF : HALF + 2 * PACK].bitcast(F32)
        late = tile("weighed1", [P, 2, N], F32)
        scores(1, 0, neg_max[1][:, 0:1])
        scores(1, 1, late[:, 1, 0:1])
        scores(1, 2, late[:, 0, 0:1])
        invert_sums(0)
        scores(1, PACK - 1, held["xm0_packed"][:, 0:2].bitcast(F32))
        row_factors(0)
        deal("xm0", held["xm0_1"], 64, 64, 128, on_vector)
        gradient(0, 0, 512, range(PACK))
        deal("xm0", held["xm0_0"], 0, 0, 64, on_scalar)
        weigh_on_scalar(1, 1, held["xm0_0"][:, 0:2, :].rearrange("p j c -> p (j c)"))
        weigh_on_scalar(1, 2, late[:, 0, :])
        weigh_on_scalar(1, 3, late[:, 1, :])
        invert_sums(1)
        pack_pm(on_vector)
        pack_g(0, 0, 256, on_vector)
        quantise("xm0", E4M3, 0, D)
        quantise("g0", E5M2, 0, 256)
        row_factors(1)
        pack_g(0, 256, 512, on_scalar)
        deal("xm1", held["xm1_0"], 0, 0, 64, on_vector)
        held["dw0_packed"] = held["g_tiles0"].rearrange("p t c -> p (t c)")
        for h in range(2):
            held["dw0_%d_packed" % h] = held["dw0_packed"][:, h * PACK * HALF : (h + 1) * PACK * HALF]
        held["g1_packed"] = held["dw0_packed"]
        table_gradient(0, 0, 0)
        table_gradient(0, 1, 1)
        gradient(1, 0, 256, [0])
        quantise("g0", E5M2, 256, 256)
        table_gradient(0, 2, 2)
        table_gradient(0, 3, 3)
        pack_dw(0, 0, 0, on_scalar)
        pack_dw(0, 1, 1, on_scalar)
        pack_dw(0, 2, 2, on_scalar)
        pack_dw(0, 3, 3, on_scalar)
        gradient(1, 0, 256, [1])
        quantise("pm", E4M3, 0, K)
        deal("xm1", held["xm1_1"], 64, 64, 128, on_vector)
        quantise("dw0_0", E4M3, 0, HALF)
        project(0, 0, 256, 4)
        empty(0, 0, 256, 4, on_scalar)
        scatter_on_scalar(0, 0, 256)
        gradient(1, 0, 256, [2, 3])
        quantise("xm1", E4M3, 0, D)
        pack_g(1, 0, 256, on_vector)
        gradient(1, 256, 384, [0])
        quantise("g1", E5M2, 0, 256)
        quantise("dw0_1", E4M3, 0, HALF)
        table_gradient(1, 0, 6)
        table_gradient(1, 1, 7)
        project(0, 256, 256, 5)
        pack_dw(1, 0, 6, on_scalar)
        pack_dw(1, 1, 7, on_scalar)
        gradient(1, 256, 384, [1, 2, 3])
        gradient(1, 384, 512, [0, 1, 2])
        empty(0, 256, 256, 5, on_vector)
        scatter_on_scalar(0, 256, 256)
        pack_g(1, 256, 384, on_vector)
        gradient(1, 384, 512, [3])
        quantise("dw1", E4M3, 0, 256)
        project(1, 0, 256, 0)
        quantise("g1", E5M2, 256, 128)
        table_gradient(1, 2, 1)
        pack_g(1, 384, 512, on_vector)
        empty(1, 0, 256, 0, on_vector)
        scatter_on_scalar(1, 0, 256)
        quantise("g1", E5M2, 384, 128)
        table_gradient(1, 3, 2)
        pack_dw(1, 2, 1, on_vector)
        quantise("dw1", E4M3, 256, 128)
        project(1, 256, 128, 3)
        pack_dw(1, 3, 2, on_vector)
        empty(1, 256, 128, 3, on_vector)
        quantise("dw1", E4M3, 384, 128)
        project(1, 384, 128, 4)
        scatter_short(1, 256, 128)
        empty(1, 384, 128, 4, on_scalar)
        scatter_short(1, 384, 128)
        nc.sync.dma_start(out=out, in_=window[:])
